import numpy as np
import ml_dtypes


def mxq(x, axis, fmt="e4m3"):
    dtype, down = {"e4m3": (ml_dtypes.float8_e4m3fn, 7), "e5m2": (ml_dtypes.float8_e5m2, 14)}[fmt]
    v = np.moveaxis(np.asarray(x, np.float32).astype(ml_dtypes.bfloat16).astype(np.float64), axis, -1)
    blocks = v.reshape(v.shape[:-1] + (-1, 32))
    amax = np.abs(blocks).max(-1, keepdims=True)
    byte = np.maximum(np.where(amax > 0, np.frexp(amax)[1] - 1 + 127, 0) - down, 1)
    scale = np.exp2(byte - 127.0)
    codes = (blocks / scale).astype(np.float32).astype(dtype).astype(np.float64)
    return np.moveaxis((codes * scale).reshape(v.shape), -1, axis)


WIDE = False


def mx_kscale(k):
    if not WIDE:
        return np.ones(k)
    levels = np.array([24, -24, 12, -12, 0])
    if k % 512:
        return np.exp2(np.random.permutation(np.resize(levels, k // 32))).repeat(32)
    a = np.empty((k // 512, 16))
    for p in range(k // 512):
        a[p, :8] = np.random.permutation(np.resize(levels, 8))
        for g in range(8):
            far = levels[np.abs(levels - a[p, g]) >= 10]
            a[p, g + 8] = far[np.random.randint(len(far))]
    return np.exp2(a.ravel()).repeat(32)


def f64(x):
    return np.asarray(x).astype(np.float64)


def striped(idx):
    return np.tile(idx.reshape(-1, 16).T, (8, 1)).astype(np.uint16)


def unstriped(offs):
    return offs[:16].T.reshape(-1).astype(np.int64)


def striped8(idx):
    return np.concatenate([v.reshape(-1, 16).T for v in idx]).astype(np.uint16)


def unstriped8(offs):
    return np.stack([offs[16 * g:16 * g + 16].T.reshape(-1) for g in range(8)]).astype(np.int64)


E2M1 = np.array([0.0, 0.5, 1.0, 1.5, 2.0, 3.0, 4.0, 6.0, -0.0, -0.5, -1.0, -1.5, -2.0, -3.0, -4.0, -6.0])


def pack_weight(w, fmt):
    k, n = w.shape
    w = f64(np.asarray(w, np.float32).astype(ml_dtypes.bfloat16)).reshape(k // 32, 32, n)
    amax = np.abs(w).max(1)
    if fmt == "e4m3":
        byte = np.frexp(amax)[1] - 1 + 127 - 7
    else:
        mant, ex = np.frexp(amax / 6.0)
        byte = np.where(mant > 0.5, ex, ex - 1) + 127
    byte = np.clip(np.where(amax > 0, byte, 1), 1, 254)
    scaled = (w * np.exp2(127.0 - byte)[:, None, :]).reshape(k, n).astype(np.float32)
    by_word = np.ascontiguousarray(scaled.reshape(k // 512, 128, 4, n).transpose(0, 1, 3, 2))
    if fmt == "e4m3":
        words = by_word.astype(ml_dtypes.float8_e4m3fn).view(np.uint8)
    else:
        c = by_word.astype(ml_dtypes.float4_e2m1fn).view(np.uint8) & 0xF
        words = (c[..., 0::2] | (c[..., 1::2] << 4)).reshape(k // 512, 128, 2 * n)
    return np.ascontiguousarray(words), np.ascontiguousarray(byte.astype(np.uint8).reshape(k // 512, 16, n))


def unpack_weight(words, scales, fmt):
    g, _, n = scales.shape
    words = np.ascontiguousarray(words).reshape(g, 128, n, -1)
    if fmt == "e4m3":
        vals = words.view(ml_dtypes.float8_e4m3fn).astype(np.float64)
    else:
        nib = np.empty((g, 128, n, 4), np.uint8)
        nib[..., 0::2] = words & 0xF
        nib[..., 1::2] = words >> 4
        vals = E2M1[nib]
    vals = vals * np.repeat(np.exp2(scales.astype(np.float64) - 127.0), 8, axis=1)[..., None]
    return vals.transpose(0, 1, 3, 2).reshape(g * 512, n)


def pack_table4(v):
    words, scales = pack_weight(v, "e2m1")
    g, t = words.shape[0] // 2, v.shape[1]
    return np.ascontiguousarray(words.reshape(g, 2, 128, t, 2).transpose(0, 2, 3, 1, 4).reshape(g, 128, t, 4)), scales


def unpack_table4(words, scales):
    g, _, t, _ = words.shape
    return unpack_weight(words.reshape(g, 128, t, 2, 2).transpose(0, 3, 1, 2, 4).reshape(2 * g, 128, 2 * t), scales, "e2m1")


K, L, R, N, T, J = 512, 1024, 512, 512, 2048, 1024


def setup_inputs():
    n = np.random.standard_normal
    s = mx_kscale(K)[:, None]
    s2 = mx_kscale(L)[:, None]
    u = mx_kscale(R)[:, None]
    p_tab = pack_table4(n((L, T)) * s2)
    p_wa = pack_weight(n((K, R)) / np.sqrt(K) / s * u.T, "e4m3")
    p_wb = pack_weight(n((L, R)) / np.sqrt(L) / s2 * u.T, "e4m3")
    p_wd = pack_weight(n((R, N)) / np.sqrt(R) / u, "e4m3")
    return {
        "tab_words": p_tab[0],
        "tab_scales": p_tab[1],
        "xT": (n((K, T)) * s).astype(np.float32),
        "wgt2": np.repeat(np.random.uniform(0.5, 2.0, (8, J)), 16, axis=0).astype(np.float32),
        "wa_words": p_wa[0],
        "wa_scales": p_wa[1],
        "wb_words": p_wb[0],
        "wb_scales": p_wb[1],
        "wd_words": p_wd[0],
        "wd_scales": p_wd[1],
        "res": (n((N, J))).astype(np.float32),
        "offs": striped(np.random.permutation(T)[:J]),
        "offs2": striped8(np.stack([np.random.permutation(T)[:J] for _ in range(8)])),
    }


def reference(tab_words, tab_scales, xT, wgt2, wa_words, wa_scales, wb_words, wb_scales, wd_words, wd_scales, res, offs, offs2):
    idx = unstriped(offs)
    idx2 = unstriped8(offs2)
    tab_ = unpack_table4(tab_words, tab_scales)[:, idx]
    rows = np.arange(K)
    xg = f64(wgt2)[rows // 4 % 128] * f64(xT)[rows[:, None], idx2[rows % 512 // 64]]
    xT_ = mxq(xg, 0, "e4m3")
    wa_ = unpack_weight(wa_words, wa_scales, "e4m3")
    wb_ = unpack_weight(wb_words, wb_scales, "e4m3")
    ya = wa_.T @ xT_
    yb = wb_.T @ tab_
    h = np.maximum(ya, yb)
    h_ = mxq(h, 0, "e4m3")
    wd_ = unpack_weight(wd_words, wd_scales, "e4m3")
    y = wd_.T @ h_
    return f64(res) + y

@@ -1,0 +1,207 @@
+from contextlib import ExitStack
+
+import concourse.mybir as mybir
+
+K, L, R, N, T, J = 512, 1024, 512, 512, 2048, 1024
+FLOPS = 2 * J * (K * R + L * R + R * N)
+
+F32 = mybir.dt.float32
+BF16 = mybir.dt.bfloat16
+I32 = mybir.dt.int32
+U32 = mybir.dt.uint32
+U16 = mybir.dt.uint16
+U8 = mybir.dt.uint8
+FP8X4 = mybir.dt.float8_e4m3fn_x4
+FP4X4 = mybir.dt.float4_e2m1fn_x4
+MULT = mybir.AluOpType.mult
+MAX = mybir.AluOpType.max
+ADD = mybir.AluOpType.add
+
+P = 128
+PACK = 4
+QUADS = 4
+CHUNK = 256
+BANK_COLS = 128
+SHIFT_ROWS = 100
+
+
+def tile_list_htabg_max_res_kernel(
+    tc, tab_words, tab_scales, xT, wgt2, wa_words, wa_scales, wb_words, wb_scales, wd_words, wd_scales, res, offs, offs2, out
+):
+    nc = tc.nc
+    chunks = J // CHUNK
+
+    with ExitStack() as ctx:
+        keep = ctx.enter_context(tc.tile_pool(name="keep", bufs=1))
+        ps_h = ctx.enter_context(tc.psum_pool(name="ps_h", bufs=4))
+        ps_y = ctx.enter_context(tc.psum_pool(name="ps_y", bufs=4))
+
+        idx = keep.tile([P, J // 16], U16, name="idx")
+        idx2 = keep.tile([P, J // 16], U16, name="idx2")
+        tab_sc = keep.tile([P, T // 4], I32, name="tab_sc", align_bytes=64)
+        tab_w = keep.tile([P, T], I32, name="tab_w", align_bytes=64)
+        got_sc = keep.tile([P, J // 4], I32, name="got_sc", align_bytes=64)
+        planes = keep.tile([P, 2, J // 4], I32, name="planes", align_bytes=64)
+        got_w = keep.tile([P, J], I32, name="got_w", align_bytes=64)
+        part_w = [keep.tile([P, 2, J // 4], I32, name="part_w%d" % i, align_bytes=64) for i in range(2)]
+        w_raw = keep.tile([P, 3, R], I32, name="w_raw", align_bytes=64)
+        w_perm = keep.tile([P, PACK, 3, P], I32, name="w_perm", align_bytes=64)
+        wd_w = keep.tile([P, N], I32, name="wd_w", align_bytes=64)
+        sc_raw = keep.tile([P, 2, R // 4], I32, name="sc_raw", align_bytes=64)
+        wd_sc = keep.tile([P, N // 4], I32, name="wd_sc", align_bytes=64)
+        sc_perm = keep.tile([P, PACK, 2, P], U8, name="sc_perm", align_bytes=64)
+        wgt = keep.tile([P, J], F32, name="wgt", align_bytes=64)
+        x_pl = [keep.tile([P, T], F32, name="x_pl%d" % i, align_bytes=64) for i in range(PACK)]
+        res_sb = keep.tile([P, N // P, J], F32, name="res_sb", align_bytes=64)
+        xg_lo = [keep.tile([P, 2, J // 2], F32, name="xg_lo%d" % i, align_bytes=64) for i in range(2)]
+        xg_hi = [keep.tile([P, 2, CHUNK], F32, name="xg_hi%d" % i, align_bytes=64) for i in range(chunks)]
+        xg_bf = keep.tile([P, J, PACK], BF16, name="xg_bf", align_bytes=64)
+        xq = keep.tile([P, J], U32, name="xq", align_bytes=64)
+        xq_sc = keep.tile([P, J], U8, name="xq_sc", align_bytes=64)
+        ya_bf = keep.tile([P, J, PACK], BF16, name="ya_bf", align_bytes=64)
+        yb_bf = keep.tile([P, J, PACK], BF16, name="yb_bf", align_bytes=64)
+        h_bf = keep.tile([P, J, PACK], BF16, name="h_bf", align_bytes=64)
+        hq = keep.tile([P, J], U32, name="hq", align_bytes=64)
+        hq_sc = keep.tile([P, J], U8, name="hq_sc", align_bytes=64)
+        o_sb = keep.tile([P, chunks, N // P, CHUNK], F32, name="o_sb", align_bytes=64)
+
+        def words(dram, a):
+            return dram[a].rearrange("p n t -> p (n t)").bitcast(I32)
+
+        for q in range(QUADS):
+            nc.vector.memset(tab_sc[32 * q : 32 * q + 24, :], 0)
+        nc.gpsimd.memset(sc_raw[:], 0)
+        nc.vector.memset(planes[:], 0)
+        nc.gpsimd.memset(wd_sc[:], 0)
+
+        nc.sync.dma_start(idx[:], offs)
+        for q in range(QUADS):
+            nc.sync.dma_start(tab_sc[32 * q + 24 : 32 * q + 32, :], tab_scales[:, 4 * q : 4 * q + 4, :].bitcast(I32))
+        nc.sync.dma_start(tab_w[:], words(tab_words, 0))
+        nc.sync.dma_start(idx2[:], offs2)
+        nc.sync.dma_start(
+            w_raw[:, 0:2, :], wb_words.rearrange("a p n t -> p a (n t)").bitcast(I32)
+        )
+        for q in range(QUADS):
+            nc.scalar.dma_start(
+                sc_raw[32 * q : 32 * q + 4, :, :], wb_scales[:, 4 * q : 4 * q + 4, :].rearrange("a r c -> r a c").bitcast(I32)
+            )
+        x_rows = xT.rearrange("(p i) t -> i p t", i=PACK)
+        nc.sync.dma_start(wgt[:], wgt2)
+        nc.sync.dma_start(x_pl[0][:], x_rows[0])
+        for q in range(QUADS):
+            nc.scalar.dma_start(sc_raw[32 * q + 4 : 32 * q + 8, 0, :], wa_scales[0, 4 * q : 4 * q + 4, :].bitcast(I32))
+        nc.sync.dma_start(x_pl[1][:], x_rows[1])
+        nc.sync.dma_start(w_raw[:, 2, :], words(wa_words, 0))
+        nc.sync.dma_start(x_pl[2][:], x_rows[2])
+        nc.sync.dma_start(x_pl[3][:], x_rows[3])
+        nc.sync.dma_start(wd_w[:], words(wd_words, 0))
+        for q in range(QUADS):
+            nc.sync.dma_start(wd_sc[32 * q : 32 * q + 4, :], wd_scales[0, 4 * q : 4 * q + 4, :].bitcast(I32))
+        res_rows = res.rearrange("(a p) j -> p a j", p=P)
+        for hf in range(2):
+            cols = slice(hf * J // 2, (hf + 1) * J // 2)
+            nc.sync.dma_start(res_sb[:, :, cols], res_rows[:, :, cols])
+
+        nc.vector.tensor_copy(got_sc[:].bitcast(U8), tab_sc[:].bitcast(U8).indirect(idx[:]))
+        for a in range(2):
+            nc.scalar.dma_start(planes[0:SHIFT_ROWS, a, :], got_sc[24 + 4 * a : 24 + 4 * a + SHIFT_ROWS, :])
+        for hf in range(2):
+            nc.vector.tensor_copy(
+                got_w[:, hf * 512 : (hf + 1) * 512].bitcast(U32), tab_w[:].bitcast(U32).indirect(idx[:, hf * 32 : (hf + 1) * 32])
+            )
+        for hf in range(2):
+            src = got_w[:, hf * 512 : (hf + 1) * 512].bitcast(U16).rearrange("p (c i d) -> p c d i", i=8, d=2)
+            dst = part_w[hf][:].bitcast(U16).rearrange("p d (c i) -> p c d i", i=8)
+            nc.vector.tensor_copy(dst, src)
+
+        def permute_words(a0, a1):
+            nc.vector.tensor_copy(
+                w_perm[:, :, a0:a1, :].rearrange("p t a (c i) -> p (a c) t i", i=4),
+                w_raw[:, a0:a1, :].rearrange("p a (c i t) -> p (a c) t i", i=4, t=PACK),
+            )
+
+        permute_words(0, 2)
+        nc.vector.tensor_copy(
+            sc_perm[:].rearrange("p t a (c i) -> p (a c) t i", i=16),
+            sc_raw[:].bitcast(U8).rearrange("p a (c i t) -> p (a c) t i", i=16, t=PACK),
+        )
+
+        for b in range(J // BANK_COLS):
+            cols = slice(b * BANK_COLS, (b + 1) * BANK_COLS)
+            acc = ps_h.tile([P, PACK, BANK_COLS], F32, name="acc")
+            for t in range(PACK):
+                for a in range(2):
+                    nc.tensor.matmul_mx(
+                        out=acc[:, t, :],
+                        lhsT=w_perm[:, t, a, :].bitcast(FP8X4),
+                        lhsT_scale=sc_perm[:, t, a, :],
+                        rhs=part_w[b // 4][:, a, b % 4 * 64 : (b % 4 + 1) * 64].bitcast(U8).bitcast(FP4X4),
+                        rhs_scale=planes[:, a, :].bitcast(U8)[:, cols],
+                        start=(a == 0),
+                        stop=(a == 1),
+                    )
+            nc.scalar.copy(yb_bf[:, cols, :], acc[:].rearrange("p t n -> p n t"))
+
+        def gather_x(dst, i, c0, c1):
+            nc.vector.tensor_tensor(
+                dst[:, i % 2, :], x_pl[i][:].indirect(idx2[:, c0 // 16 : c1 // 16]), wgt[:, c0:c1], MULT
+            )
+
+        def interleave(src, i0, i1, c0, c1):
+            nc.scalar.copy(
+                xg_bf[:, c0:c1, i0:i1].rearrange("p (c k) t -> p c t k", k=4),
+                src[:].rearrange("p t (c k) -> p c t k", k=4),
+            )
+
+        for hf in range(2):
+            gather_x(xg_lo[hf], 0, hf * 512, (hf + 1) * 512)
+        for hf in range(2):
+            gather_x(xg_lo[hf], 1, hf * 512, (hf + 1) * 512)
+            interleave(xg_lo[hf], 0, 2, hf * 512, (hf + 1) * 512)
+        permute_words(2, 3)
+        for c in range(chunks):
+            gather_x(xg_hi[c], 2, c * CHUNK, (c + 1) * CHUNK)
+            gather_x(xg_hi[c], 3, c * CHUNK, (c + 1) * CHUNK)
+            interleave(xg_hi[c], 2, 4, c * CHUNK, (c + 1) * CHUNK)
+
+        out_rows = out.rearrange("(a p) j -> p a j", p=P)
+        for c in range(chunks):
+            ch = slice(c * CHUNK, (c + 1) * CHUNK)
+            nc.vector.quantize_mx(
+                out=xq[:, ch].bitcast(FP8X4), scales=xq_sc[:, ch], in_=xg_bf[:, ch, :].rearrange("p n t -> p (n t)")
+            )
+            for b in range(c * CHUNK // BANK_COLS, (c + 1) * CHUNK // BANK_COLS):
+                cols = slice(b * BANK_COLS, (b + 1) * BANK_COLS)
+                acc = ps_h.tile([P, PACK, BANK_COLS], F32, name="acc")
+                for t in range(PACK):
+                    nc.tensor.matmul_mx(
+                        out=acc[:, t, :],
+                        lhsT=w_perm[:, t, 2, :].bitcast(FP8X4),
+                        lhsT_scale=sc_perm[4:P, t, 0, :],
+                        rhs=xq[:, cols].bitcast(FP8X4),
+                        rhs_scale=xq_sc[:, cols],
+                        start=True,
+                        stop=True,
+                    )
+                nc.scalar.copy(ya_bf[:, cols, :], acc[:].rearrange("p t n -> p n t"))
+            nc.vector.tensor_tensor(h_bf[:, ch, :], ya_bf[:, ch, :], yb_bf[:, ch, :], MAX)
+            nc.vector.quantize_mx(
+                out=hq[:, ch].bitcast(FP8X4), scales=hq_sc[:, ch], in_=h_bf[:, ch, :].rearrange("p n t -> p (n t)")
+            )
+            for pair in range(2):
+                y = ps_y.tile([P, 2, CHUNK], F32, name="y")
+                for u in range(2):
+                    nt = 2 * pair + u
+                    nc.tensor.matmul_mx(
+                        out=y[:, u, :],
+                        lhsT=wd_w[:, nt * P : (nt + 1) * P].bitcast(FP8X4),
+                        lhsT_scale=wd_sc[:, nt * 32 : (nt + 1) * 32].bitcast(U8),
+                        rhs=hq[:, ch].bitcast(FP8X4),
+                        rhs_scale=hq_sc[:, ch],
+                        start=True,
+                        stop=True,
+                    )
+                nts = slice(2 * pair, 2 * pair + 2)
+                nc.vector.tensor_tensor(o_sb[:, c, nts, :], y[:], res_sb[:, nts, ch], ADD)
+                nc.sync.dma_start(out_rows[:, nts, ch], o_sb[:, c, nts, :])

@@ -20,7 +20,10 @@ ADD = mybir.AluOpType.add
 P = 128
 PACK = 4
 QUADS = 4
-CHUNK = 256
+HALF = J // 2
+STARTS = (0, 256, 512, 768, 896, 1024)
+DIRECT = (0,)
+LAG = 1
 BANK_COLS = 128
 SHIFT_ROWS = 100
 
@@ -29,7 +32,6 @@ def tile_list_htabg_max_res_kernel(
     tc, tab_words, tab_scales, xT, wgt2, wa_words, wa_scales, wb_words, wb_scales, wd_words, wd_scales, res, offs, offs2, out
 ):
     nc = tc.nc
-    chunks = J // CHUNK
 
     with ExitStack() as ctx:
         keep = ctx.enter_context(tc.tile_pool(name="keep", bufs=1))
@@ -52,9 +54,8 @@ def tile_list_htabg_max_res_kernel(
         sc_perm = keep.tile([P, PACK, 2, P], U8, name="sc_perm", align_bytes=64)
         wgt = keep.tile([P, J], F32, name="wgt", align_bytes=64)
         x_pl = [keep.tile([P, T], F32, name="x_pl%d" % i, align_bytes=64) for i in range(PACK)]
-        res_sb = keep.tile([P, N // P, J], F32, name="res_sb", align_bytes=64)
-        xg_lo = [keep.tile([P, 2, J // 2], F32, name="xg_lo%d" % i, align_bytes=64) for i in range(2)]
-        xg_hi = [keep.tile([P, 2, CHUNK], F32, name="xg_hi%d" % i, align_bytes=64) for i in range(chunks)]
+        res_sb = [keep.tile([P, N // P, HALF], F32, name="res_sb%d" % i, align_bytes=64) for i in range(2)]
+        xg = [keep.tile([P, PACK, HALF], F32, name="xg%d" % i, align_bytes=64) for i in range(2)]
         xg_bf = keep.tile([P, J, PACK], BF16, name="xg_bf", align_bytes=64)
         xq = keep.tile([P, J], U32, name="xq", align_bytes=64)
         xq_sc = keep.tile([P, J], U8, name="xq_sc", align_bytes=64)
@@ -63,7 +64,7 @@ def tile_list_htabg_max_res_kernel(
         h_bf = keep.tile([P, J, PACK], BF16, name="h_bf", align_bytes=64)
         hq = keep.tile([P, J], U32, name="hq", align_bytes=64)
         hq_sc = keep.tile([P, J], U8, name="hq_sc", align_bytes=64)
-        o_sb = keep.tile([P, chunks, N // P, CHUNK], F32, name="o_sb", align_bytes=64)
+        o_sb = keep.tile([P, J // BANK_COLS, 512], F32, name="o_sb", align_bytes=64)
 
         def words(dram, a):
             return dram[a].rearrange("p n t -> p (n t)").bitcast(I32)
@@ -71,7 +72,7 @@ def tile_list_htabg_max_res_kernel(
         for q in range(QUADS):
             nc.vector.memset(tab_sc[32 * q : 32 * q + 24, :], 0)
         nc.gpsimd.memset(sc_raw[:], 0)
-        nc.vector.memset(planes[:], 0)
+        nc.gpsimd.memset(planes[:], 0)
         nc.gpsimd.memset(wd_sc[:], 0)
 
         nc.sync.dma_start(idx[:], offs)
@@ -83,29 +84,29 @@ def tile_list_htabg_max_res_kernel(
             w_raw[:, 0:2, :], wb_words.rearrange("a p n t -> p a (n t)").bitcast(I32)
         )
         for q in range(QUADS):
-            nc.scalar.dma_start(
+            nc.sync.dma_start(
                 sc_raw[32 * q : 32 * q + 4, :, :], wb_scales[:, 4 * q : 4 * q + 4, :].rearrange("a r c -> r a c").bitcast(I32)
             )
         x_rows = xT.rearrange("(p i) t -> i p t", i=PACK)
         nc.sync.dma_start(wgt[:], wgt2)
         nc.sync.dma_start(x_pl[0][:], x_rows[0])
         for q in range(QUADS):
-            nc.scalar.dma_start(sc_raw[32 * q + 4 : 32 * q + 8, 0, :], wa_scales[0, 4 * q : 4 * q + 4, :].bitcast(I32))
+            nc.sync.dma_start(sc_raw[32 * q + 4 : 32 * q + 8, 0, :], wa_scales[0, 4 * q : 4 * q + 4, :].bitcast(I32))
         nc.sync.dma_start(x_pl[1][:], x_rows[1])
-        nc.sync.dma_start(w_raw[:, 2, :], words(wa_words, 0))
         nc.sync.dma_start(x_pl[2][:], x_rows[2])
         nc.sync.dma_start(x_pl[3][:], x_rows[3])
+        nc.sync.dma_start(w_raw[:, 2, :], words(wa_words, 0))
         nc.sync.dma_start(wd_w[:], words(wd_words, 0))
         for q in range(QUADS):
             nc.sync.dma_start(wd_sc[32 * q : 32 * q + 4, :], wd_scales[0, 4 * q : 4 * q + 4, :].bitcast(I32))
         res_rows = res.rearrange("(a p) j -> p a j", p=P)
         for hf in range(2):
             cols = slice(hf * J // 2, (hf + 1) * J // 2)
-            nc.sync.dma_start(res_sb[:, :, cols], res_rows[:, :, cols])
+            nc.sync.dma_start(res_sb[hf][:], res_rows[:, :, cols])
 
         nc.vector.tensor_copy(got_sc[:].bitcast(U8), tab_sc[:].bitcast(U8).indirect(idx[:]))
         for a in range(2):
-            nc.scalar.dma_start(planes[0:SHIFT_ROWS, a, :], got_sc[24 + 4 * a : 24 + 4 * a + SHIFT_ROWS, :])
+            nc.gpsimd.dma_start(planes[0:SHIFT_ROWS, a, :], got_sc[24 + 4 * a : 24 + 4 * a + SHIFT_ROWS, :])
         for hf in range(2):
             nc.vector.tensor_copy(
                 got_w[:, hf * 512 : (hf + 1) * 512].bitcast(U32), tab_w[:].bitcast(U32).indirect(idx[:, hf * 32 : (hf + 1) * 32])
@@ -143,35 +144,29 @@ def tile_list_htabg_max_res_kernel(
                     )
             nc.scalar.copy(yb_bf[:, cols, :], acc[:].rearrange("p t n -> p n t"))
 
-        def gather_x(dst, i, c0, c1):
+        def gather_x(i, c0, c1):
             nc.vector.tensor_tensor(
-                dst[:, i % 2, :], x_pl[i][:].indirect(idx2[:, c0 // 16 : c1 // 16]), wgt[:, c0:c1], MULT
+                xg[c0 // HALF][:, i, c0 % HALF : c0 % HALF + c1 - c0], x_pl[i][:].indirect(idx2[:, c0 // 16 : c1 // 16]), wgt[:, c0:c1], MULT
             )
-
-        def interleave(src, i0, i1, c0, c1):
-            nc.scalar.copy(
-                xg_bf[:, c0:c1, i0:i1].rearrange("p (c k) t -> p c t k", k=4),
-                src[:].rearrange("p t (c k) -> p c t k", k=4),
-            )
-
-        for hf in range(2):
-            gather_x(xg_lo[hf], 0, hf * 512, (hf + 1) * 512)
-        for hf in range(2):
-            gather_x(xg_lo[hf], 1, hf * 512, (hf + 1) * 512)
-            interleave(xg_lo[hf], 0, 2, hf * 512, (hf + 1) * 512)
-        permute_words(2, 3)
-        for c in range(chunks):
-            gather_x(xg_hi[c], 2, c * CHUNK, (c + 1) * CHUNK)
-            gather_x(xg_hi[c], 3, c * CHUNK, (c + 1) * CHUNK)
-            interleave(xg_hi[c], 2, 4, c * CHUNK, (c + 1) * CHUNK)
 
         out_rows = out.rearrange("(a p) j -> p a j", p=P)
-        for c in range(chunks):
-            ch = slice(c * CHUNK, (c + 1) * CHUNK)
+
+        def front(c):
+            c0, c1 = STARTS[c], STARTS[c + 1]
+            hf, h0 = divmod(c0, HALF)
+            gather_x(3, c0, c1)
+            nc.scalar.copy(
+                xg_bf[:, c0:c1, :].rearrange("p (c k) t -> p c t k", k=4),
+                xg[hf][:, :, h0 : h0 + c1 - c0].rearrange("p t (c k) -> p c t k", k=4),
+            )
+
+        def chain(c):
+            c0, c1 = STARTS[c], STARTS[c + 1]
+            ch = slice(c0, c1)
             nc.vector.quantize_mx(
                 out=xq[:, ch].bitcast(FP8X4), scales=xq_sc[:, ch], in_=xg_bf[:, ch, :].rearrange("p n t -> p (n t)")
             )
-            for b in range(c * CHUNK // BANK_COLS, (c + 1) * CHUNK // BANK_COLS):
+            for b in range(c0 // BANK_COLS, c1 // BANK_COLS):
                 cols = slice(b * BANK_COLS, (b + 1) * BANK_COLS)
                 acc = ps_h.tile([P, PACK, BANK_COLS], F32, name="acc")
                 for t in range(PACK):
@@ -184,15 +179,21 @@ def tile_list_htabg_max_res_kernel(
                         start=True,
                         stop=True,
                     )
-                nc.scalar.copy(ya_bf[:, cols, :], acc[:].rearrange("p t n -> p n t"))
-            nc.vector.tensor_tensor(h_bf[:, ch, :], ya_bf[:, ch, :], yb_bf[:, ch, :], MAX)
+                if c in DIRECT:
+                    nc.vector.tensor_tensor(h_bf[:, cols, :], acc[:].rearrange("p t n -> p n t"), yb_bf[:, cols, :], MAX)
+                else:
+                    nc.scalar.copy(ya_bf[:, cols, :], acc[:].rearrange("p t n -> p n t"))
+            if c not in DIRECT:
+                nc.vector.tensor_tensor(h_bf[:, ch, :], ya_bf[:, ch, :], yb_bf[:, ch, :], MAX)
             nc.vector.quantize_mx(
                 out=hq[:, ch].bitcast(FP8X4), scales=hq_sc[:, ch], in_=h_bf[:, ch, :].rearrange("p n t -> p (n t)")
             )
-            for pair in range(2):
-                y = ps_y.tile([P, 2, CHUNK], F32, name="y")
-                for u in range(2):
-                    nt = 2 * pair + u
+            width = c1 - c0
+            per_bank = 512 // width
+            for g in range(N // P // per_bank):
+                y = ps_y.tile([P, per_bank, width], F32, name="y")
+                for u in range(per_bank):
+                    nt = per_bank * g + u
                     nc.tensor.matmul_mx(
                         out=y[:, u, :],
                         lhsT=wd_w[:, nt * P : (nt + 1) * P].bitcast(FP8X4),
@@ -202,6 +203,21 @@ def tile_list_htabg_max_res_kernel(
                         start=True,
                         stop=True,
                     )
-                nts = slice(2 * pair, 2 * pair + 2)
-                nc.vector.tensor_tensor(o_sb[:, c, nts, :], y[:], res_sb[:, nts, ch], ADD)
-                nc.sync.dma_start(out_rows[:, nts, ch], o_sb[:, c, nts, :])
+                nts = slice(per_bank * g, per_bank * (g + 1))
+                o = o_sb[:, c0 // BANK_COLS + g, :].rearrange("p (u n) -> p u n", u=per_bank)
+                nc.vector.tensor_tensor(o, y[:], res_sb[c0 // HALF][:, nts, c0 % HALF : c0 % HALF + width], ADD)
+                nc.sync.dma_start(out_rows[:, nts, ch], o)
+
+        for i in range(2):
+            for hf in range(2):
+                gather_x(i, hf * HALF, (hf + 1) * HALF)
+        gather_x(2, 0, HALF)
+        permute_words(2, 3)
+        for c in range(len(STARTS) - 1):
+            if STARTS[c] == HALF:
+                gather_x(2, HALF, J)
+            front(c)
+            if c >= LAG:
+                chain(c - LAG)
+        for c in range(len(STARTS) - 1 - LAG, len(STARTS) - 1):
+            chain(c)

@@ -22,7 +22,7 @@ PACK = 4
 QUADS = 4
 HALF = J // 2
 STARTS = (0, 256, 512, 768, 896, 1024)
-DIRECT = (0,)
+DIRECT = ()
 LAG = 1
 BANK_COLS = 128
 SHIFT_ROWS = 100
@@ -40,21 +40,18 @@ def tile_list_htabg_max_res_kernel(
 
         idx = keep.tile([P, J // 16], U16, name="idx")
         idx2 = keep.tile([P, J // 16], U16, name="idx2")
-        tab_sc = keep.tile([P, T // 4], I32, name="tab_sc", align_bytes=64)
-        tab_w = keep.tile([P, T], I32, name="tab_w", align_bytes=64)
-        got_sc = keep.tile([P, J // 4], I32, name="got_sc", align_bytes=64)
+        tab_sc = keep.tile([P, T // 4], I32, name="tab_sc", tag="a", align_bytes=64)
+        tab_w = keep.tile([P, T], I32, name="tab_w", tag="b", align_bytes=64)
+        got_sc = keep.tile([P, J // 4], I32, name="got_sc", tag="c", align_bytes=64)
         planes = keep.tile([P, 2, J // 4], I32, name="planes", align_bytes=64)
-        got_w = keep.tile([P, J], I32, name="got_w", align_bytes=64)
+        got_w = keep.tile([P, J], I32, name="got_w", tag="e", align_bytes=64)
         part_w = [keep.tile([P, 2, J // 4], I32, name="part_w%d" % i, align_bytes=64) for i in range(2)]
-        w_raw = keep.tile([P, 3, R], I32, name="w_raw", align_bytes=64)
+        wb_raw = keep.tile([P, 2, R], I32, name="wb_raw", tag="f", align_bytes=64)
         w_perm = keep.tile([P, PACK, 3, P], I32, name="w_perm", align_bytes=64)
-        wd_w = keep.tile([P, N], I32, name="wd_w", align_bytes=64)
         sc_raw = keep.tile([P, 2, R // 4], I32, name="sc_raw", align_bytes=64)
-        wd_sc = keep.tile([P, N // 4], I32, name="wd_sc", align_bytes=64)
         sc_perm = keep.tile([P, PACK, 2, P], U8, name="sc_perm", align_bytes=64)
         wgt = keep.tile([P, J], F32, name="wgt", align_bytes=64)
-        x_pl = [keep.tile([P, T], F32, name="x_pl%d" % i, align_bytes=64) for i in range(PACK)]
-        res_sb = [keep.tile([P, N // P, HALF], F32, name="res_sb%d" % i, align_bytes=64) for i in range(2)]
+        x_pl = [keep.tile([P, T], F32, name="x_pl0", tag="d", align_bytes=64)]
         xg = [keep.tile([P, PACK, HALF], F32, name="xg%d" % i, align_bytes=64) for i in range(2)]
         xg_bf = keep.tile([P, J, PACK], BF16, name="xg_bf", align_bytes=64)
         xq = keep.tile([P, J], U32, name="xq", align_bytes=64)
@@ -69,11 +66,11 @@ def tile_list_htabg_max_res_kernel(
         def words(dram, a):
             return dram[a].rearrange("p n t -> p (n t)").bitcast(I32)
 
-        for q in range(QUADS):
-            nc.vector.memset(tab_sc[32 * q : 32 * q + 24, :], 0)
         nc.gpsimd.memset(sc_raw[:], 0)
+        for q in range(QUADS):
+            eng = nc.gpsimd if q < 2 else nc.vector
+            eng.memset(tab_sc[32 * q : 32 * q + 24, :], 0)
         nc.gpsimd.memset(planes[:], 0)
-        nc.gpsimd.memset(wd_sc[:], 0)
 
         nc.sync.dma_start(idx[:], offs)
         for q in range(QUADS):
@@ -81,7 +78,7 @@ def tile_list_htabg_max_res_kernel(
         nc.sync.dma_start(tab_w[:], words(tab_words, 0))
         nc.sync.dma_start(idx2[:], offs2)
         nc.sync.dma_start(
-            w_raw[:, 0:2, :], wb_words.rearrange("a p n t -> p a (n t)").bitcast(I32)
+            wb_raw[:], wb_words.rearrange("a p n t -> p a (n t)").bitcast(I32)
         )
         for q in range(QUADS):
             nc.sync.dma_start(
@@ -92,41 +89,42 @@ def tile_list_htabg_max_res_kernel(
         nc.sync.dma_start(x_pl[0][:], x_rows[0])
         for q in range(QUADS):
             nc.sync.dma_start(sc_raw[32 * q + 4 : 32 * q + 8, 0, :], wa_scales[0, 4 * q : 4 * q + 4, :].bitcast(I32))
-        nc.sync.dma_start(x_pl[1][:], x_rows[1])
-        nc.sync.dma_start(x_pl[2][:], x_rows[2])
-        nc.sync.dma_start(x_pl[3][:], x_rows[3])
-        nc.sync.dma_start(w_raw[:, 2, :], words(wa_words, 0))
-        nc.sync.dma_start(wd_w[:], words(wd_words, 0))
-        for q in range(QUADS):
-            nc.sync.dma_start(wd_sc[32 * q : 32 * q + 4, :], wd_scales[0, 4 * q : 4 * q + 4, :].bitcast(I32))
-        res_rows = res.rearrange("(a p) j -> p a j", p=P)
-        for hf in range(2):
-            cols = slice(hf * J // 2, (hf + 1) * J // 2)
-            nc.sync.dma_start(res_sb[hf][:], res_rows[:, :, cols])
 
         nc.vector.tensor_copy(got_sc[:].bitcast(U8), tab_sc[:].bitcast(U8).indirect(idx[:]))
         for a in range(2):
-            nc.gpsimd.dma_start(planes[0:SHIFT_ROWS, a, :], got_sc[24 + 4 * a : 24 + 4 * a + SHIFT_ROWS, :])
+            nc.sync.dma_start(planes[0:SHIFT_ROWS, a, :], got_sc[24 + 4 * a : 24 + 4 * a + SHIFT_ROWS, :])
+        x_pl.append(keep.tile([P, T], F32, name="x_pl1", tag="a", align_bytes=64))
+        nc.sync.dma_start(x_pl[1][:], x_rows[1])
         for hf in range(2):
             nc.vector.tensor_copy(
                 got_w[:, hf * 512 : (hf + 1) * 512].bitcast(U32), tab_w[:].bitcast(U32).indirect(idx[:, hf * 32 : (hf + 1) * 32])
             )
+        for i, tag in ((2, "b"), (3, "c")):
+            x_pl.append(keep.tile([P, T], F32, name="x_pl%d" % i, tag=tag, align_bytes=64))
+            nc.sync.dma_start(x_pl[i][:], x_rows[i])
         for hf in range(2):
             src = got_w[:, hf * 512 : (hf + 1) * 512].bitcast(U16).rearrange("p (c i d) -> p c d i", i=8, d=2)
             dst = part_w[hf][:].bitcast(U16).rearrange("p d (c i) -> p c d i", i=8)
             nc.vector.tensor_copy(dst, src)
 
-        def permute_words(a0, a1):
+        def permute_words(raw, a0, a1):
             nc.vector.tensor_copy(
                 w_perm[:, :, a0:a1, :].rearrange("p t a (c i) -> p (a c) t i", i=4),
-                w_raw[:, a0:a1, :].rearrange("p a (c i t) -> p (a c) t i", i=4, t=PACK),
+                raw[:].rearrange("p a (c i t) -> p (a c) t i", i=4, t=PACK),
             )
 
-        permute_words(0, 2)
+        wa_raw = keep.tile([P, 1, R], I32, name="wa_raw", tag="e", align_bytes=64)
+        nc.sync.dma_start(wa_raw[:, 0, :], words(wa_words, 0))
+        permute_words(wb_raw, 0, 2)
         nc.vector.tensor_copy(
             sc_perm[:].rearrange("p t a (c i) -> p (a c) t i", i=16),
             sc_raw[:].bitcast(U8).rearrange("p a (c i t) -> p (a c) t i", i=16, t=PACK),
         )
+
+        wd_w = keep.tile([P, N], I32, name="wd_w", tag="f", align_bytes=64)
+        nc.sync.dma_start(wd_w[:], words(wd_words, 0))
+        for q in range(QUADS):
+            nc.sync.dma_start(sc_raw[32 * q + 4 : 32 * q + 8, 1, :], wd_scales[0, 4 * q : 4 * q + 4, :].bitcast(I32))
 
         for b in range(J // BANK_COLS):
             cols = slice(b * BANK_COLS, (b + 1) * BANK_COLS)
@@ -197,7 +195,7 @@ def tile_list_htabg_max_res_kernel(
                     nc.tensor.matmul_mx(
                         out=y[:, u, :],
                         lhsT=wd_w[:, nt * P : (nt + 1) * P].bitcast(FP8X4),
-                        lhsT_scale=wd_sc[:, nt * 32 : (nt + 1) * 32].bitcast(U8),
+                        lhsT_scale=sc_raw[4:P, 1, nt * 32 : (nt + 1) * 32].bitcast(U8),
                         rhs=hq[:, ch].bitcast(FP8X4),
                         rhs_scale=hq_sc[:, ch],
                         start=True,
@@ -208,11 +206,15 @@ def tile_list_htabg_max_res_kernel(
                 nc.vector.tensor_tensor(o, y[:], res_sb[c0 // HALF][:, nts, c0 % HALF : c0 % HALF + width], ADD)
                 nc.sync.dma_start(out_rows[:, nts, ch], o)
 
-        for i in range(2):
+        res_rows = res.rearrange("(a p) j -> p a j", p=P)
+        res_sb = []
+        for i, tag in ((0, "d"), (1, "a")):
             for hf in range(2):
                 gather_x(i, hf * HALF, (hf + 1) * HALF)
+            res_sb.append(keep.tile([P, N // P, HALF], F32, name="res_sb%d" % i, tag=tag, align_bytes=64))
+            nc.sync.dma_start(res_sb[i][:], res_rows[:, :, i * HALF : (i + 1) * HALF])
         gather_x(2, 0, HALF)
-        permute_words(2, 3)
+        permute_words(wa_raw, 2, 3)
         for c in range(len(STARTS) - 1):
             if STARTS[c] == HALF:
                 gather_x(2, HALF, J)

@@ -25,7 +25,6 @@ STARTS = (0, 256, 512, 768, 896, 1024)
 DIRECT = ()
 LAG = 1
 BANK_COLS = 128
-SHIFT_ROWS = 100
 
 
 def tile_list_htabg_max_res_kernel(
@@ -35,23 +34,28 @@ def tile_list_htabg_max_res_kernel(
 
     with ExitStack() as ctx:
         keep = ctx.enter_context(tc.tile_pool(name="keep", bufs=1))
+        stage = ctx.enter_context(tc.tile_pool(name="stage", bufs=1))
         ps_h = ctx.enter_context(tc.psum_pool(name="ps_h", bufs=4))
         ps_y = ctx.enter_context(tc.psum_pool(name="ps_y", bufs=4))
 
+        def staged(name, shape, dtype, kib):
+            return stage.tile(shape, dtype, name=name, offset=int(kib * 1024), align_bytes=64)
+
         idx = keep.tile([P, J // 16], U16, name="idx")
         idx2 = keep.tile([P, J // 16], U16, name="idx2")
-        tab_sc = keep.tile([P, T // 4], I32, name="tab_sc", tag="a", align_bytes=64)
-        tab_w = keep.tile([P, T], I32, name="tab_w", tag="b", align_bytes=64)
-        got_sc = keep.tile([P, J // 4], I32, name="got_sc", tag="c", align_bytes=64)
+        tab_sc = staged("tab_sc", [P, T // 4], I32, 7)
+        tab_w = staged("tab_w", [P, T], I32, 16)
+        got_sc = keep.tile([P, J // 4], I32, name="got_sc", align_bytes=64)
         planes = keep.tile([P, 2, J // 4], I32, name="planes", align_bytes=64)
-        got_w = keep.tile([P, J], I32, name="got_w", tag="e", align_bytes=64)
+        got_w = keep.tile([P, J], I32, name="got_w", align_bytes=64)
         part_w = [keep.tile([P, 2, J // 4], I32, name="part_w%d" % i, align_bytes=64) for i in range(2)]
-        wb_raw = keep.tile([P, 2, R], I32, name="wb_raw", tag="f", align_bytes=64)
+        wb_raw = staged("wb_raw", [P, 2, R], I32, 26)
         w_perm = keep.tile([P, PACK, 3, P], I32, name="w_perm", align_bytes=64)
         sc_raw = keep.tile([P, 2, R // 4], I32, name="sc_raw", align_bytes=64)
         sc_perm = keep.tile([P, PACK, 2, P], U8, name="sc_perm", align_bytes=64)
+        sa_perm = keep.tile([P, PACK, 1, P], U8, name="sa_perm", align_bytes=64)
         wgt = keep.tile([P, J], F32, name="wgt", align_bytes=64)
-        x_pl = [keep.tile([P, T], F32, name="x_pl0", tag="d", align_bytes=64)]
+        x_pl = []
         xg = [keep.tile([P, PACK, HALF], F32, name="xg%d" % i, align_bytes=64) for i in range(2)]
         xg_bf = keep.tile([P, J, PACK], BF16, name="xg_bf", align_bytes=64)
         xq = keep.tile([P, J], U32, name="xq", align_bytes=64)
@@ -67,41 +71,44 @@ def tile_list_htabg_max_res_kernel(
             return dram[a].rearrange("p n t -> p (n t)").bitcast(I32)
 
         nc.gpsimd.memset(sc_raw[:], 0)
-        for q in range(QUADS):
-            eng = nc.gpsimd if q < 2 else nc.vector
-            eng.memset(tab_sc[32 * q : 32 * q + 24, :], 0)
-        nc.gpsimd.memset(planes[:], 0)
+        nc.vector.memset(tab_sc[32:64, :], 0)
+        nc.vector.memset(tab_sc[64:128, :], 0)
+        nc.vector.memset(planes[:], 0)
 
         nc.sync.dma_start(idx[:], offs)
-        for q in range(QUADS):
-            nc.sync.dma_start(tab_sc[32 * q + 24 : 32 * q + 32, :], tab_scales[:, 4 * q : 4 * q + 4, :].bitcast(I32))
+        nc.sync.dma_start(tab_sc[0:32, :], tab_scales.rearrange("a r c -> (a r) c").bitcast(I32))
         nc.sync.dma_start(tab_w[:], words(tab_words, 0))
         nc.sync.dma_start(idx2[:], offs2)
         nc.sync.dma_start(
             wb_raw[:], wb_words.rearrange("a p n t -> p a (n t)").bitcast(I32)
         )
+        nc.sync.dma_start(wgt[:], wgt2)
         for q in range(QUADS):
-            nc.sync.dma_start(
+            nc.scalar.dma_start(
                 sc_raw[32 * q : 32 * q + 4, :, :], wb_scales[:, 4 * q : 4 * q + 4, :].rearrange("a r c -> r a c").bitcast(I32)
             )
         x_rows = xT.rearrange("(p i) t -> i p t", i=PACK)
-        nc.sync.dma_start(wgt[:], wgt2)
-        nc.sync.dma_start(x_pl[0][:], x_rows[0])
-        for q in range(QUADS):
-            nc.sync.dma_start(sc_raw[32 * q + 4 : 32 * q + 8, 0, :], wa_scales[0, 4 * q : 4 * q + 4, :].bitcast(I32))
+
+        def load_x(i, kib):
+            x_pl.append(staged("x_pl%d" % i, [P, T], F32, kib))
+            nc.sync.dma_start(x_pl[i][:], x_rows[i])
+
+        def place(a, q):
+            nc.sync.dma_start(planes[32 * q : 32 * q + 4, a, :], got_sc[16 * a + 4 * q : 16 * a + 4 * q + 4, :])
 
         nc.vector.tensor_copy(got_sc[:].bitcast(U8), tab_sc[:].bitcast(U8).indirect(idx[:]))
-        for a in range(2):
-            nc.sync.dma_start(planes[0:SHIFT_ROWS, a, :], got_sc[24 + 4 * a : 24 + 4 * a + SHIFT_ROWS, :])
-        x_pl.append(keep.tile([P, T], F32, name="x_pl1", tag="a", align_bytes=64))
-        nc.sync.dma_start(x_pl[1][:], x_rows[1])
+        for n in range(2 * QUADS):
+            if n == 2:
+                load_x(0, 0)
+            place(n // QUADS, n % QUADS)
+        load_x(1, 8)
         for hf in range(2):
             nc.vector.tensor_copy(
                 got_w[:, hf * 512 : (hf + 1) * 512].bitcast(U32), tab_w[:].bitcast(U32).indirect(idx[:, hf * 32 : (hf + 1) * 32])
             )
-        for i, tag in ((2, "b"), (3, "c")):
-            x_pl.append(keep.tile([P, T], F32, name="x_pl%d" % i, tag=tag, align_bytes=64))
-            nc.sync.dma_start(x_pl[i][:], x_rows[i])
+        load_x(2, 18)
+        wa_raw = staged("wa_raw", [P, 1, R], I32, 16)
+        nc.sync.dma_start(wa_raw[:, 0, :], words(wa_words, 0))
         for hf in range(2):
             src = got_w[:, hf * 512 : (hf + 1) * 512].bitcast(U16).rearrange("p (c i d) -> p c d i", i=8, d=2)
             dst = part_w[hf][:].bitcast(U16).rearrange("p d (c i) -> p c d i", i=8)
@@ -110,21 +117,26 @@ def tile_list_htabg_max_res_kernel(
         def permute_words(raw, a0, a1):
             nc.vector.tensor_copy(
                 w_perm[:, :, a0:a1, :].rearrange("p t a (c i) -> p (a c) t i", i=4),
-                raw[:].rearrange("p a (c i t) -> p (a c) t i", i=4, t=PACK),
+                raw.rearrange("p a (c i t) -> p (a c) t i", i=4, t=PACK),
             )
 
-        wa_raw = keep.tile([P, 1, R], I32, name="wa_raw", tag="e", align_bytes=64)
-        nc.sync.dma_start(wa_raw[:, 0, :], words(wa_words, 0))
-        permute_words(wb_raw, 0, 2)
-        nc.vector.tensor_copy(
-            sc_perm[:].rearrange("p t a (c i) -> p (a c) t i", i=16),
-            sc_raw[:].bitcast(U8).rearrange("p a (c i t) -> p (a c) t i", i=16, t=PACK),
-        )
+        def permute_scales(dst, raw):
+            nc.vector.tensor_copy(
+                dst.rearrange("p t a (c i) -> p (a c) t i", i=16),
+                raw.bitcast(U8).rearrange("p a (c i t) -> p (a c) t i", i=16, t=PACK),
+            )
 
-        wd_w = keep.tile([P, N], I32, name="wd_w", tag="f", align_bytes=64)
-        nc.sync.dma_start(wd_w[:], words(wd_words, 0))
+        permute_scales(sc_perm[:], sc_raw[:])
         for q in range(QUADS):
-            nc.sync.dma_start(sc_raw[32 * q + 4 : 32 * q + 8, 1, :], wd_scales[0, 4 * q : 4 * q + 4, :].bitcast(I32))
+            nc.sync.dma_start(sc_raw[32 * q : 32 * q + 4, 0, :], wa_scales[0, 4 * q : 4 * q + 4, :].bitcast(I32))
+        permute_words(wb_raw[:], 0, 2)
+        load_x(3, 28.5)
+        wd_w = staged("wd_w", [P, N], I32, 26)
+        nc.sync.dma_start(wd_w[:], words(wd_words, 0))
+        wd_sc = staged("wd_sc", [P, N // 4], I32, 28)
+        nc.gpsimd.memset(wd_sc[:], 0)
+        for q in range(QUADS):
+            nc.sync.dma_start(wd_sc[32 * q : 32 * q + 4, :], wd_scales[0, 4 * q : 4 * q + 4, :].bitcast(I32))
 
         for b in range(J // BANK_COLS):
             cols = slice(b * BANK_COLS, (b + 1) * BANK_COLS)
@@ -171,7 +183,7 @@ def tile_list_htabg_max_res_kernel(
                     nc.tensor.matmul_mx(
                         out=acc[:, t, :],
                         lhsT=w_perm[:, t, 2, :].bitcast(FP8X4),
-                        lhsT_scale=sc_perm[4:P, t, 0, :],
+                        lhsT_scale=sa_perm[:, t, 0, :],
                         rhs=xq[:, cols].bitcast(FP8X4),
                         rhs_scale=xq_sc[:, cols],
                         start=True,
@@ -195,7 +207,7 @@ def tile_list_htabg_max_res_kernel(
                     nc.tensor.matmul_mx(
                         out=y[:, u, :],
                         lhsT=wd_w[:, nt * P : (nt + 1) * P].bitcast(FP8X4),
-                        lhsT_scale=sc_raw[4:P, 1, nt * 32 : (nt + 1) * 32].bitcast(U8),
+                        lhsT_scale=wd_sc[:, nt * 32 : (nt + 1) * 32].bitcast(U8),
                         rhs=hq[:, ch].bitcast(FP8X4),
                         rhs_scale=hq_sc[:, ch],
                         start=True,
@@ -208,13 +220,14 @@ def tile_list_htabg_max_res_kernel(
 
         res_rows = res.rearrange("(a p) j -> p a j", p=P)
         res_sb = []
-        for i, tag in ((0, "d"), (1, "a")):
+        for i in range(2):
             for hf in range(2):
                 gather_x(i, hf * HALF, (hf + 1) * HALF)
-            res_sb.append(keep.tile([P, N // P, HALF], F32, name="res_sb%d" % i, tag=tag, align_bytes=64))
+            res_sb.append(staged("res_sb%d" % i, [P, N // P, HALF], F32, 8 * i))
             nc.sync.dma_start(res_sb[i][:], res_rows[:, :, i * HALF : (i + 1) * HALF])
         gather_x(2, 0, HALF)
-        permute_words(wa_raw, 2, 3)
+        permute_words(wa_raw[:], 2, 3)
+        permute_scales(sa_perm[:], sc_raw[:, 0:1, :])
         for c in range(len(STARTS) - 1):
             if STARTS[c] == HALF:
                 gather_x(2, HALF, J)

@@ -21,6 +21,7 @@ P = 128
 PACK = 4
 QUADS = 4
 HALF = J // 2
+EARLY = 896
 STARTS = (0, 256, 512, 768, 896, 1024)
 DIRECT = ()
 LAG = 1
@@ -43,20 +44,19 @@ def tile_list_htabg_max_res_kernel(
 
         idx = keep.tile([P, J // 16], U16, name="idx")
         idx2 = keep.tile([P, J // 16], U16, name="idx2")
-        tab_sc = staged("tab_sc", [P, T // 4], I32, 7)
-        tab_w = staged("tab_w", [P, T], I32, 16)
-        got_sc = keep.tile([P, J // 4], I32, name="got_sc", align_bytes=64)
-        planes = keep.tile([P, 2, J // 4], I32, name="planes", align_bytes=64)
-        got_w = keep.tile([P, J], I32, name="got_w", align_bytes=64)
-        part_w = [keep.tile([P, 2, J // 4], I32, name="part_w%d" % i, align_bytes=64) for i in range(2)]
-        wb_raw = staged("wb_raw", [P, 2, R], I32, 26)
-        w_perm = keep.tile([P, PACK, 3, P], I32, name="w_perm", align_bytes=64)
+        tab_sc = keep.tile([P, T // 4], I32, name="tab_sc", align_bytes=64)
+        tab_w = staged("tab_w", [P, T], I32, 29)
+        got_sc = staged("got_sc", [P, J // 4], I32, 15.5)
+        got_w = staged("got_w", [P, J], I32, 41)
+        part_w = keep.tile([P, 2, J // 2], I32, name="part_w", align_bytes=64)
+        wb_raw = staged("wb_raw", [P, 2, R], I32, 37)
+        w_perm = keep.tile([P, PACK, 4, P], I32, name="w_perm", align_bytes=64)
         sc_raw = keep.tile([P, 2, R // 4], I32, name="sc_raw", align_bytes=64)
-        sc_perm = keep.tile([P, PACK, 2, P], U8, name="sc_perm", align_bytes=64)
-        sa_perm = keep.tile([P, PACK, 1, P], U8, name="sa_perm", align_bytes=64)
-        wgt = keep.tile([P, J], F32, name="wgt", align_bytes=64)
+        rows = keep.tile([P, 2, J // 4], I32, name="rows", align_bytes=64)
+        planes = [rows, keep.tile([P, 2, J // 4], I32, name="plane1", align_bytes=64)]
+        wgt = keep.tile([P, EARLY], F32, name="wgt", align_bytes=64)
         x_pl = []
-        xg = [keep.tile([P, PACK, HALF], F32, name="xg%d" % i, align_bytes=64) for i in range(2)]
+        xg = keep.tile([P, PACK, J], F32, name="xg", align_bytes=64)
         xg_bf = keep.tile([P, J, PACK], BF16, name="xg_bf", align_bytes=64)
         xq = keep.tile([P, J], U32, name="xq", align_bytes=64)
         xq_sc = keep.tile([P, J], U8, name="xq_sc", align_bytes=64)
@@ -70,73 +70,66 @@ def tile_list_htabg_max_res_kernel(
         def words(dram, a):
             return dram[a].rearrange("p n t -> p (n t)").bitcast(I32)
 
-        nc.gpsimd.memset(sc_raw[:], 0)
-        nc.vector.memset(tab_sc[32:64, :], 0)
-        nc.vector.memset(tab_sc[64:128, :], 0)
-        nc.vector.memset(planes[:], 0)
+        for p0, p1 in ((32, 64), (64, P)):
+            nc.vector.memset(tab_sc[p0:p1, :], 0)
+            nc.gpsimd.memset(sc_raw[p0:p1, :, :], 0)
+        nc.gpsimd.memset(planes[1][:], 0)
 
         nc.sync.dma_start(idx[:], offs)
         nc.sync.dma_start(tab_sc[0:32, :], tab_scales.rearrange("a r c -> (a r) c").bitcast(I32))
-        nc.sync.dma_start(tab_w[:], words(tab_words, 0))
+        nc.sync.dma_start(sc_raw[0:32, 0, :], wb_scales.rearrange("a r c -> (a r) c").bitcast(I32))
+        nc.sync.dma_start(sc_raw[0:16, 1, :], wa_scales[0].bitcast(I32))
+        nc.sync.dma_start(sc_raw[16:32, 1, :], wd_scales[0].bitcast(I32))
         nc.sync.dma_start(idx2[:], offs2)
+        nc.sync.dma_start(tab_w[:], words(tab_words, 0))
         nc.sync.dma_start(
             wb_raw[:], wb_words.rearrange("a p n t -> p a (n t)").bitcast(I32)
         )
-        nc.sync.dma_start(wgt[:], wgt2)
-        for q in range(QUADS):
-            nc.scalar.dma_start(
-                sc_raw[32 * q : 32 * q + 4, :, :], wb_scales[:, 4 * q : 4 * q + 4, :].rearrange("a r c -> r a c").bitcast(I32)
-            )
+        nc.sync.dma_start(wgt[:], wgt2[:, 0:EARLY])
         x_rows = xT.rearrange("(p i) t -> i p t", i=PACK)
 
-        def load_x(i, kib):
-            x_pl.append(staged("x_pl%d" % i, [P, T], F32, kib))
+        def load_x(i):
+            x_pl.append(staged("x_pl%d" % i, [P, T], F32, 8 * i))
             nc.sync.dma_start(x_pl[i][:], x_rows[i])
 
-        def place(a, q):
-            nc.sync.dma_start(planes[32 * q : 32 * q + 4, a, :], got_sc[16 * a + 4 * q : 16 * a + 4 * q + 4, :])
-
-        nc.vector.tensor_copy(got_sc[:].bitcast(U8), tab_sc[:].bitcast(U8).indirect(idx[:]))
-        for n in range(2 * QUADS):
-            if n == 2:
-                load_x(0, 0)
-            place(n // QUADS, n % QUADS)
-        load_x(1, 8)
-        for hf in range(2):
-            nc.vector.tensor_copy(
-                got_w[:, hf * 512 : (hf + 1) * 512].bitcast(U32), tab_w[:].bitcast(U32).indirect(idx[:, hf * 32 : (hf + 1) * 32])
-            )
-        load_x(2, 18)
-        wa_raw = staged("wa_raw", [P, 1, R], I32, 16)
-        nc.sync.dma_start(wa_raw[:, 0, :], words(wa_words, 0))
-        for hf in range(2):
-            src = got_w[:, hf * 512 : (hf + 1) * 512].bitcast(U16).rearrange("p (c i d) -> p c d i", i=8, d=2)
-            dst = part_w[hf][:].bitcast(U16).rearrange("p d (c i) -> p c d i", i=8)
-            nc.vector.tensor_copy(dst, src)
-
-        def permute_words(raw, a0, a1):
-            nc.vector.tensor_copy(
+        def permute_words(eng, raw, a0, a1):
+            eng.tensor_copy(
                 w_perm[:, :, a0:a1, :].rearrange("p t a (c i) -> p (a c) t i", i=4),
                 raw.rearrange("p a (c i t) -> p (a c) t i", i=4, t=PACK),
             )
 
-        def permute_scales(dst, raw):
-            nc.vector.tensor_copy(
-                dst.rearrange("p t a (c i) -> p (a c) t i", i=16),
-                raw.bitcast(U8).rearrange("p a (c i t) -> p (a c) t i", i=16, t=PACK),
-            )
+        def weight_scale(a, t, k):
+            return planes[a][:, 1, (2 * t + k) * 32 : (2 * t + k + 1) * 32].bitcast(U8)
 
-        permute_scales(sc_perm[:], sc_raw[:])
-        for q in range(QUADS):
-            nc.sync.dma_start(sc_raw[32 * q : 32 * q + 4, 0, :], wa_scales[0, 4 * q : 4 * q + 4, :].bitcast(I32))
-        permute_words(wb_raw[:], 0, 2)
-        load_x(3, 28.5)
-        wd_w = staged("wd_w", [P, N], I32, 26)
-        nc.sync.dma_start(wd_w[:], words(wd_words, 0))
-        wd_sc = staged("wd_sc", [P, N // 4], I32, 28)
-        nc.gpsimd.memset(wd_sc[:], 0)
-        for q in range(QUADS):
-            nc.sync.dma_start(wd_sc[32 * q : 32 * q + 4, :], wd_scales[0, 4 * q : 4 * q + 4, :].bitcast(I32))
+        load_x(0)
+        nc.vector.tensor_copy(got_sc[:].bitcast(U8), tab_sc[:].bitcast(U8).indirect(idx[:]))
+        nc.vector.tensor_copy(rows[:, 0, :], got_sc[:])
+        nc.gpsimd.tensor_copy(
+            rows[:, 1, :].bitcast(U8).rearrange("p (t a c i) -> p (a c) t i", t=PACK, a=2, i=16),
+            sc_raw[:].bitcast(U8).rearrange("p a (c i t) -> p (a c) t i", i=16, t=PACK),
+        )
+        for n in range(1, 2 * QUADS):
+            if n == 6:
+                load_x(1)
+            a, q = divmod(n, QUADS)
+            nc.sync.dma_start(planes[a][32 * q : 32 * q + 4, :, :], rows[16 * a + 4 * q : 16 * a + 4 * q + 4, :, :])
+        load_x(2)
+        nc.vector.tensor_copy(got_w[:].bitcast(U32), tab_w[:].bitcast(U32).indirect(idx[:]))
+        load_x(3)
+        wgt_late = staged("wgt_late", [P, J - EARLY], F32, 32)
+        nc.sync.dma_start(wgt_late[:], wgt2[:, EARLY:J])
+        late_w = staged("late_w", [P, 2, R], I32, 33)
+        nc.sync.dma_start(late_w[:, 0, :], words(wa_words, 0))
+        nc.sync.dma_start(late_w[:, 1, :], words(wd_words, 0))
+        nc.vector.tensor_copy(
+            part_w[:].bitcast(U16).rearrange("p d (c i) -> p c d i", i=8),
+            got_w[:].bitcast(U16).rearrange("p (c i d) -> p c d i", i=8, d=2),
+        )
+        permute_words(nc.gpsimd, wb_raw[:], 0, 2)
+        res_rows = res.rearrange("(p a) j -> p a j", a=PACK)
+        res_sb = staged("res_sb", [P, 2, N // P, HALF], F32, 41)
+        for i in range(2):
+            nc.sync.dma_start(res_sb[:, i, :, :], res_rows[:, :, i * HALF : (i + 1) * HALF])
 
         for b in range(J // BANK_COLS):
             cols = slice(b * BANK_COLS, (b + 1) * BANK_COLS)
@@ -146,28 +139,27 @@ def tile_list_htabg_max_res_kernel(
                     nc.tensor.matmul_mx(
                         out=acc[:, t, :],
                         lhsT=w_perm[:, t, a, :].bitcast(FP8X4),
-                        lhsT_scale=sc_perm[:, t, a, :],
-                        rhs=part_w[b // 4][:, a, b % 4 * 64 : (b % 4 + 1) * 64].bitcast(U8).bitcast(FP4X4),
-                        rhs_scale=planes[:, a, :].bitcast(U8)[:, cols],
+                        lhsT_scale=weight_scale(a, t, 0),
+                        rhs=part_w[:, a, b * 64 : (b + 1) * 64].bitcast(U8).bitcast(FP4X4),
+                        rhs_scale=planes[a][:, 0, :].bitcast(U8)[:, cols],
                         start=(a == 0),
                         stop=(a == 1),
                     )
             nc.scalar.copy(yb_bf[:, cols, :], acc[:].rearrange("p t n -> p n t"))
 
         def gather_x(i, c0, c1):
-            nc.vector.tensor_tensor(
-                xg[c0 // HALF][:, i, c0 % HALF : c0 % HALF + c1 - c0], x_pl[i][:].indirect(idx2[:, c0 // 16 : c1 // 16]), wgt[:, c0:c1], MULT
-            )
+            factor = wgt[:, c0:c1] if c0 < EARLY else wgt_late[:, c0 - EARLY : c1 - EARLY]
+            nc.vector.tensor_tensor(xg[:, i, c0:c1], x_pl[i][:].indirect(idx2[:, c0 // 16 : c1 // 16]), factor, MULT)
 
-        out_rows = out.rearrange("(a p) j -> p a j", p=P)
+        out_rows = out.rearrange("(p a) j -> p a j", a=PACK)
 
         def front(c):
             c0, c1 = STARTS[c], STARTS[c + 1]
-            hf, h0 = divmod(c0, HALF)
-            gather_x(3, c0, c1)
+            if c0 < EARLY:
+                gather_x(3, c0, c1)
             nc.scalar.copy(
                 xg_bf[:, c0:c1, :].rearrange("p (c k) t -> p c t k", k=4),
-                xg[hf][:, :, h0 : h0 + c1 - c0].rearrange("p t (c k) -> p c t k", k=4),
+                xg[:, :, c0:c1].rearrange("p t (c k) -> p c t k", k=4),
             )
 
         def chain(c):
@@ -183,7 +175,7 @@ def tile_list_htabg_max_res_kernel(
                     nc.tensor.matmul_mx(
                         out=acc[:, t, :],
                         lhsT=w_perm[:, t, 2, :].bitcast(FP8X4),
-                        lhsT_scale=sa_perm[:, t, 0, :],
+                        lhsT_scale=weight_scale(0, t, 1),
                         rhs=xq[:, cols].bitcast(FP8X4),
                         rhs_scale=xq_sc[:, cols],
                         start=True,
@@ -206,8 +198,8 @@ def tile_list_htabg_max_res_kernel(
                     nt = per_bank * g + u
                     nc.tensor.matmul_mx(
                         out=y[:, u, :],
-                        lhsT=wd_w[:, nt * P : (nt + 1) * P].bitcast(FP8X4),
-                        lhsT_scale=wd_sc[:, nt * 32 : (nt + 1) * 32].bitcast(U8),
+                        lhsT=w_perm[:, nt, 3, :].bitcast(FP8X4),
+                        lhsT_scale=weight_scale(1, nt, 1),
                         rhs=hq[:, ch].bitcast(FP8X4),
                         rhs_scale=hq_sc[:, ch],
                         start=True,
@@ -215,22 +207,16 @@ def tile_list_htabg_max_res_kernel(
                     )
                 nts = slice(per_bank * g, per_bank * (g + 1))
                 o = o_sb[:, c0 // BANK_COLS + g, :].rearrange("p (u n) -> p u n", u=per_bank)
-                nc.vector.tensor_tensor(o, y[:], res_sb[c0 // HALF][:, nts, c0 % HALF : c0 % HALF + width], ADD)
+                nc.vector.tensor_tensor(o, y[:], res_sb[:, c0 // HALF, nts, c0 % HALF : c0 % HALF + width], ADD)
                 nc.sync.dma_start(out_rows[:, nts, ch], o)
 
-        res_rows = res.rearrange("(a p) j -> p a j", p=P)
-        res_sb = []
-        for i in range(2):
-            for hf in range(2):
-                gather_x(i, hf * HALF, (hf + 1) * HALF)
-            res_sb.append(staged("res_sb%d" % i, [P, N // P, HALF], F32, 8 * i))
-            nc.sync.dma_start(res_sb[i][:], res_rows[:, :, i * HALF : (i + 1) * HALF])
-        gather_x(2, 0, HALF)
-        permute_words(wa_raw[:], 2, 3)
-        permute_scales(sa_perm[:], sc_raw[:, 0:1, :])
+        for i in range(3):
+            gather_x(i, 0, EARLY)
+        permute_words(nc.vector, late_w[:], 2, 4)
         for c in range(len(STARTS) - 1):
-            if STARTS[c] == HALF:
-                gather_x(2, HALF, J)
+            if STARTS[c] == EARLY:
+                for i in range(PACK):
+                    gather_x(i, EARLY, J)
             front(c)
             if c >= LAG:
                 chain(c - LAG)

@@ -23,8 +23,6 @@ QUADS = 4
 HALF = J // 2
 EARLY = 896
 STARTS = (0, 256, 512, 768, 896, 1024)
-DIRECT = ()
-LAG = 1
 BANK_COLS = 128
 
 
@@ -46,12 +44,12 @@ def tile_list_htabg_max_res_kernel(
         idx2 = keep.tile([P, J // 16], U16, name="idx2")
         tab_sc = keep.tile([P, T // 4], I32, name="tab_sc", align_bytes=64)
         tab_w = staged("tab_w", [P, T], I32, 29)
-        got_sc = staged("got_sc", [P, J // 4], I32, 15.5)
+        got_sc = keep.tile([P, J // 4], I32, name="got_sc", align_bytes=64)
         got_w = staged("got_w", [P, J], I32, 41)
         part_w = keep.tile([P, 2, J // 2], I32, name="part_w", align_bytes=64)
         wb_raw = staged("wb_raw", [P, 2, R], I32, 37)
         w_perm = keep.tile([P, PACK, 4, P], I32, name="w_perm", align_bytes=64)
-        sc_raw = keep.tile([P, 2, R // 4], I32, name="sc_raw", align_bytes=64)
+        sc_raw = staged("sc_raw", [P, 2, R // 4], I32, 15.5)
         rows = keep.tile([P, 2, J // 4], I32, name="rows", align_bytes=64)
         planes = [rows, keep.tile([P, 2, J // 4], I32, name="plane1", align_bytes=64)]
         wgt = keep.tile([P, EARLY], F32, name="wgt", align_bytes=64)
@@ -104,7 +102,7 @@ def tile_list_htabg_max_res_kernel(
         load_x(0)
         nc.vector.tensor_copy(got_sc[:].bitcast(U8), tab_sc[:].bitcast(U8).indirect(idx[:]))
         nc.vector.tensor_copy(rows[:, 0, :], got_sc[:])
-        nc.gpsimd.tensor_copy(
+        nc.vector.tensor_copy(
             rows[:, 1, :].bitcast(U8).rearrange("p (t a c i) -> p (a c) t i", t=PACK, a=2, i=16),
             sc_raw[:].bitcast(U8).rearrange("p a (c i t) -> p (a c) t i", i=16, t=PACK),
         )
@@ -125,7 +123,7 @@ def tile_list_htabg_max_res_kernel(
             part_w[:].bitcast(U16).rearrange("p d (c i) -> p c d i", i=8),
             got_w[:].bitcast(U16).rearrange("p (c i d) -> p c d i", i=8, d=2),
         )
-        permute_words(nc.gpsimd, wb_raw[:], 0, 2)
+        permute_words(nc.vector, wb_raw[:], 0, 2)
         res_rows = res.rearrange("(p a) j -> p a j", a=PACK)
         res_sb = staged("res_sb", [P, 2, N // P, HALF], F32, 41)
         for i in range(2):
@@ -162,7 +160,7 @@ def tile_list_htabg_max_res_kernel(
                 xg[:, :, c0:c1].rearrange("p t (c k) -> p c t k", k=4),
             )
 
-        def chain(c):
+        def first(c):
             c0, c1 = STARTS[c], STARTS[c + 1]
             ch = slice(c0, c1)
             nc.vector.quantize_mx(
@@ -181,12 +179,17 @@ def tile_list_htabg_max_res_kernel(
                         start=True,
                         stop=True,
                     )
-                if c in DIRECT:
-                    nc.vector.tensor_tensor(h_bf[:, cols, :], acc[:].rearrange("p t n -> p n t"), yb_bf[:, cols, :], MAX)
-                else:
-                    nc.scalar.copy(ya_bf[:, cols, :], acc[:].rearrange("p t n -> p n t"))
-            if c not in DIRECT:
-                nc.vector.tensor_tensor(h_bf[:, ch, :], ya_bf[:, ch, :], yb_bf[:, ch, :], MAX)
+                nc.scalar.copy(ya_bf[:, cols, :], acc[:].rearrange("p t n -> p n t"))
+
+        def join(c):
+            ch = slice(STARTS[c], STARTS[c + 1])
+            nc.vector.tensor_tensor(h_bf[:, ch, :], ya_bf[:, ch, :], yb_bf[:, ch, :], MAX)
+
+        sums = {}
+
+        def second(c):
+            c0, c1 = STARTS[c], STARTS[c + 1]
+            ch = slice(c0, c1)
             nc.vector.quantize_mx(
                 out=hq[:, ch].bitcast(FP8X4), scales=hq_sc[:, ch], in_=h_bf[:, ch, :].rearrange("p n t -> p (n t)")
             )
@@ -205,20 +208,34 @@ def tile_list_htabg_max_res_kernel(
                         start=True,
                         stop=True,
                     )
-                nts = slice(per_bank * g, per_bank * (g + 1))
-                o = o_sb[:, c0 // BANK_COLS + g, :].rearrange("p (u n) -> p u n", u=per_bank)
-                nc.vector.tensor_tensor(o, y[:], res_sb[:, c0 // HALF, nts, c0 % HALF : c0 % HALF + width], ADD)
-                nc.sync.dma_start(out_rows[:, nts, ch], o)
+                sums[c, g] = y
+
+        def finish(c, g):
+            if (c, g) not in sums:
+                return
+            c0, c1 = STARTS[c], STARTS[c + 1]
+            width = c1 - c0
+            per_bank = 512 // width
+            nts = slice(per_bank * g, per_bank * (g + 1))
+            o = o_sb[:, c0 // BANK_COLS + g, :].rearrange("p (u n) -> p u n", u=per_bank)
+            nc.vector.tensor_tensor(o, sums[c, g][:], res_sb[:, c0 // HALF, nts, c0 % HALF : c0 % HALF + width], ADD)
+            nc.sync.dma_start(out_rows[:, nts, c0:c1], o)
 
         for i in range(3):
             gather_x(i, 0, EARLY)
         permute_words(nc.vector, late_w[:], 2, 4)
-        for c in range(len(STARTS) - 1):
-            if STARTS[c] == EARLY:
-                for i in range(PACK):
-                    gather_x(i, EARLY, J)
-            front(c)
-            if c >= LAG:
-                chain(c - LAG)
-        for c in range(len(STARTS) - 1 - LAG, len(STARTS) - 1):
-            chain(c)
+        chunks = len(STARTS) - 1
+        for s in range(chunks + 3):
+            if s < chunks:
+                if STARTS[s] == EARLY:
+                    for i in range(PACK):
+                        gather_x(i, EARLY, J)
+                front(s)
+            if 0 <= s - 1 < chunks:
+                first(s - 1)
+            if 0 <= s - 2 < chunks:
+                join(s - 2)
+            finish(s - 3, 0)
+            if 0 <= s - 2 < chunks:
+                second(s - 2)
+            finish(s - 3, 1)

@@ -21,7 +21,6 @@ P = 128
 PACK = 4
 QUADS = 4
 HALF = J // 2
-EARLY = 896
 STARTS = (0, 256, 512, 768, 896, 1024)
 BANK_COLS = 128
 
@@ -52,7 +51,7 @@ def tile_list_htabg_max_res_kernel(
         sc_raw = staged("sc_raw", [P, 2, R // 4], I32, 15.5)
         rows = keep.tile([P, 2, J // 4], I32, name="rows", align_bytes=64)
         planes = [rows, keep.tile([P, 2, J // 4], I32, name="plane1", align_bytes=64)]
-        wgt = keep.tile([P, EARLY], F32, name="wgt", align_bytes=64)
+        wgt = keep.tile([P, J], F32, name="wgt", align_bytes=64)
         x_pl = []
         xg = keep.tile([P, PACK, J], F32, name="xg", align_bytes=64)
         xg_bf = keep.tile([P, J, PACK], BF16, name="xg_bf", align_bytes=64)
@@ -83,7 +82,7 @@ def tile_list_htabg_max_res_kernel(
         nc.sync.dma_start(
             wb_raw[:], wb_words.rearrange("a p n t -> p a (n t)").bitcast(I32)
         )
-        nc.sync.dma_start(wgt[:], wgt2[:, 0:EARLY])
+        nc.sync.dma_start(wgt[:], wgt2)
         x_rows = xT.rearrange("(p i) t -> i p t", i=PACK)
 
         def load_x(i):
@@ -114,8 +113,6 @@ def tile_list_htabg_max_res_kernel(
         load_x(2)
         nc.vector.tensor_copy(got_w[:].bitcast(U32), tab_w[:].bitcast(U32).indirect(idx[:]))
         load_x(3)
-        wgt_late = staged("wgt_late", [P, J - EARLY], F32, 32)
-        nc.sync.dma_start(wgt_late[:], wgt2[:, EARLY:J])
         late_w = staged("late_w", [P, 2, R], I32, 33)
         nc.sync.dma_start(late_w[:, 0, :], words(wa_words, 0))
         nc.sync.dma_start(late_w[:, 1, :], words(wd_words, 0))
@@ -146,15 +143,13 @@ def tile_list_htabg_max_res_kernel(
             nc.scalar.copy(yb_bf[:, cols, :], acc[:].rearrange("p t n -> p n t"))
 
         def gather_x(i, c0, c1):
-            factor = wgt[:, c0:c1] if c0 < EARLY else wgt_late[:, c0 - EARLY : c1 - EARLY]
-            nc.vector.tensor_tensor(xg[:, i, c0:c1], x_pl[i][:].indirect(idx2[:, c0 // 16 : c1 // 16]), factor, MULT)
+            nc.vector.tensor_tensor(xg[:, i, c0:c1], x_pl[i][:].indirect(idx2[:, c0 // 16 : c1 // 16]), wgt[:, c0:c1], MULT)
 
         out_rows = out.rearrange("(p a) j -> p a j", a=PACK)
 
         def front(c):
             c0, c1 = STARTS[c], STARTS[c + 1]
-            if c0 < EARLY:
-                gather_x(3, c0, c1)
+            gather_x(3, c0, c1)
             nc.scalar.copy(
                 xg_bf[:, c0:c1, :].rearrange("p (c k) t -> p c t k", k=4),
                 xg[:, :, c0:c1].rearrange("p t (c k) -> p c t k", k=4),
@@ -222,14 +217,11 @@ def tile_list_htabg_max_res_kernel(
             nc.sync.dma_start(out_rows[:, nts, c0:c1], o)
 
         for i in range(3):
-            gather_x(i, 0, EARLY)
+            gather_x(i, 0, J)
         permute_words(nc.vector, late_w[:], 2, 4)
         chunks = len(STARTS) - 1
         for s in range(chunks + 3):
             if s < chunks:
-                if STARTS[s] == EARLY:
-                    for i in range(PACK):
-                        gather_x(i, EARLY, J)
                 front(s)
             if 0 <= s - 1 < chunks:
                 first(s - 1)

@@ -1,6 +1,7 @@
 from contextlib import ExitStack
 
 import concourse.mybir as mybir
+from concourse.masks import make_identity
 
 K, L, R, N, T, J = 512, 1024, 512, 512, 2048, 1024
 FLOPS = 2 * J * (K * R + L * R + R * N)
@@ -44,7 +45,7 @@ def tile_list_htabg_max_res_kernel(
         tab_sc = keep.tile([P, T // 4], I32, name="tab_sc", align_bytes=64)
         tab_w = staged("tab_w", [P, T], I32, 29)
         got_sc = keep.tile([P, J // 4], I32, name="got_sc", align_bytes=64)
-        got_w = staged("got_w", [P, J], I32, 41)
+        got_w = keep.tile([P, J], I32, name="got_w", align_bytes=64)
         part_w = keep.tile([P, 2, J // 2], I32, name="part_w", align_bytes=64)
         wb_raw = staged("wb_raw", [P, 2, R], I32, 37)
         w_perm = keep.tile([P, PACK, 4, P], I32, name="w_perm", align_bytes=64)
@@ -52,6 +53,9 @@ def tile_list_htabg_max_res_kernel(
         rows = keep.tile([P, 2, J // 4], I32, name="rows", align_bytes=64)
         planes = [rows, keep.tile([P, 2, J // 4], I32, name="plane1", align_bytes=64)]
         wgt = keep.tile([P, J], F32, name="wgt", align_bytes=64)
+        wgt_rows = keep.tile([P, P], F32, name="wgt_rows", align_bytes=64)
+        wgt_t = keep.tile([P, J // P, P], F32, name="wgt_t", align_bytes=64)
+        ident = keep.tile([P, P], F32, name="ident", align_bytes=64)
         x_pl = []
         xg = keep.tile([P, PACK, J], F32, name="xg", align_bytes=64)
         xg_bf = keep.tile([P, J, PACK], BF16, name="xg_bf", align_bytes=64)
@@ -70,6 +74,8 @@ def tile_list_htabg_max_res_kernel(
         for p0, p1 in ((32, 64), (64, P)):
             nc.vector.memset(tab_sc[p0:p1, :], 0)
             nc.gpsimd.memset(sc_raw[p0:p1, :, :], 0)
+        nc.gpsimd.memset(wgt_rows[64:P, :], 0.0)
+        make_identity(nc, ident[:])
         nc.gpsimd.memset(planes[1][:], 0)
 
         nc.sync.dma_start(idx[:], offs)
@@ -78,11 +84,13 @@ def tile_list_htabg_max_res_kernel(
         nc.sync.dma_start(sc_raw[0:16, 1, :], wa_scales[0].bitcast(I32))
         nc.sync.dma_start(sc_raw[16:32, 1, :], wd_scales[0].bitcast(I32))
         nc.sync.dma_start(idx2[:], offs2)
+        nc.sync.dma_start(
+            wgt_rows[0:64, :], wgt2.rearrange("(g r) j -> g r j", r=16)[:, 0, :].rearrange("g (b k) -> g b k", k=P)
+        )
         nc.sync.dma_start(tab_w[:], words(tab_words, 0))
         nc.sync.dma_start(
             wb_raw[:], wb_words.rearrange("a p n t -> p a (n t)").bitcast(I32)
         )
-        nc.sync.dma_start(wgt[:], wgt2)
         x_rows = xT.rearrange("(p i) t -> i p t", i=PACK)
 
         def load_x(i):
@@ -99,6 +107,17 @@ def tile_list_htabg_max_res_kernel(
             return planes[a][:, 1, (2 * t + k) * 32 : (2 * t + k + 1) * 32].bitcast(U8)
 
         load_x(0)
+        turned = ps_y.tile([P, 512], F32, name="y")
+        nc.tensor.transpose(turned[:, 0:P], wgt_rows[:], ident[:])
+        nc.scalar.copy(
+            wgt_t[:].rearrange("p b (g r) -> p b g r", r=16),
+            turned[:, 0:64].rearrange("p (g b) -> p b g", g=8).unsqueeze(3).to_broadcast([P, 8, 8, 16]),
+        )
+        for hf in range(2):
+            spread = ps_y.tile([P, 512], F32, name="y")
+            for u in range(4):
+                nc.tensor.transpose(spread[:, u * P : (u + 1) * P], wgt_t[:, 4 * hf + u, :], ident[:])
+            nc.scalar.copy(wgt[:, hf * HALF : (hf + 1) * HALF], spread[:])
         nc.vector.tensor_copy(got_sc[:].bitcast(U8), tab_sc[:].bitcast(U8).indirect(idx[:]))
         nc.vector.tensor_copy(rows[:, 0, :], got_sc[:])
         nc.vector.tensor_copy(
@@ -113,18 +132,11 @@ def tile_list_htabg_max_res_kernel(
         load_x(2)
         nc.vector.tensor_copy(got_w[:].bitcast(U32), tab_w[:].bitcast(U32).indirect(idx[:]))
         load_x(3)
-        late_w = staged("late_w", [P, 2, R], I32, 33)
-        nc.sync.dma_start(late_w[:, 0, :], words(wa_words, 0))
-        nc.sync.dma_start(late_w[:, 1, :], words(wd_words, 0))
         nc.vector.tensor_copy(
             part_w[:].bitcast(U16).rearrange("p d (c i) -> p c d i", i=8),
             got_w[:].bitcast(U16).rearrange("p (c i d) -> p c d i", i=8, d=2),
         )
         permute_words(nc.vector, wb_raw[:], 0, 2)
-        res_rows = res.rearrange("(p a) j -> p a j", a=PACK)
-        res_sb = staged("res_sb", [P, 2, N // P, HALF], F32, 41)
-        for i in range(2):
-            nc.sync.dma_start(res_sb[:, i, :, :], res_rows[:, :, i * HALF : (i + 1) * HALF])
 
         for b in range(J // BANK_COLS):
             cols = slice(b * BANK_COLS, (b + 1) * BANK_COLS)
@@ -213,21 +225,29 @@ def tile_list_htabg_max_res_kernel(
             per_bank = 512 // width
             nts = slice(per_bank * g, per_bank * (g + 1))
             o = o_sb[:, c0 // BANK_COLS + g, :].rearrange("p (u n) -> p u n", u=per_bank)
-            nc.vector.tensor_tensor(o, sums[c, g][:], res_sb[:, c0 // HALF, nts, c0 % HALF : c0 % HALF + width], ADD)
+            nc.vector.tensor_tensor(o, sums[c, g][:], res_sb[c0 // HALF][:, nts, c0 % HALF : c0 % HALF + width], ADD)
             nc.sync.dma_start(out_rows[:, nts, c0:c1], o)
 
-        for i in range(3):
-            gather_x(i, 0, J)
+        gather_x(0, 0, J)
+        late_w = staged("late_w", [P, 2, R], I32, 0)
+        nc.sync.dma_start(late_w[:, 0, :], words(wa_words, 0))
+        nc.sync.dma_start(late_w[:, 1, :], words(wd_words, 0))
+        res_rows = res.rearrange("(p a) j -> p a j", a=PACK)
+        res_sb = []
+        for i in range(2):
+            gather_x(i + 1, 0, J)
+            res_sb.append(staged("res_sb%d" % i, [P, N // P, HALF], F32, 8 * (i + 1)))
+            nc.sync.dma_start(res_sb[i][:], res_rows[:, :, i * HALF : (i + 1) * HALF])
         permute_words(nc.vector, late_w[:], 2, 4)
         chunks = len(STARTS) - 1
-        for s in range(chunks + 3):
+        for s in range(chunks + 4):
             if s < chunks:
                 front(s)
-            if 0 <= s - 1 < chunks:
-                first(s - 1)
             if 0 <= s - 2 < chunks:
-                join(s - 2)
-            finish(s - 3, 0)
-            if 0 <= s - 2 < chunks:
-                second(s - 2)
-            finish(s - 3, 1)
+                first(s - 2)
+            if 0 <= s - 3 < chunks:
+                join(s - 3)
+            finish(s - 4, 0)
+            if 0 <= s - 3 < chunks:
+                second(s - 3)
+            finish(s - 4, 1)

@@ -24,6 +24,7 @@ QUADS = 4
 HALF = J // 2
 STARTS = (0, 256, 512, 768, 896, 1024)
 BANK_COLS = 128
+KEPT = 6
 
 
 def tile_list_htabg_max_res_kernel(
@@ -125,7 +126,7 @@ def tile_list_htabg_max_res_kernel(
             sc_raw[:].bitcast(U8).rearrange("p a (c i t) -> p (a c) t i", i=16, t=PACK),
         )
         for n in range(1, 2 * QUADS):
-            if n == 6:
+            if n == 7:
                 load_x(1)
             a, q = divmod(n, QUADS)
             nc.sync.dma_start(planes[a][32 * q : 32 * q + 4, :, :], rows[16 * a + 4 * q : 16 * a + 4 * q + 4, :, :])
@@ -138,9 +139,13 @@ def tile_list_htabg_max_res_kernel(
         )
         permute_words(nc.vector, wb_raw[:], 0, 2)
 
+        waiting = []
         for b in range(J // BANK_COLS):
             cols = slice(b * BANK_COLS, (b + 1) * BANK_COLS)
-            acc = ps_h.tile([P, PACK, BANK_COLS], F32, name="acc")
+            if b < KEPT:
+                acc = ps_h.tile([P, PACK, BANK_COLS], F32, name="acc")
+            else:
+                acc = ps_y.tile([P, PACK, BANK_COLS], F32, name="y")
             for t in range(PACK):
                 for a in range(2):
                     nc.tensor.matmul_mx(
@@ -152,7 +157,10 @@ def tile_list_htabg_max_res_kernel(
                         start=(a == 0),
                         stop=(a == 1),
                     )
-            nc.scalar.copy(yb_bf[:, cols, :], acc[:].rearrange("p t n -> p n t"))
+            if b < KEPT:
+                nc.scalar.copy(yb_bf[:, cols, :], acc[:].rearrange("p t n -> p n t"))
+            else:
+                waiting.append(acc)
 
         def gather_x(i, c0, c1):
             nc.vector.tensor_tensor(xg[:, i, c0:c1], x_pl[i][:].indirect(idx2[:, c0 // 16 : c1 // 16]), wgt[:, c0:c1], MULT)
@@ -188,9 +196,14 @@ def tile_list_htabg_max_res_kernel(
                     )
                 nc.scalar.copy(ya_bf[:, cols, :], acc[:].rearrange("p t n -> p n t"))
 
+        def late_yb(b):
+            return xg[:, b - KEPT, 0:256].bitcast(BF16).rearrange("p (n t) -> p n t", t=PACK)
+
         def join(c):
             ch = slice(STARTS[c], STARTS[c + 1])
-            nc.vector.tensor_tensor(h_bf[:, ch, :], ya_bf[:, ch, :], yb_bf[:, ch, :], MAX)
+            b = STARTS[c] // BANK_COLS
+            other = yb_bf[:, ch, :] if b < KEPT else late_yb(b)
+            nc.vector.tensor_tensor(h_bf[:, ch, :], ya_bf[:, ch, :], other, MAX)
 
         sums = {}
 
@@ -245,6 +258,9 @@ def tile_list_htabg_max_res_kernel(
                 front(s)
             if 0 <= s - 2 < chunks:
                 first(s - 2)
+            if s == 4:
+                for i, acc in enumerate(waiting):
+                    nc.scalar.copy(late_yb(KEPT + i), acc[:].rearrange("p t n -> p n t"))
             if 0 <= s - 3 < chunks:
                 join(s - 3)
             finish(s - 4, 0)

@@ -253,17 +253,18 @@ def tile_list_htabg_max_res_kernel(
             nc.sync.dma_start(res_sb[i][:], res_rows[:, :, i * HALF : (i + 1) * HALF])
         permute_words(nc.vector, late_w[:], 2, 4)
         chunks = len(STARTS) - 1
-        for s in range(chunks + 4):
+        for c in range(chunks):
+            front(c)
+            if c >= 2:
+                first(c - 2)
+        for i, acc in enumerate(waiting):
+            nc.scalar.copy(late_yb(KEPT + i), acc[:].rearrange("p t n -> p n t"))
+        for s in range(chunks + 2):
+            if s < 2:
+                first(chunks - 2 + s)
             if s < chunks:
-                front(s)
-            if 0 <= s - 2 < chunks:
-                first(s - 2)
-            if s == 4:
-                for i, acc in enumerate(waiting):
-                    nc.scalar.copy(late_yb(KEPT + i), acc[:].rearrange("p t n -> p n t"))
-            if 0 <= s - 3 < chunks:
-                join(s - 3)
-            finish(s - 4, 0)
-            if 0 <= s - 3 < chunks:
-                second(s - 3)
-            finish(s - 4, 1)
+                join(s)
+            finish(s - 2, 0)
+            finish(s - 2, 1)
+            if s < chunks:
+                second(s)

@@ -24,7 +24,10 @@ QUADS = 4
 HALF = J // 2
 STARTS = (0, 256, 512, 768, 896, 1024)
 BANK_COLS = 128
-KEPT = 6
+QUARTER = J // 4
+X_KIB = (0, 8, 16, 26)
+BANK_BYTES = 2048
+Y_BANKS = ((2, 3), (7, 6), (5, 2), (3,), (7,))
 
 
 def tile_list_htabg_max_res_kernel(
@@ -35,8 +38,10 @@ def tile_list_htabg_max_res_kernel(
     with ExitStack() as ctx:
         keep = ctx.enter_context(tc.tile_pool(name="keep", bufs=1))
         stage = ctx.enter_context(tc.tile_pool(name="stage", bufs=1))
-        ps_h = ctx.enter_context(tc.psum_pool(name="ps_h", bufs=4))
-        ps_y = ctx.enter_context(tc.psum_pool(name="ps_y", bufs=4))
+        psum = ctx.enter_context(tc.psum_pool(name="psum", bufs=1))
+
+        def bank(name, shape, number):
+            return psum.tile(shape, F32, name=name, offset=number * BANK_BYTES)
 
         def staged(name, shape, dtype, kib):
             return stage.tile(shape, dtype, name=name, offset=int(kib * 1024), align_bytes=64)
@@ -45,14 +50,14 @@ def tile_list_htabg_max_res_kernel(
         idx2 = keep.tile([P, J // 16], U16, name="idx2")
         tab_sc = keep.tile([P, T // 4], I32, name="tab_sc", align_bytes=64)
         tab_w = staged("tab_w", [P, T], I32, 29)
-        got_sc = keep.tile([P, J // 4], I32, name="got_sc", align_bytes=64)
+        got_sc = staged("got_sc", [P, J // 4], I32, 15.5)
         got_w = keep.tile([P, J], I32, name="got_w", align_bytes=64)
-        part_w = keep.tile([P, 2, J // 2], I32, name="part_w", align_bytes=64)
-        wb_raw = staged("wb_raw", [P, 2, R], I32, 37)
-        w_perm = keep.tile([P, PACK, 4, P], I32, name="w_perm", align_bytes=64)
-        sc_raw = staged("sc_raw", [P, 2, R // 4], I32, 15.5)
-        rows = keep.tile([P, 2, J // 4], I32, name="rows", align_bytes=64)
-        planes = [rows, keep.tile([P, 2, J // 4], I32, name="plane1", align_bytes=64)]
+        part_w = [keep.tile([P, 2, HALF // 2], I32, name="part_w%d" % h, align_bytes=64) for h in range(2)]
+        wb_raw = keep.tile([P, 2, R], I32, name="wb_raw", align_bytes=64)
+        w_perm = [staged("w_perm0", [P, PACK, 1, P], I32, 16)]
+        sc_raw = keep.tile([P, R // 4], I32, name="sc_raw", align_bytes=64)
+        rows = keep.tile([P, 512], I32, name="rows", align_bytes=64)
+        planes = keep.tile([P, 2, 512], I32, name="planes", align_bytes=64)
         wgt = keep.tile([P, J], F32, name="wgt", align_bytes=64)
         wgt_rows = keep.tile([P, P], F32, name="wgt_rows", align_bytes=64)
         wgt_t = keep.tile([P, J // P, P], F32, name="wgt_t", align_bytes=64)
@@ -63,7 +68,7 @@ def tile_list_htabg_max_res_kernel(
         xq = keep.tile([P, J], U32, name="xq", align_bytes=64)
         xq_sc = keep.tile([P, J], U8, name="xq_sc", align_bytes=64)
         ya_bf = keep.tile([P, J, PACK], BF16, name="ya_bf", align_bytes=64)
-        yb_bf = keep.tile([P, J, PACK], BF16, name="yb_bf", align_bytes=64)
+        ybt_bf = [keep.tile([P, R], BF16, name="ybt_bf%d" % b, align_bytes=64) for b in range(J // BANK_COLS)]
         h_bf = keep.tile([P, J, PACK], BF16, name="h_bf", align_bytes=64)
         hq = keep.tile([P, J], U32, name="hq", align_bytes=64)
         hq_sc = keep.tile([P, J], U8, name="hq_sc", align_bytes=64)
@@ -73,105 +78,118 @@ def tile_list_htabg_max_res_kernel(
             return dram[a].rearrange("p n t -> p (n t)").bitcast(I32)
 
         for p0, p1 in ((32, 64), (64, P)):
+            nc.vector.memset(sc_raw[p0:p1, :], 0)
             nc.vector.memset(tab_sc[p0:p1, :], 0)
-            nc.gpsimd.memset(sc_raw[p0:p1, :, :], 0)
         nc.gpsimd.memset(wgt_rows[64:P, :], 0.0)
         make_identity(nc, ident[:])
-        nc.gpsimd.memset(planes[1][:], 0)
+        nc.gpsimd.memset(planes[:], 0)
 
+        nc.sync.dma_start(sc_raw[0:32:2, :], wa_scales[0].bitcast(I32))
+        nc.sync.dma_start(sc_raw[1:32:2, :].bitcast(U16)[:, 0:255], wa_scales[0].bitcast(U16)[:, 1:256])
         nc.sync.dma_start(idx[:], offs)
-        nc.sync.dma_start(tab_sc[0:32, :], tab_scales.rearrange("a r c -> (a r) c").bitcast(I32))
-        nc.sync.dma_start(sc_raw[0:32, 0, :], wb_scales.rearrange("a r c -> (a r) c").bitcast(I32))
-        nc.sync.dma_start(sc_raw[0:16, 1, :], wa_scales[0].bitcast(I32))
-        nc.sync.dma_start(sc_raw[16:32, 1, :], wd_scales[0].bitcast(I32))
-        nc.sync.dma_start(idx2[:], offs2)
+        nc.sync.dma_start(tab_sc[0:32, :], tab_scales.bitcast(I32).rearrange("a r c -> r a c"))
         nc.sync.dma_start(
             wgt_rows[0:64, :], wgt2.rearrange("(g r) j -> g r j", r=16)[:, 0, :].rearrange("g (b k) -> g b k", k=P)
         )
         nc.sync.dma_start(tab_w[:], words(tab_words, 0))
+        nc.sync.dma_start(rows[0:32, 256:384], wb_scales.bitcast(I32).rearrange("a r c -> r a c"))
+        nc.sync.dma_start(rows[0:32, 448:512], wd_scales[0].bitcast(I32).rearrange("i (a c) -> (i a) c", a=2))
+        nc.sync.dma_start(idx2[:], offs2)
         nc.sync.dma_start(
             wb_raw[:], wb_words.rearrange("a p n t -> p a (n t)").bitcast(I32)
         )
         x_rows = xT.rearrange("(p i) t -> i p t", i=PACK)
 
         def load_x(i):
-            x_pl.append(staged("x_pl%d" % i, [P, T], F32, 8 * i))
+            x_pl.append(staged("x_pl%d" % i, [P, T], F32, X_KIB[i]))
             nc.sync.dma_start(x_pl[i][:], x_rows[i])
 
-        def permute_words(eng, raw, a0, a1):
+        def permute_words(eng, perm, raw):
             eng.tensor_copy(
-                w_perm[:, :, a0:a1, :].rearrange("p t a (c i) -> p (a c) t i", i=4),
+                perm.rearrange("p t a (c i) -> p (a c) t i", i=4),
                 raw.rearrange("p a (c i t) -> p (a c) t i", i=4, t=PACK),
             )
 
-        def weight_scale(a, t, k):
-            return planes[a][:, 1, (2 * t + k) * 32 : (2 * t + k + 1) * 32].bitcast(U8)
+        def weight_scale(k, t):
+            c0 = 384 + 64 * k + 32 * (t % 2)
+            return planes[:, t // 2, c0 : c0 + 32].bitcast(U8)
 
         load_x(0)
-        turned = ps_y.tile([P, 512], F32, name="y")
+        turned = bank("turned", [P, 512], 4)
         nc.tensor.transpose(turned[:, 0:P], wgt_rows[:], ident[:])
         nc.scalar.copy(
             wgt_t[:].rearrange("p b (g r) -> p b g r", r=16),
             turned[:, 0:64].rearrange("p (g b) -> p b g", g=8).unsqueeze(3).to_broadcast([P, 8, 8, 16]),
         )
         for hf in range(2):
-            spread = ps_y.tile([P, 512], F32, name="y")
+            spread = bank("spread%d" % hf, [P, 512], 5 + hf)
             for u in range(4):
                 nc.tensor.transpose(spread[:, u * P : (u + 1) * P], wgt_t[:, 4 * hf + u, :], ident[:])
             nc.scalar.copy(wgt[:, hf * HALF : (hf + 1) * HALF], spread[:])
-        nc.vector.tensor_copy(got_sc[:].bitcast(U8), tab_sc[:].bitcast(U8).indirect(idx[:]))
-        nc.vector.tensor_copy(rows[:, 0, :], got_sc[:])
         nc.vector.tensor_copy(
-            rows[:, 1, :].bitcast(U8).rearrange("p (t a c i) -> p (a c) t i", t=PACK, a=2, i=16),
-            sc_raw[:].bitcast(U8).rearrange("p a (c i t) -> p (a c) t i", i=16, t=PACK),
+            rows[:, 384:448].bitcast(U8).rearrange("p (t c i) -> p c t i", t=2, i=16),
+            sc_raw[:].bitcast(U8).rearrange("p (c i t) -> p c t i", i=16, t=PACK)[:, :, 0:2, :],
         )
-        for n in range(1, 2 * QUADS):
-            if n == 7:
-                load_x(1)
-            a, q = divmod(n, QUADS)
-            nc.sync.dma_start(planes[a][32 * q : 32 * q + 4, :, :], rows[16 * a + 4 * q : 16 * a + 4 * q + 4, :, :])
+        nc.vector.tensor_copy(got_sc[:].bitcast(U8), tab_sc[:].bitcast(U8).indirect(idx[:]))
+        nc.vector.tensor_copy(rows[0:32, 0:256], got_sc[0:32, :])
+        for q in (0, 2, 1, 3):
+            nc.sync.dma_start(planes[32 * q : 32 * q + 4, :, :], rows[8 * q : 8 * q + 8, :])
+        load_x(1)
         load_x(2)
         nc.vector.tensor_copy(got_w[:].bitcast(U32), tab_w[:].bitcast(U32).indirect(idx[:]))
         load_x(3)
-        nc.vector.tensor_copy(
-            part_w[:].bitcast(U16).rearrange("p d (c i) -> p c d i", i=8),
-            got_w[:].bitcast(U16).rearrange("p (c i d) -> p c d i", i=8, d=2),
-        )
-        permute_words(nc.vector, wb_raw[:], 0, 2)
+        for h in range(2):
+            nc.vector.tensor_copy(
+                part_w[h][:].bitcast(U16).rearrange("p d (c i) -> p c d i", i=8),
+                got_w[:, h * HALF : (h + 1) * HALF].bitcast(U16).rearrange("p (c i d) -> p c d i", i=8, d=2),
+            )
 
-        waiting = []
-        for b in range(J // BANK_COLS):
-            cols = slice(b * BANK_COLS, (b + 1) * BANK_COLS)
-            if b < KEPT:
-                acc = ps_h.tile([P, PACK, BANK_COLS], F32, name="acc")
-            else:
-                acc = ps_y.tile([P, PACK, BANK_COLS], F32, name="y")
-            for t in range(PACK):
-                for a in range(2):
-                    nc.tensor.matmul_mx(
-                        out=acc[:, t, :],
-                        lhsT=w_perm[:, t, a, :].bitcast(FP8X4),
-                        lhsT_scale=weight_scale(a, t, 0),
-                        rhs=part_w[:, a, b * 64 : (b + 1) * 64].bitcast(U8).bitcast(FP4X4),
-                        rhs_scale=planes[a][:, 0, :].bitcast(U8)[:, cols],
-                        start=(a == 0),
-                        stop=(a == 1),
+        yb = {}
+
+        def turn_yb(c):
+            yb[c] = bank("yb%d" % c, [P, 2, QUARTER], 7 - c)
+            for half in range(2):
+                for u in range(2):
+                    nc.tensor.transpose(
+                        yb[c][:, u, half * BANK_COLS : (half + 1) * BANK_COLS],
+                        ybt_bf[2 * c + half][:].bitcast(F32)[:, u * P : (u + 1) * P],
+                        ident[:],
                     )
-            if b < KEPT:
-                nc.scalar.copy(yb_bf[:, cols, :], acc[:].rearrange("p t n -> p n t"))
-            else:
-                waiting.append(acc)
+
+        for b in range(J // BANK_COLS):
+            acc = bank("ybt%d" % b, [P, R], b)
+            for a in range(2):
+                nc.tensor.matmul_mx(
+                    out=acc[:],
+                    lhsT=part_w[b // 4][:, a, (b % 4) * 64 : (b % 4 + 1) * 64].bitcast(U8).bitcast(FP4X4),
+                    lhsT_scale=planes[:, a, 32 * b : 32 * b + 32].bitcast(U8),
+                    rhs=wb_raw[:, a, :].bitcast(FP8X4),
+                    rhs_scale=planes[:, a, 256:384].bitcast(U8),
+                    start=(a == 0),
+                    stop=(a == 1),
+                )
+            nc.scalar.copy(
+                ybt_bf[b][:].rearrange("p (u m e) -> p u m e", u=2, e=2), acc[:].rearrange("p (m u e) -> p u m e", u=2, e=2)
+            )
+        for c in range(4):
+            turn_yb(c)
 
         def gather_x(i, c0, c1):
             nc.vector.tensor_tensor(xg[:, i, c0:c1], x_pl[i][:].indirect(idx2[:, c0 // 16 : c1 // 16]), wgt[:, c0:c1], MULT)
 
-        out_rows = out.rearrange("(p a) j -> p a j", a=PACK)
+        out_rows = out.rearrange("(a p) j -> p a j", p=P)
+
+        def rounded(c):
+            if c == 0:
+                return xg[:, 3, HALF:J].bitcast(BF16).rearrange("p (n t) -> p n t", t=PACK)
+            return xg_bf[:, STARTS[c] : STARTS[c + 1], :]
 
         def front(c):
             c0, c1 = STARTS[c], STARTS[c + 1]
-            gather_x(3, c0, c1)
+            if c0 % QUARTER == 0:
+                gather_x(3, c0, c0 + QUARTER)
             nc.scalar.copy(
-                xg_bf[:, c0:c1, :].rearrange("p (c k) t -> p c t k", k=4),
+                rounded(c).rearrange("p (c k) t -> p c t k", k=4),
                 xg[:, :, c0:c1].rearrange("p t (c k) -> p c t k", k=4),
             )
 
@@ -179,16 +197,16 @@ def tile_list_htabg_max_res_kernel(
             c0, c1 = STARTS[c], STARTS[c + 1]
             ch = slice(c0, c1)
             nc.vector.quantize_mx(
-                out=xq[:, ch].bitcast(FP8X4), scales=xq_sc[:, ch], in_=xg_bf[:, ch, :].rearrange("p n t -> p (n t)")
+                out=xq[:, ch].bitcast(FP8X4), scales=xq_sc[:, ch], in_=rounded(c).rearrange("p n t -> p (n t)")
             )
             for b in range(c0 // BANK_COLS, c1 // BANK_COLS):
                 cols = slice(b * BANK_COLS, (b + 1) * BANK_COLS)
-                acc = ps_h.tile([P, PACK, BANK_COLS], F32, name="acc")
+                acc = bank("ya%d" % b, [P, PACK, BANK_COLS], b % 2)
                 for t in range(PACK):
                     nc.tensor.matmul_mx(
                         out=acc[:, t, :],
-                        lhsT=w_perm[:, t, 2, :].bitcast(FP8X4),
-                        lhsT_scale=weight_scale(0, t, 1),
+                        lhsT=w_perm[0][:, t, 0, :].bitcast(FP8X4),
+                        lhsT_scale=weight_scale(0, t),
                         rhs=xq[:, cols].bitcast(FP8X4),
                         rhs_scale=xq_sc[:, cols],
                         start=True,
@@ -196,14 +214,15 @@ def tile_list_htabg_max_res_kernel(
                     )
                 nc.scalar.copy(ya_bf[:, cols, :], acc[:].rearrange("p t n -> p n t"))
 
-        def late_yb(b):
-            return xg[:, b - KEPT, 0:256].bitcast(BF16).rearrange("p (n t) -> p n t", t=PACK)
-
         def join(c):
-            ch = slice(STARTS[c], STARTS[c + 1])
-            b = STARTS[c] // BANK_COLS
-            other = yb_bf[:, ch, :] if b < KEPT else late_yb(b)
-            nc.vector.tensor_tensor(h_bf[:, ch, :], ya_bf[:, ch, :], other, MAX)
+            c0, c1 = STARTS[c], STARTS[c + 1]
+            n0 = c0 % QUARTER
+            nc.vector.tensor_tensor(
+                h_bf[:, c0:c1, :].rearrange("p n (u e) -> p n u e", u=2),
+                yb[c0 // QUARTER][:].bitcast(BF16).rearrange("p u (n e) -> p n u e", e=2)[:, n0 : n0 + c1 - c0, :, :],
+                ya_bf[:, c0:c1, :].rearrange("p n (u e) -> p n u e", u=2),
+                MAX,
+            )
 
         sums = {}
 
@@ -216,13 +235,13 @@ def tile_list_htabg_max_res_kernel(
             width = c1 - c0
             per_bank = 512 // width
             for g in range(N // P // per_bank):
-                y = ps_y.tile([P, per_bank, width], F32, name="y")
+                y = bank("y%d_%d" % (c, g), [P, per_bank, width], Y_BANKS[c][g])
                 for u in range(per_bank):
                     nt = per_bank * g + u
                     nc.tensor.matmul_mx(
                         out=y[:, u, :],
-                        lhsT=w_perm[:, nt, 3, :].bitcast(FP8X4),
-                        lhsT_scale=weight_scale(1, nt, 1),
+                        lhsT=late_w[1][:, 0, nt * P : (nt + 1) * P].bitcast(FP8X4),
+                        lhsT_scale=weight_scale(1, nt),
                         rhs=hq[:, ch].bitcast(FP8X4),
                         rhs_scale=hq_sc[:, ch],
                         start=True,
@@ -242,26 +261,25 @@ def tile_list_htabg_max_res_kernel(
             nc.sync.dma_start(out_rows[:, nts, c0:c1], o)
 
         gather_x(0, 0, J)
-        late_w = staged("late_w", [P, 2, R], I32, 0)
-        nc.sync.dma_start(late_w[:, 0, :], words(wa_words, 0))
-        nc.sync.dma_start(late_w[:, 1, :], words(wd_words, 0))
-        res_rows = res.rearrange("(p a) j -> p a j", a=PACK)
+        late_w = [staged("late_w%d" % a, [P, 1, R], I32, 2 * a) for a in range(2)]
+        nc.sync.dma_start(late_w[0][:, 0, :], words(wa_words, 0))
+        nc.sync.dma_start(late_w[1][:, 0, :], words(wd_words, 0))
+        res_rows = res.rearrange("(a p) j -> p a j", p=P)
         res_sb = []
         for i in range(2):
             gather_x(i + 1, 0, J)
-            res_sb.append(staged("res_sb%d" % i, [P, N // P, HALF], F32, 8 * (i + 1)))
+            res_sb.append(staged("res_sb%d" % i, [P, N // P, HALF], F32, (8, 18)[i]))
             nc.sync.dma_start(res_sb[i][:], res_rows[:, :, i * HALF : (i + 1) * HALF])
-        permute_words(nc.vector, late_w[:], 2, 4)
         chunks = len(STARTS) - 1
         for c in range(chunks):
             front(c)
-            if c >= 2:
-                first(c - 2)
-        for i, acc in enumerate(waiting):
-            nc.scalar.copy(late_yb(KEPT + i), acc[:].rearrange("p t n -> p n t"))
+            if c == 1:
+                permute_words(nc.vector, w_perm[0][:], late_w[0][:])
+            if c >= 1:
+                first(c - 1)
         for s in range(chunks + 2):
-            if s < 2:
-                first(chunks - 2 + s)
+            if s < 1:
+                first(chunks - 1 + s)
             if s < chunks:
                 join(s)
             finish(s - 2, 0)

@@ -188,10 +188,12 @@ def tile_list_htabg_max_res_kernel(
             c0, c1 = STARTS[c], STARTS[c + 1]
             if c0 % QUARTER == 0:
                 gather_x(3, c0, c0 + QUARTER)
-            nc.scalar.copy(
-                rounded(c).rearrange("p (c k) t -> p c t k", k=4),
-                xg[:, :, c0:c1].rearrange("p t (c k) -> p c t k", k=4),
-            )
+            woven = rounded(c).rearrange("p (c k) t -> p c t k", k=4)
+            planes_in = xg[:, :, c0:c1].rearrange("p t (c k) -> p c t k", k=4)
+            if c1 == J:
+                nc.vector.tensor_copy(woven, planes_in)
+            else:
+                nc.scalar.copy(woven, planes_in)
 
         def first(c):
             c0, c1 = STARTS[c], STARTS[c + 1]
@@ -257,7 +259,13 @@ def tile_list_htabg_max_res_kernel(
             per_bank = 512 // width
             nts = slice(per_bank * g, per_bank * (g + 1))
             o = o_sb[:, c0 // BANK_COLS + g, :].rearrange("p (u n) -> p u n", u=per_bank)
-            nc.vector.tensor_tensor(o, sums[c, g][:], res_sb[c0 // HALF][:, nts, c0 % HALF : c0 % HALF + width], ADD)
+            res_part = res_sb[c0 // HALF][:, nts, c0 % HALF : c0 % HALF + width]
+            if (c, g) == (1, 1):
+                y_sb = keep.tile([P, per_bank, width], F32, name="y_sb", align_bytes=64)
+                nc.scalar.copy(y_sb[:], sums[c, g][:])
+                nc.gpsimd.tensor_tensor(o, y_sb[:], res_part, ADD)
+            else:
+                nc.vector.tensor_tensor(o, sums[c, g][:], res_part, ADD)
             nc.sync.dma_start(out_rows[:, nts, c0:c1], o)
 
         gather_x(0, 0, J)

@@ -84,16 +84,16 @@ def tile_list_htabg_max_res_kernel(
         make_identity(nc, ident[:])
         nc.gpsimd.memset(planes[:], 0)
 
-        nc.sync.dma_start(sc_raw[0:32:2, :], wa_scales[0].bitcast(I32))
-        nc.sync.dma_start(sc_raw[1:32:2, :].bitcast(U16)[:, 0:255], wa_scales[0].bitcast(U16)[:, 1:256])
         nc.sync.dma_start(idx[:], offs)
-        nc.sync.dma_start(tab_sc[0:32, :], tab_scales.bitcast(I32).rearrange("a r c -> r a c"))
-        nc.sync.dma_start(
+        nc.scalar.dma_start(tab_sc[0:32, :], tab_scales.bitcast(I32).rearrange("a r c -> r a c"))
+        nc.scalar.dma_start(sc_raw[0:32:2, :], wa_scales[0].bitcast(I32))
+        nc.sync.dma_start(sc_raw[1:32:2, :].bitcast(U16)[:, 0:255], wa_scales[0].bitcast(U16)[:, 1:256])
+        nc.scalar.dma_start(
             wgt_rows[0:64, :], wgt2.rearrange("(g r) j -> g r j", r=16)[:, 0, :].rearrange("g (b k) -> g b k", k=P)
         )
         nc.sync.dma_start(tab_w[:], words(tab_words, 0))
-        nc.sync.dma_start(rows[0:32, 256:384], wb_scales.bitcast(I32).rearrange("a r c -> r a c"))
-        nc.sync.dma_start(rows[0:32, 448:512], wd_scales[0].bitcast(I32).rearrange("i (a c) -> (i a) c", a=2))
+        nc.scalar.dma_start(rows[0:32, 256:384], wb_scales.bitcast(I32).rearrange("a r c -> r a c"))
+        nc.scalar.dma_start(rows[0:32, 448:512], wd_scales[0].bitcast(I32).rearrange("i (a c) -> (i a) c", a=2))
         nc.sync.dma_start(idx2[:], offs2)
         nc.sync.dma_start(
             wb_raw[:], wb_words.rearrange("a p n t -> p a (n t)").bitcast(I32)

@@ -84,10 +84,10 @@ def tile_list_htabg_max_res_kernel(
         make_identity(nc, ident[:])
         nc.gpsimd.memset(planes[:], 0)
 
+        nc.sync.dma_start(sc_raw[1:32:2, :].bitcast(U16)[:, 0:255], wa_scales[0].bitcast(U16)[:, 1:256])
+        nc.scalar.dma_start(sc_raw[0:32:2, :], wa_scales[0].bitcast(I32))
         nc.sync.dma_start(idx[:], offs)
         nc.scalar.dma_start(tab_sc[0:32, :], tab_scales.bitcast(I32).rearrange("a r c -> r a c"))
-        nc.scalar.dma_start(sc_raw[0:32:2, :], wa_scales[0].bitcast(I32))
-        nc.sync.dma_start(sc_raw[1:32:2, :].bitcast(U16)[:, 0:255], wa_scales[0].bitcast(U16)[:, 1:256])
         nc.scalar.dma_start(
             wgt_rows[0:64, :], wgt2.rearrange("(g r) j -> g r j", r=16)[:, 0, :].rearrange("g (b k) -> g b k", k=P)
         )
@@ -260,7 +260,7 @@ def tile_list_htabg_max_res_kernel(
             nts = slice(per_bank * g, per_bank * (g + 1))
             o = o_sb[:, c0 // BANK_COLS + g, :].rearrange("p (u n) -> p u n", u=per_bank)
             res_part = res_sb[c0 // HALF][:, nts, c0 % HALF : c0 % HALF + width]
-            if (c, g) == (1, 1):
+            if (c, g) == (0, 1):
                 y_sb = keep.tile([P, per_bank, width], F32, name="y_sb", align_bytes=64)
                 nc.scalar.copy(y_sb[:], sums[c, g][:])
                 nc.gpsimd.tensor_tensor(o, y_sb[:], res_part, ADD)
@@ -285,12 +285,22 @@ def tile_list_htabg_max_res_kernel(
                 permute_words(nc.vector, w_perm[0][:], late_w[0][:])
             if c >= 1:
                 first(c - 1)
-        for s in range(chunks + 2):
-            if s < 1:
-                first(chunks - 1 + s)
-            if s < chunks:
-                join(s)
-            finish(s - 2, 0)
-            finish(s - 2, 1)
-            if s < chunks:
-                second(s)
+        first(chunks - 1)
+        join(0)
+        second(0)
+        join(1)
+        finish(0, 1)
+        second(1)
+        finish(0, 0)
+        join(2)
+        second(2)
+        finish(1, 0)
+        join(3)
+        finish(1, 1)
+        second(3)
+        finish(2, 0)
+        join(4)
+        finish(2, 1)
+        second(4)
+        finish(3, 0)
+        finish(4, 0)

@@ -136,7 +136,10 @@ def tile_list_htabg_max_res_kernel(
             nc.sync.dma_start(planes[32 * q : 32 * q + 4, :, :], rows[8 * q : 8 * q + 8, :])
         load_x(1)
         load_x(2)
-        nc.vector.tensor_copy(got_w[:].bitcast(U32), tab_w[:].bitcast(U32).indirect(idx[:]))
+        for h in range(2):
+            nc.vector.tensor_copy(
+                got_w[:, h * HALF : (h + 1) * HALF].bitcast(U32), tab_w[:].bitcast(U32).indirect(idx[:, 32 * h : 32 * h + 32])
+            )
         load_x(3)
         for h in range(2):
             nc.vector.tensor_copy(
@@ -290,17 +293,17 @@ def tile_list_htabg_max_res_kernel(
         second(0)
         join(1)
         finish(0, 1)
-        second(1)
         finish(0, 0)
+        second(1)
         join(2)
-        second(2)
         finish(1, 0)
+        second(2)
         join(3)
         finish(1, 1)
         second(3)
-        finish(2, 0)
         join(4)
-        finish(2, 1)
+        finish(2, 0)
         second(4)
+        finish(2, 1)
         finish(3, 0)
         finish(4, 0)

@@ -64,12 +64,14 @@ def tile_list_htabg_max_res_kernel(
         ident = keep.tile([P, P], F32, name="ident", align_bytes=64)
         x_pl = []
         xg = keep.tile([P, PACK, J], F32, name="xg", align_bytes=64)
-        xg_bf = keep.tile([P, J, PACK], BF16, name="xg_bf", align_bytes=64)
+        xg_bf = {}
+        ya_second = staged("ya_second", [P, QUARTER, PACK], BF16, 46)
         xq = keep.tile([P, J], U32, name="xq", align_bytes=64)
         xq_sc = keep.tile([P, J], U8, name="xq_sc", align_bytes=64)
         ya_bf = keep.tile([P, J, PACK], BF16, name="ya_bf", align_bytes=64)
         ybt_bf = [keep.tile([P, R], BF16, name="ybt_bf%d" % b, align_bytes=64) for b in range(J // BANK_COLS)]
         h_bf = keep.tile([P, J, PACK], BF16, name="h_bf", align_bytes=64)
+        h_early = [staged("h_early%d" % c, [P, QUARTER, PACK], BF16, (44, 50)[c]) for c in range(2)]
         hq = keep.tile([P, J], U32, name="hq", align_bytes=64)
         hq_sc = keep.tile([P, J], U8, name="hq_sc", align_bytes=64)
         o_sb = keep.tile([P, J // BANK_COLS, 512], F32, name="o_sb", align_bytes=64)
@@ -185,24 +187,33 @@ def tile_list_htabg_max_res_kernel(
         def rounded(c):
             if c == 0:
                 return xg[:, 3, HALF:J].bitcast(BF16).rearrange("p (n t) -> p n t", t=PACK)
-            return xg_bf[:, STARTS[c] : STARTS[c + 1], :]
+            if c not in xg_bf:
+                xg_bf[c] = staged("xg_bf%d" % c, [P, STARTS[c + 1] - STARTS[c], PACK], BF16, (0, 40, 42, 48, 52)[c])
+            return xg_bf[c][:]
 
         def front(c):
             c0, c1 = STARTS[c], STARTS[c + 1]
-            if c0 % QUARTER == 0:
+            if c < 3:
                 gather_x(3, c0, c0 + QUARTER)
             woven = rounded(c).rearrange("p (c k) t -> p c t k", k=4)
             planes_in = xg[:, :, c0:c1].rearrange("p t (c k) -> p c t k", k=4)
-            if c1 == J:
-                nc.vector.tensor_copy(woven, planes_in)
+            if c in (0, 2):
+                nc.scalar.copy(woven[:, 32:64], planes_in[:, 32:64])
+                nc.vector.tensor_copy(woven[:, 0:32], planes_in[:, 0:32])
             else:
                 nc.scalar.copy(woven, planes_in)
+
+        def rounded_ya(c0, c1):
+            if QUARTER <= c0 < HALF:
+                return ya_second[:, c0 - QUARTER : c1 - QUARTER, :]
+            return ya_bf[:, c0:c1, :]
 
         def first(c):
             c0, c1 = STARTS[c], STARTS[c + 1]
             ch = slice(c0, c1)
+            codes = staged("xq_third", [P, c1 - c0], U32, 52)[:] if c == 2 else xq[:, ch]
             nc.vector.quantize_mx(
-                out=xq[:, ch].bitcast(FP8X4), scales=xq_sc[:, ch], in_=rounded(c).rearrange("p n t -> p (n t)")
+                out=codes.bitcast(FP8X4), scales=xq_sc[:, ch], in_=rounded(c).rearrange("p n t -> p (n t)")
             )
             for b in range(c0 // BANK_COLS, c1 // BANK_COLS):
                 cols = slice(b * BANK_COLS, (b + 1) * BANK_COLS)
@@ -212,20 +223,23 @@ def tile_list_htabg_max_res_kernel(
                         out=acc[:, t, :],
                         lhsT=w_perm[0][:, t, 0, :].bitcast(FP8X4),
                         lhsT_scale=weight_scale(0, t),
-                        rhs=xq[:, cols].bitcast(FP8X4),
+                        rhs=codes[:, b * BANK_COLS - c0 : (b + 1) * BANK_COLS - c0].bitcast(FP8X4),
                         rhs_scale=xq_sc[:, cols],
                         start=True,
                         stop=True,
                     )
-                nc.scalar.copy(ya_bf[:, cols, :], acc[:].rearrange("p t n -> p n t"))
+                nc.scalar.copy(rounded_ya(b * BANK_COLS, (b + 1) * BANK_COLS), acc[:].rearrange("p t n -> p n t"))
+
+        def joined(c):
+            return h_early[c][:] if c < 2 else h_bf[:, STARTS[c] : STARTS[c + 1], :]
 
         def join(c):
             c0, c1 = STARTS[c], STARTS[c + 1]
             n0 = c0 % QUARTER
             nc.vector.tensor_tensor(
-                h_bf[:, c0:c1, :].rearrange("p n (u e) -> p n u e", u=2),
+                joined(c).rearrange("p n (u e) -> p n u e", u=2),
                 yb[c0 // QUARTER][:].bitcast(BF16).rearrange("p u (n e) -> p n u e", e=2)[:, n0 : n0 + c1 - c0, :, :],
-                ya_bf[:, c0:c1, :].rearrange("p n (u e) -> p n u e", u=2),
+                rounded_ya(c0, c1).rearrange("p n (u e) -> p n u e", u=2),
                 MAX,
             )
 
@@ -235,7 +249,7 @@ def tile_list_htabg_max_res_kernel(
             c0, c1 = STARTS[c], STARTS[c + 1]
             ch = slice(c0, c1)
             nc.vector.quantize_mx(
-                out=hq[:, ch].bitcast(FP8X4), scales=hq_sc[:, ch], in_=h_bf[:, ch, :].rearrange("p n t -> p (n t)")
+                out=hq[:, ch].bitcast(FP8X4), scales=hq_sc[:, ch], in_=joined(c).rearrange("p n t -> p (n t)")
             )
             width = c1 - c0
             per_bank = 512 // width
@@ -263,12 +277,7 @@ def tile_list_htabg_max_res_kernel(
             nts = slice(per_bank * g, per_bank * (g + 1))
             o = o_sb[:, c0 // BANK_COLS + g, :].rearrange("p (u n) -> p u n", u=per_bank)
             res_part = res_sb[c0 // HALF][:, nts, c0 % HALF : c0 % HALF + width]
-            if (c, g) == (0, 1):
-                y_sb = keep.tile([P, per_bank, width], F32, name="y_sb", align_bytes=64)
-                nc.scalar.copy(y_sb[:], sums[c, g][:])
-                nc.gpsimd.tensor_tensor(o, y_sb[:], res_part, ADD)
-            else:
-                nc.vector.tensor_tensor(o, sums[c, g][:], res_part, ADD)
+            nc.vector.tensor_tensor(o, sums[c, g][:], res_part, ADD)
             nc.sync.dma_start(out_rows[:, nts, c0:c1], o)
 
         gather_x(0, 0, J)
@@ -281,23 +290,27 @@ def tile_list_htabg_max_res_kernel(
             gather_x(i + 1, 0, J)
             res_sb.append(staged("res_sb%d" % i, [P, N // P, HALF], F32, (8, 18)[i]))
             nc.sync.dma_start(res_sb[i][:], res_rows[:, :, i * HALF : (i + 1) * HALF])
-        chunks = len(STARTS) - 1
-        for c in range(chunks):
-            front(c)
-            if c == 1:
-                permute_words(nc.vector, w_perm[0][:], late_w[0][:])
-            if c >= 1:
-                first(c - 1)
-        first(chunks - 1)
+        front(0)
+        front(1)
+        permute_words(nc.vector, w_perm[0][:], late_w[0][:])
+        first(0)
+        front(2)
+        first(1)
+        gather_x(3, J - QUARTER, J)
+        front(3)
         join(0)
+        first(2)
         second(0)
         join(1)
-        finish(0, 1)
+        first(3)
+        front(4)
         finish(0, 0)
         second(1)
         join(2)
-        finish(1, 0)
+        finish(0, 1)
+        first(4)
         second(2)
+        finish(1, 0)
         join(3)
         finish(1, 1)
         second(3)

@@ -22,12 +22,16 @@ P = 128
 PACK = 4
 QUADS = 4
 HALF = J // 2
-STARTS = (0, 256, 512, 768, 896, 1024)
+UNITS = ((0, 128), (128, 256), (256, 512), (512, 768), (768, 1024))
+HEAD_BASE = 3 * J + 640
+HEAD_STEP = 384
+DIRECT = 2
 BANK_COLS = 128
 QUARTER = J // 4
-X_KIB = (0, 8, 16, 26)
+X_KIB = (0, 8, 17, 26)
 BANK_BYTES = 2048
-Y_BANKS = ((2, 3), (7, 6), (5, 2), (3,), (7,))
+YA_BANKS = (4, 5, 6, 7, 0, 6, 4, 5)
+Y_BANKS = ((4,), (5,), (7, 1), (0, 6), (2, 3))
 
 
 def tile_list_htabg_max_res_kernel(
@@ -48,30 +52,32 @@ def tile_list_htabg_max_res_kernel(
 
         idx = keep.tile([P, J // 16], U16, name="idx")
         idx2 = keep.tile([P, J // 16], U16, name="idx2")
-        tab_sc = keep.tile([P, T // 4], I32, name="tab_sc", align_bytes=64)
+        tab_sc = staged("tab_sc", [P, T // 4], I32, 15.5)
         tab_w = staged("tab_w", [P, T], I32, 29)
-        got_sc = staged("got_sc", [P, J // 4], I32, 15.5)
+        got_sc = keep.tile([P, J // 4], I32, name="got_sc", align_bytes=64)
         got_w = keep.tile([P, J], I32, name="got_w", align_bytes=64)
         part_w = [keep.tile([P, 2, HALF // 2], I32, name="part_w%d" % h, align_bytes=64) for h in range(2)]
         wb_raw = keep.tile([P, 2, R], I32, name="wb_raw", align_bytes=64)
-        w_perm = [staged("w_perm0", [P, PACK, 1, P], I32, 16)]
-        sc_raw = keep.tile([P, R // 4], I32, name="sc_raw", align_bytes=64)
-        rows = keep.tile([P, 512], I32, name="rows", align_bytes=64)
-        planes = keep.tile([P, 2, 512], I32, name="planes", align_bytes=64)
+        wgt_head = staged("wgt_head", [P, QUARTER], F32, 54)
+        planes = keep.tile([P, 2, 256], I32, name="planes", align_bytes=64)
+        wb_sc = keep.tile([P, 2, R // 4], I32, name="wb_sc", align_bytes=64)
+        late_sc = keep.tile([P, 2, R // 4], I32, name="late_sc", align_bytes=64)
         wgt = keep.tile([P, J], F32, name="wgt", align_bytes=64)
         wgt_rows = keep.tile([P, P], F32, name="wgt_rows", align_bytes=64)
         wgt_t = keep.tile([P, J // P, P], F32, name="wgt_t", align_bytes=64)
         ident = keep.tile([P, P], F32, name="ident", align_bytes=64)
         x_pl = []
-        xg = keep.tile([P, PACK, J], F32, name="xg", align_bytes=64)
-        xg_bf = {}
-        ya_second = staged("ya_second", [P, QUARTER, PACK], BF16, 46)
+        xg = keep.tile([P, 5 * J], F32, name="xg", align_bytes=64)
+        xb = [staged("xb%d" % u, [P, PACK * (UNITS[u][1] - UNITS[u][0])], BF16, 36 + 2 * u)[:] for u in (0, 2, 3, 4)]
+        xb.insert(1, xg[:, 0:QUARTER].bitcast(BF16))
         xq = keep.tile([P, J], U32, name="xq", align_bytes=64)
         xq_sc = keep.tile([P, J], U8, name="xq_sc", align_bytes=64)
-        ya_bf = keep.tile([P, J, PACK], BF16, name="ya_bf", align_bytes=64)
+        ya_bf = keep.tile([P, J * PACK], BF16, name="ya_bf", align_bytes=64)
         ybt_bf = [keep.tile([P, R], BF16, name="ybt_bf%d" % b, align_bytes=64) for b in range(J // BANK_COLS)]
-        h_bf = keep.tile([P, J, PACK], BF16, name="h_bf", align_bytes=64)
-        h_early = [staged("h_early%d" % c, [P, QUARTER, PACK], BF16, (44, 50)[c]) for c in range(2)]
+        yb_sb = keep.tile([P, 2 * QUARTER], F32, name="yb_sb", align_bytes=64)
+        h_late = keep.tile([P, HALF * PACK], BF16, name="h_late", align_bytes=64)
+        h_bf = [xg[:, HALF * c : HALF * (c + 1)].bitcast(BF16) for c in range(2)]
+        h_bf += [h_late[:, J * c : J * (c + 1)] for c in range(2)]
         hq = keep.tile([P, J], U32, name="hq", align_bytes=64)
         hq_sc = keep.tile([P, J], U8, name="hq_sc", align_bytes=64)
         o_sb = keep.tile([P, J // BANK_COLS, 512], F32, name="o_sb", align_bytes=64)
@@ -80,26 +86,22 @@ def tile_list_htabg_max_res_kernel(
             return dram[a].rearrange("p n t -> p (n t)").bitcast(I32)
 
         for p0, p1 in ((32, 64), (64, P)):
-            nc.vector.memset(sc_raw[p0:p1, :], 0)
             nc.vector.memset(tab_sc[p0:p1, :], 0)
         nc.gpsimd.memset(wgt_rows[64:P, :], 0.0)
         make_identity(nc, ident[:])
-        nc.gpsimd.memset(planes[:], 0)
 
-        nc.sync.dma_start(sc_raw[1:32:2, :].bitcast(U16)[:, 0:255], wa_scales[0].bitcast(U16)[:, 1:256])
-        nc.scalar.dma_start(sc_raw[0:32:2, :], wa_scales[0].bitcast(I32))
         nc.sync.dma_start(idx[:], offs)
-        nc.scalar.dma_start(tab_sc[0:32, :], tab_scales.bitcast(I32).rearrange("a r c -> r a c"))
+        nc.sync.dma_start(tab_sc[0:32, :], tab_scales.bitcast(I32).rearrange("a r c -> r a c"))
+        nc.sync.dma_start(tab_w[:], words(tab_words, 0))
         nc.scalar.dma_start(
             wgt_rows[0:64, :], wgt2.rearrange("(g r) j -> g r j", r=16)[:, 0, :].rearrange("g (b k) -> g b k", k=P)
         )
-        nc.sync.dma_start(tab_w[:], words(tab_words, 0))
-        nc.scalar.dma_start(rows[0:32, 256:384], wb_scales.bitcast(I32).rearrange("a r c -> r a c"))
-        nc.scalar.dma_start(rows[0:32, 448:512], wd_scales[0].bitcast(I32).rearrange("i (a c) -> (i a) c", a=2))
         nc.sync.dma_start(idx2[:], offs2)
-        nc.sync.dma_start(
-            wb_raw[:], wb_words.rearrange("a p n t -> p a (n t)").bitcast(I32)
-        )
+        nc.sync.dma_start(wb_raw[:], wb_words.rearrange("a p n t -> p a (n t)").bitcast(I32))
+        for q in (0, 2, 1, 3):
+            nc.scalar.dma_start(
+                wb_sc[32 * q : 32 * q + 4, :, :], wb_scales.bitcast(I32).rearrange("a r c -> r a c")[4 * q : 4 * q + 4]
+            )
         x_rows = xT.rearrange("(p i) t -> i p t", i=PACK)
 
         def load_x(i):
@@ -113,8 +115,8 @@ def tile_list_htabg_max_res_kernel(
             )
 
         def weight_scale(k, t):
-            c0 = 384 + 64 * k + 32 * (t % 2)
-            return planes[:, t // 2, c0 : c0 + 32].bitcast(U8)
+            c0 = 64 * k + 32 * (t % 2)
+            return late_sc[:, t // 2, c0 : c0 + 32].bitcast(U8)
 
         load_x(0)
         turned = bank("turned", [P, 512], 4)
@@ -127,16 +129,22 @@ def tile_list_htabg_max_res_kernel(
             spread = bank("spread%d" % hf, [P, 512], 5 + hf)
             for u in range(4):
                 nc.tensor.transpose(spread[:, u * P : (u + 1) * P], wgt_t[:, 4 * hf + u, :], ident[:])
-            nc.scalar.copy(wgt[:, hf * HALF : (hf + 1) * HALF], spread[:])
-        nc.vector.tensor_copy(
-            rows[:, 384:448].bitcast(U8).rearrange("p (t c i) -> p c t i", t=2, i=16),
-            sc_raw[:].bitcast(U8).rearrange("p (c i t) -> p c t i", i=16, t=PACK)[:, :, 0:2, :],
-        )
+            if hf == 0:
+                nc.scalar.copy(wgt_head[:], spread[:, 0:QUARTER])
+                nc.scalar.copy(wgt[:, QUARTER:HALF], spread[:, QUARTER:HALF])
+            else:
+                nc.scalar.copy(wgt[:, HALF:J], spread[:])
         nc.vector.tensor_copy(got_sc[:].bitcast(U8), tab_sc[:].bitcast(U8).indirect(idx[:]))
-        nc.vector.tensor_copy(rows[0:32, 0:256], got_sc[0:32, :])
         for q in (0, 2, 1, 3):
-            nc.sync.dma_start(planes[32 * q : 32 * q + 4, :, :], rows[8 * q : 8 * q + 8, :])
+            nc.sync.dma_start(planes[32 * q : 32 * q + 4, :, :], got_sc[8 * q : 8 * q + 8, :])
         load_x(1)
+        sc_raw = staged("sc_raw", [P, R // 4], I32, 16)
+        for p0, p1 in ((32, 64), (64, P)):
+            nc.gpsimd.memset(sc_raw[p0:p1, :], 0)
+        nc.sync.dma_start(sc_raw[1:32:2, :].bitcast(U16)[:, 0:255], wa_scales[0].bitcast(U16)[:, 1:256])
+        nc.sync.dma_start(sc_raw[0:32:2, :], wa_scales[0].bitcast(I32))
+        late_rows = staged("late_rows", [P, R // 4], I32, 16.5)
+        nc.sync.dma_start(late_rows[0:32, 64:128], wd_scales[0].bitcast(I32).rearrange("i (a c) -> (i a) c", a=2))
         load_x(2)
         for h in range(2):
             nc.vector.tensor_copy(
@@ -152,7 +160,7 @@ def tile_list_htabg_max_res_kernel(
         yb = {}
 
         def turn_yb(c):
-            yb[c] = bank("yb%d" % c, [P, 2, QUARTER], 7 - c)
+            yb[c] = bank("yb%d" % c, [P, 2, QUARTER], c)
             for half in range(2):
                 for u in range(2):
                     nc.tensor.transpose(
@@ -169,7 +177,7 @@ def tile_list_htabg_max_res_kernel(
                     lhsT=part_w[b // 4][:, a, (b % 4) * 64 : (b % 4 + 1) * 64].bitcast(U8).bitcast(FP4X4),
                     lhsT_scale=planes[:, a, 32 * b : 32 * b + 32].bitcast(U8),
                     rhs=wb_raw[:, a, :].bitcast(FP8X4),
-                    rhs_scale=planes[:, a, 256:384].bitcast(U8),
+                    rhs_scale=wb_sc[:, a, :].bitcast(U8),
                     start=(a == 0),
                     stop=(a == 1),
                 )
@@ -178,87 +186,89 @@ def tile_list_htabg_max_res_kernel(
             )
         for c in range(4):
             turn_yb(c)
+        nc.scalar.copy(yb_sb[:].rearrange("p (n u) -> p n u", u=2), yb[0][:].rearrange("p u n -> p n u"))
+
+        def place(i, c0):
+            if c0 < QUARTER:
+                return HEAD_BASE + i * HEAD_STEP + c0
+            return i * J + c0
 
         def gather_x(i, c0, c1):
-            nc.vector.tensor_tensor(xg[:, i, c0:c1], x_pl[i][:].indirect(idx2[:, c0 // 16 : c1 // 16]), wgt[:, c0:c1], MULT)
-
-        out_rows = out.rearrange("(a p) j -> p a j", p=P)
-
-        def rounded(c):
-            if c == 0:
-                return xg[:, 3, HALF:J].bitcast(BF16).rearrange("p (n t) -> p n t", t=PACK)
-            if c not in xg_bf:
-                xg_bf[c] = staged("xg_bf%d" % c, [P, STARTS[c + 1] - STARTS[c], PACK], BF16, (0, 40, 42, 48, 52)[c])
-            return xg_bf[c][:]
-
-        def front(c):
-            c0, c1 = STARTS[c], STARTS[c + 1]
-            if c < 3:
-                gather_x(3, c0, c0 + QUARTER)
-            woven = rounded(c).rearrange("p (c k) t -> p c t k", k=4)
-            planes_in = xg[:, :, c0:c1].rearrange("p t (c k) -> p c t k", k=4)
-            if c in (0, 2):
-                nc.scalar.copy(woven[:, 32:64], planes_in[:, 32:64])
-                nc.vector.tensor_copy(woven[:, 0:32], planes_in[:, 0:32])
-            else:
-                nc.scalar.copy(woven, planes_in)
-
-        def rounded_ya(c0, c1):
-            if QUARTER <= c0 < HALF:
-                return ya_second[:, c0 - QUARTER : c1 - QUARTER, :]
-            return ya_bf[:, c0:c1, :]
-
-        def first(c):
-            c0, c1 = STARTS[c], STARTS[c + 1]
-            ch = slice(c0, c1)
-            codes = staged("xq_third", [P, c1 - c0], U32, 52)[:] if c == 2 else xq[:, ch]
-            nc.vector.quantize_mx(
-                out=codes.bitcast(FP8X4), scales=xq_sc[:, ch], in_=rounded(c).rearrange("p n t -> p (n t)")
+            at = place(i, c0)
+            weights = wgt_head if c0 < QUARTER else wgt
+            nc.vector.tensor_tensor(
+                xg[:, at : at + c1 - c0], x_pl[i][:].indirect(idx2[:, c0 // 16 : c1 // 16]), weights[:, c0:c1], MULT
             )
+
+        def weave(u):
+            c0, c1 = UNITS[u]
+            if c0 < QUARTER:
+                four = xg[:, HEAD_BASE - P : HEAD_BASE - P + PACK * HEAD_STEP].rearrange("p (t s) -> p t s", t=PACK)
+                four = four[:, :, P + c0 : P + c1]
+            else:
+                four = xg[:, 0 : PACK * J].rearrange("p (t s) -> p t s", t=PACK)[:, :, c0:c1]
+            nc.scalar.copy(
+                xb[u].rearrange("p (c k t) -> p c t k", k=4, t=PACK), four.rearrange("p t (c k) -> p c t k", k=4)
+            )
+
+        ya = {}
+
+        def first(u):
+            c0, c1 = UNITS[u]
+            nc.vector.quantize_mx(out=xq[:, c0:c1].bitcast(FP8X4), scales=xq_sc[:, c0:c1], in_=xb[u])
             for b in range(c0 // BANK_COLS, c1 // BANK_COLS):
                 cols = slice(b * BANK_COLS, (b + 1) * BANK_COLS)
-                acc = bank("ya%d" % b, [P, PACK, BANK_COLS], b % 2)
+                ya[b] = bank("ya%d" % b, [P, PACK, BANK_COLS], YA_BANKS[b])
                 for t in range(PACK):
                     nc.tensor.matmul_mx(
-                        out=acc[:, t, :],
+                        out=ya[b][:, t, :],
                         lhsT=w_perm[0][:, t, 0, :].bitcast(FP8X4),
                         lhsT_scale=weight_scale(0, t),
-                        rhs=codes[:, b * BANK_COLS - c0 : (b + 1) * BANK_COLS - c0].bitcast(FP8X4),
+                        rhs=xq[:, cols].bitcast(FP8X4),
                         rhs_scale=xq_sc[:, cols],
                         start=True,
                         stop=True,
                     )
-                nc.scalar.copy(rounded_ya(b * BANK_COLS, (b + 1) * BANK_COLS), acc[:].rearrange("p t n -> p n t"))
 
-        def joined(c):
-            return h_early[c][:] if c < 2 else h_bf[:, STARTS[c] : STARTS[c + 1], :]
-
-        def join(c):
-            c0, c1 = STARTS[c], STARTS[c + 1]
-            n0 = c0 % QUARTER
-            nc.vector.tensor_tensor(
-                joined(c).rearrange("p n (u e) -> p n u e", u=2),
-                yb[c0 // QUARTER][:].bitcast(BF16).rearrange("p u (n e) -> p n u e", e=2)[:, n0 : n0 + c1 - c0, :, :],
-                rounded_ya(c0, c1).rearrange("p n (u e) -> p n u e", u=2),
-                MAX,
+        def empty_ya(b):
+            nc.scalar.copy(
+                ya_bf[:, b * R : (b + 1) * R].rearrange("p (n t) -> p n t", t=PACK), ya[b][:].rearrange("p t n -> p n t")
             )
+
+        def join(b, count=1):
+            c, n0, width = b // 2, (b % 2) * BANK_COLS, count * BANK_COLS
+            dst = h_bf[c][:, PACK * n0 : PACK * (n0 + width)]
+            if b < DIRECT:
+                nc.vector.tensor_tensor(
+                    dst.rearrange("p (n t) -> p n t", t=PACK),
+                    ya[b][:].rearrange("p t n -> p n t"),
+                    yb_sb[:, 2 * n0 : 2 * (n0 + width)].bitcast(BF16).rearrange("p (n t) -> p n t", t=PACK),
+                    MAX,
+                )
+            else:
+                nc.vector.tensor_tensor(
+                    dst.rearrange("p (n u e) -> p n u e", u=2, e=2),
+                    yb[c][:].bitcast(BF16).rearrange("p u (n e) -> p n u e", e=2)[:, n0 : n0 + width, :, :],
+                    ya_bf[:, b * R : (b + count) * R].rearrange("p (n u e) -> p n u e", u=2, e=2),
+                    MAX,
+                )
 
         sums = {}
 
-        def second(c):
-            c0, c1 = STARTS[c], STARTS[c + 1]
-            ch = slice(c0, c1)
+        def second(u):
+            c0, c1 = UNITS[u]
+            ch, width = slice(c0, c1), c1 - c0
+            n0 = PACK * (c0 % QUARTER)
             nc.vector.quantize_mx(
-                out=hq[:, ch].bitcast(FP8X4), scales=hq_sc[:, ch], in_=joined(c).rearrange("p n t -> p (n t)")
+                out=hq[:, ch].bitcast(FP8X4), scales=hq_sc[:, ch], in_=h_bf[c0 // QUARTER][:, n0 : n0 + PACK * width]
             )
-            width = c1 - c0
             per_bank = 512 // width
             for g in range(N // P // per_bank):
-                y = bank("y%d_%d" % (c, g), [P, per_bank, width], Y_BANKS[c][g])
-                for u in range(per_bank):
-                    nt = per_bank * g + u
+                y = bank("y%d_%d" % (u, g), [P, per_bank, width], Y_BANKS[u][g])
+                for e in range(per_bank):
+                    nt = per_bank * g + e
                     nc.tensor.matmul_mx(
-                        out=y[:, u, :],
+                        out=y[:, e, :],
                         lhsT=late_w[1][:, 0, nt * P : (nt + 1) * P].bitcast(FP8X4),
                         lhsT_scale=weight_scale(1, nt),
                         rhs=hq[:, ch].bitcast(FP8X4),
@@ -266,57 +276,88 @@ def tile_list_htabg_max_res_kernel(
                         start=True,
                         stop=True,
                     )
-                sums[c, g] = y
+                sums[u, g] = y
 
-        def finish(c, g):
-            if (c, g) not in sums:
-                return
-            c0, c1 = STARTS[c], STARTS[c + 1]
+        out_rows = out.rearrange("(a p) j -> p a j", p=P)
+
+        def finish(u, g, pieces=1):
+            c0, c1 = UNITS[u]
             width = c1 - c0
             per_bank = 512 // width
-            nts = slice(per_bank * g, per_bank * (g + 1))
-            o = o_sb[:, c0 // BANK_COLS + g, :].rearrange("p (u n) -> p u n", u=per_bank)
-            res_part = res_sb[c0 // HALF][:, nts, c0 % HALF : c0 % HALF + width]
-            nc.vector.tensor_tensor(o, sums[c, g][:], res_part, ADD)
-            nc.sync.dma_start(out_rows[:, nts, c0:c1], o)
+            step = per_bank // pieces
+            for e0 in range(0, per_bank, step):
+                nts = slice(per_bank * g + e0, per_bank * g + e0 + step)
+                o = o_sb[:, c0 // BANK_COLS + g, :].rearrange("p (e n) -> p e n", e=per_bank)[:, e0 : e0 + step, :]
+                part, base = res_sb[c0 // BANK_COLS]
+                res_part = part[:, nts, c0 - base : c1 - base]
+                nc.vector.tensor_tensor(o, sums[u, g][:, e0 : e0 + step, :], res_part, ADD)
+                nc.sync.dma_start(out_rows[:, nts, c0:c1], o)
 
-        gather_x(0, 0, J)
+        gather_x(0, 0, QUARTER)
+        gather_x(0, QUARTER, J)
         late_w = [staged("late_w%d" % a, [P, 1, R], I32, 2 * a) for a in range(2)]
         nc.sync.dma_start(late_w[0][:, 0, :], words(wa_words, 0))
-        nc.sync.dma_start(late_w[1][:, 0, :], words(wd_words, 0))
         res_rows = res.rearrange("(a p) j -> p a j", p=P)
         res_sb = []
+
+        def load_res(c0, c1, kib):
+            part = staged("res_sb%d" % c0, [P, N // P, c1 - c0], F32, kib)
+            nc.sync.dma_start(part[:], res_rows[:, :, c0:c1])
+            res_sb.extend((part, c0) for c in range(c0, c1, BANK_COLS))
+
         for i in range(2):
-            gather_x(i + 1, 0, J)
-            res_sb.append(staged("res_sb%d" % i, [P, N // P, HALF], F32, (8, 18)[i]))
-            nc.sync.dma_start(res_sb[i][:], res_rows[:, :, i * HALF : (i + 1) * HALF])
-        front(0)
-        front(1)
+            gather_x(i + 1, 0, QUARTER)
+            if i == 0:
+                nc.vector.tensor_copy(
+                    late_rows[:, 0:64].bitcast(U8).rearrange("p (t c i) -> p c t i", t=2, i=16),
+                    sc_raw[:].bitcast(U8).rearrange("p (c i t) -> p c t i", i=16, t=PACK)[:, :, 0:2, :],
+                )
+                for q in (0, 2, 1, 3):
+                    nc.sync.dma_start(late_sc[32 * q : 32 * q + 4, :, :], late_rows[8 * q : 8 * q + 8, :])
+                nc.sync.dma_start(late_w[1][:, 0, :], words(wd_words, 0))
+            gather_x(i + 1, QUARTER, J)
+            if i == 0:
+                load_res(0, BANK_COLS, 8)
+                load_res(BANK_COLS, QUARTER, 10)
+                load_res(QUARTER, HALF, 12)
+            else:
+                load_res(HALF, J, 18)
+        for u in range(3):
+            gather_x(3, *UNITS[u])
+            weave(u)
+        w_perm = [staged("w_perm0", [P, PACK, 1, P], I32, 54)]
         permute_words(nc.vector, w_perm[0][:], late_w[0][:])
         first(0)
-        front(2)
+        gather_x(3, *UNITS[3])
+        weave(3)
         first(1)
-        gather_x(3, J - QUARTER, J)
-        front(3)
+        gather_x(3, *UNITS[4])
+        weave(4)
         join(0)
         first(2)
         second(0)
         join(1)
         first(3)
-        front(4)
-        finish(0, 0)
         second(1)
-        join(2)
-        finish(0, 1)
         first(4)
-        second(2)
+        empty_ya(2)
+        empty_ya(3)
+        finish(0, 0)
         finish(1, 0)
-        join(3)
-        finish(1, 1)
+        h_bf[1] = staged("h_second", [P, J], BF16, 8)[:]
+        join(2, 2)
+        empty_ya(4)
+        empty_ya(5)
+        join(4, 2)
+        second(2)
+        empty_ya(6)
+        empty_ya(7)
+        join(6, 2)
         second(3)
-        join(4)
         finish(2, 0)
         second(4)
         finish(2, 1)
         finish(3, 0)
+        finish(3, 1)
         finish(4, 0)
+        finish(4, 1, 2)

@@ -85,13 +85,13 @@ def tile_list_htabg_max_res_kernel(
         def words(dram, a):
             return dram[a].rearrange("p n t -> p (n t)").bitcast(I32)
 
-        for p0, p1 in ((32, 64), (64, P)):
+        for p0, p1 in ((0, 64), (96, P)):
             nc.vector.memset(tab_sc[p0:p1, :], 0)
         nc.gpsimd.memset(wgt_rows[64:P, :], 0.0)
         make_identity(nc, ident[:])
 
         nc.sync.dma_start(idx[:], offs)
-        nc.sync.dma_start(tab_sc[0:32, :], tab_scales.bitcast(I32).rearrange("a r c -> r a c"))
+        nc.sync.dma_start(tab_sc[64:96, :], tab_scales.bitcast(I32).rearrange("a r c -> r a c"))
         nc.sync.dma_start(tab_w[:], words(tab_words, 0))
         nc.scalar.dma_start(
             wgt_rows[0:64, :], wgt2.rearrange("(g r) j -> g r j", r=16)[:, 0, :].rearrange("g (b k) -> g b k", k=P)
@@ -136,7 +136,7 @@ def tile_list_htabg_max_res_kernel(
                 nc.scalar.copy(wgt[:, HALF:J], spread[:])
         nc.vector.tensor_copy(got_sc[:].bitcast(U8), tab_sc[:].bitcast(U8).indirect(idx[:]))
         for q in (0, 2, 1, 3):
-            nc.sync.dma_start(planes[32 * q : 32 * q + 4, :, :], got_sc[8 * q : 8 * q + 8, :])
+            nc.sync.dma_start(planes[32 * q : 32 * q + 4, :, :], got_sc[64 + 8 * q : 72 + 8 * q, :])
         load_x(1)
         sc_raw = staged("sc_raw", [P, R // 4], I32, 16)
         for p0, p1 in ((32, 64), (64, P)):

@@ -25,13 +25,13 @@ HALF = J // 2
 UNITS = ((0, 128), (128, 256), (256, 512), (512, 768), (768, 1024))
 HEAD_BASE = 3 * J + 640
 HEAD_STEP = 384
-DIRECT = 2
+DIRECT = 3
 BANK_COLS = 128
 QUARTER = J // 4
 X_KIB = (0, 8, 17, 26)
 BANK_BYTES = 2048
-YA_BANKS = (4, 5, 6, 7, 0, 6, 4, 5)
-Y_BANKS = ((4,), (5,), (7, 1), (0, 6), (2, 3))
+YA_BANKS = (4, 5, 6, 7, 0, 6, 7, 0)
+Y_BANKS = ((4,), (5,), (4, 1), (5, 6), (2, 3))
 
 
 def tile_list_htabg_max_res_kernel(
@@ -74,7 +74,7 @@ def tile_list_htabg_max_res_kernel(
         xq_sc = keep.tile([P, J], U8, name="xq_sc", align_bytes=64)
         ya_bf = keep.tile([P, J * PACK], BF16, name="ya_bf", align_bytes=64)
         ybt_bf = [keep.tile([P, R], BF16, name="ybt_bf%d" % b, align_bytes=64) for b in range(J // BANK_COLS)]
-        yb_sb = keep.tile([P, 2 * QUARTER], F32, name="yb_sb", align_bytes=64)
+        yb_sb = keep.tile([P, 3 * QUARTER], F32, name="yb_sb", align_bytes=64)
         h_late = keep.tile([P, HALF * PACK], BF16, name="h_late", align_bytes=64)
         h_bf = [xg[:, HALF * c : HALF * (c + 1)].bitcast(BF16) for c in range(2)]
         h_bf += [h_late[:, J * c : J * (c + 1)] for c in range(2)]
@@ -186,7 +186,10 @@ def tile_list_htabg_max_res_kernel(
             )
         for c in range(4):
             turn_yb(c)
-        nc.scalar.copy(yb_sb[:].rearrange("p (n u) -> p n u", u=2), yb[0][:].rearrange("p u n -> p n u"))
+        nc.scalar.copy(yb_sb[:, 0:HALF].rearrange("p (n u) -> p n u", u=2), yb[0][:].rearrange("p u n -> p n u"))
+        nc.scalar.copy(
+            yb_sb[:, HALF:].rearrange("p (n u) -> p n u", u=2), yb[1][:, :, 0:BANK_COLS].rearrange("p u n -> p n u")
+        )
 
         def place(i, c0):
             if c0 < QUARTER:
@@ -242,7 +245,7 @@ def tile_list_htabg_max_res_kernel(
                 nc.vector.tensor_tensor(
                     dst.rearrange("p (n t) -> p n t", t=PACK),
                     ya[b][:].rearrange("p t n -> p n t"),
-                    yb_sb[:, 2 * n0 : 2 * (n0 + width)].bitcast(BF16).rearrange("p (n t) -> p n t", t=PACK),
+                    yb_sb[:, 2 * b * BANK_COLS : 2 * (b + 1) * BANK_COLS].bitcast(BF16).rearrange("p (n t) -> p n t", t=PACK),
                     MAX,
                 )
             else:
@@ -339,15 +342,15 @@ def tile_list_htabg_max_res_kernel(
         join(1)
         first(3)
         second(1)
+        join(2)
         first(4)
-        empty_ya(2)
         empty_ya(3)
         finish(0, 0)
         finish(1, 0)
-        h_bf[1] = staged("h_second", [P, J], BF16, 8)[:]
-        join(2, 2)
+        join(3)
         empty_ya(4)
         empty_ya(5)
+        h_bf[2] = staged("h_third", [P, J], BF16, 8)[:]
         join(4, 2)
         second(2)
         empty_ya(6)

@@ -184,12 +184,15 @@ def tile_list_htabg_max_res_kernel(
             nc.scalar.copy(
                 ybt_bf[b][:].rearrange("p (u m e) -> p u m e", u=2, e=2), acc[:].rearrange("p (m u e) -> p u m e", u=2, e=2)
             )
-        for c in range(4):
-            turn_yb(c)
-        nc.scalar.copy(yb_sb[:, 0:HALF].rearrange("p (n u) -> p n u", u=2), yb[0][:].rearrange("p u n -> p n u"))
-        nc.scalar.copy(
-            yb_sb[:, HALF:].rearrange("p (n u) -> p n u", u=2), yb[1][:, :, 0:BANK_COLS].rearrange("p u n -> p n u")
-        )
+            if b == 3:
+                turn_yb(0)
+                turn_yb(1)
+                nc.scalar.copy(yb_sb[:, 0:HALF].rearrange("p (n u) -> p n u", u=2), yb[0][:].rearrange("p u n -> p n u"))
+                nc.scalar.copy(
+                    yb_sb[:, HALF:].rearrange("p (n u) -> p n u", u=2), yb[1][:, :, 0:BANK_COLS].rearrange("p u n -> p n u")
+                )
+        turn_yb(2)
+        turn_yb(3)
 
         def place(i, c0):
             if c0 < QUARTER:
@@ -345,18 +348,19 @@ def tile_list_htabg_max_res_kernel(
         join(2)
         first(4)
         empty_ya(3)
-        finish(0, 0)
-        finish(1, 0)
         join(3)
+        finish(0, 0)
+        second(2)
         empty_ya(4)
         empty_ya(5)
         h_bf[2] = staged("h_third", [P, J], BF16, 8)[:]
         join(4, 2)
-        second(2)
+        finish(1, 0)
+        second(3)
         empty_ya(6)
         empty_ya(7)
+        h_bf[3] = staged("h_fourth", [P, J], BF16, 10)[:]
         join(6, 2)
-        second(3)
         finish(2, 0)
         second(4)
         finish(2, 1)

@@ -246,9 +246,11 @@ def tile_list_htabg_max_res_kernel(
             dst = h_bf[c][:, PACK * n0 : PACK * (n0 + width)]
             if b < DIRECT:
                 nc.vector.tensor_tensor(
-                    dst.rearrange("p (n t) -> p n t", t=PACK),
-                    ya[b][:].rearrange("p t n -> p n t"),
-                    yb_sb[:, 2 * b * BANK_COLS : 2 * (b + 1) * BANK_COLS].bitcast(BF16).rearrange("p (n t) -> p n t", t=PACK),
+                    dst.rearrange("p (c e t) -> p c t e", e=2, t=PACK),
+                    ya[b][:].rearrange("p t (c e) -> p c t e", e=2),
+                    yb_sb[:, 2 * b * BANK_COLS : 2 * (b + 1) * BANK_COLS]
+                    .bitcast(BF16)
+                    .rearrange("p (c e t) -> p c t e", e=2, t=PACK),
                     MAX,
                 )
             else:

@@ -20,18 +20,34 @@ ADD = mybir.AluOpType.add
 
 P = 128
 PACK = 4
-QUADS = 4
 HALF = J // 2
+QUARTER = J // 4
+BLOCK = 128
+BANK_BYTES = 2048
+BANK_FLOATS = 512
+
 UNITS = ((0, 128), (128, 256), (256, 512), (512, 768), (768, 1024))
+DIRECT = 3
+
 HEAD_BASE = 3 * J + 640
 HEAD_STEP = 384
-DIRECT = 3
-BANK_COLS = 128
-QUARTER = J // 4
+
 X_KIB = (0, 8, 17, 26)
-BANK_BYTES = 2048
+TAB_SCALES_KIB = 15.5
+TAB_WORDS_KIB = 29
+WA_RAW_ROWS_KIB = 16
+LATE_ROWS_KIB = 16.5
+LATE_WORDS_KIB = (0, 2)
+RES_KIB = (8, 10, 12, 18)
+WOVEN_KIB = 36
+HEAD_WEIGHTS_KIB = 54
+H_LATE_KIB = (8, 10)
+
+QUADRANTS = (0, 2, 1, 3)
+TAB_ROWS = 64
+
 YA_BANKS = (4, 5, 6, 7, 0, 6, 7, 0)
-Y_BANKS = ((4,), (5,), (4, 1), (5, 6), (2, 3))
+Y_BANKS = ((4, 5), (4, 1), (5, 6), (2, 3))
 
 
 def tile_list_htabg_max_res_kernel(
@@ -50,55 +66,56 @@ def tile_list_htabg_max_res_kernel(
         def staged(name, shape, dtype, kib):
             return stage.tile(shape, dtype, name=name, offset=int(kib * 1024), align_bytes=64)
 
+        def kept(name, shape, dtype):
+            return keep.tile(shape, dtype, name=name, align_bytes=64)
+
         idx = keep.tile([P, J // 16], U16, name="idx")
         idx2 = keep.tile([P, J // 16], U16, name="idx2")
-        tab_sc = staged("tab_sc", [P, T // 4], I32, 15.5)
-        tab_w = staged("tab_w", [P, T], I32, 29)
-        got_sc = keep.tile([P, J // 4], I32, name="got_sc", align_bytes=64)
-        got_w = keep.tile([P, J], I32, name="got_w", align_bytes=64)
-        part_w = [keep.tile([P, 2, HALF // 2], I32, name="part_w%d" % h, align_bytes=64) for h in range(2)]
-        wb_raw = keep.tile([P, 2, R], I32, name="wb_raw", align_bytes=64)
-        wgt_head = staged("wgt_head", [P, QUARTER], F32, 54)
-        planes = keep.tile([P, 2, 256], I32, name="planes", align_bytes=64)
-        wb_sc = keep.tile([P, 2, R // 4], I32, name="wb_sc", align_bytes=64)
-        late_sc = keep.tile([P, 2, R // 4], I32, name="late_sc", align_bytes=64)
-        wgt = keep.tile([P, J], F32, name="wgt", align_bytes=64)
-        wgt_rows = keep.tile([P, P], F32, name="wgt_rows", align_bytes=64)
-        wgt_t = keep.tile([P, J // P, P], F32, name="wgt_t", align_bytes=64)
-        ident = keep.tile([P, P], F32, name="ident", align_bytes=64)
+        tab_sc = staged("tab_sc", [P, T // 4], I32, TAB_SCALES_KIB)
+        tab_w = staged("tab_w", [P, T], I32, TAB_WORDS_KIB)
+        got_sc = kept("got_sc", [P, J // 4], I32)
+        got_w = kept("got_w", [P, J], I32)
+        part_w = [kept("part_w%d" % h, [P, 2, HALF // 2], I32) for h in range(2)]
+        wb_raw = kept("wb_raw", [P, 2, R], I32)
+        wgt_head = staged("wgt_head", [P, QUARTER], F32, HEAD_WEIGHTS_KIB)
+        planes = kept("planes", [P, 2, J // 4], I32)
+        wb_sc = kept("wb_sc", [P, 2, R // 4], I32)
+        late_sc = kept("late_sc", [P, 2, R // 4], I32)
+        wgt = kept("wgt", [P, J], F32)
+        wgt_rows = kept("wgt_rows", [P, P], F32)
+        wgt_t = kept("wgt_t", [P, J // P, P], F32)
+        ident = kept("ident", [P, P], F32)
         x_pl = []
-        xg = keep.tile([P, 5 * J], F32, name="xg", align_bytes=64)
-        xb = [staged("xb%d" % u, [P, PACK * (UNITS[u][1] - UNITS[u][0])], BF16, 36 + 2 * u)[:] for u in (0, 2, 3, 4)]
+        xg = kept("xg", [P, 5 * J], F32)
+        xb = [staged("xb%d" % u, [P, PACK * (UNITS[u][1] - UNITS[u][0])], BF16, WOVEN_KIB + 2 * u)[:] for u in (0, 2, 3, 4)]
         xb.insert(1, xg[:, 0:QUARTER].bitcast(BF16))
-        xq = keep.tile([P, J], U32, name="xq", align_bytes=64)
-        xq_sc = keep.tile([P, J], U8, name="xq_sc", align_bytes=64)
-        ya_bf = keep.tile([P, J * PACK], BF16, name="ya_bf", align_bytes=64)
-        ybt_bf = [keep.tile([P, R], BF16, name="ybt_bf%d" % b, align_bytes=64) for b in range(J // BANK_COLS)]
-        yb_sb = keep.tile([P, 3 * QUARTER], F32, name="yb_sb", align_bytes=64)
-        h_late = keep.tile([P, HALF * PACK], BF16, name="h_late", align_bytes=64)
+        xq = kept("xq", [P, J], U32)
+        xq_sc = kept("xq_sc", [P, J], U8)
+        ya_bf = kept("ya_bf", [P, J * PACK], BF16)
+        ybt_bf = [kept("ybt_bf%d" % b, [P, R], BF16) for b in range(J // BLOCK)]
+        yb_sb = kept("yb_sb", [P, 2 * DIRECT * BLOCK], F32)
         h_bf = [xg[:, HALF * c : HALF * (c + 1)].bitcast(BF16) for c in range(2)]
-        h_bf += [h_late[:, J * c : J * (c + 1)] for c in range(2)]
-        hq = keep.tile([P, J], U32, name="hq", align_bytes=64)
-        hq_sc = keep.tile([P, J], U8, name="hq_sc", align_bytes=64)
-        o_sb = keep.tile([P, J // BANK_COLS, 512], F32, name="o_sb", align_bytes=64)
+        hq = kept("hq", [P, J], U32)
+        hq_sc = kept("hq_sc", [P, J], U8)
+        o_sb = kept("o_sb", [P, J // BLOCK, BANK_FLOATS], F32)
 
-        def words(dram, a):
-            return dram[a].rearrange("p n t -> p (n t)").bitcast(I32)
+        def words(dram):
+            return dram[0].rearrange("p n t -> p (n t)").bitcast(I32)
 
-        for p0, p1 in ((0, 64), (96, P)):
+        for p0, p1 in ((0, TAB_ROWS), (TAB_ROWS + 32, P)):
             nc.vector.memset(tab_sc[p0:p1, :], 0)
         nc.gpsimd.memset(wgt_rows[64:P, :], 0.0)
         make_identity(nc, ident[:])
 
         nc.sync.dma_start(idx[:], offs)
-        nc.sync.dma_start(tab_sc[64:96, :], tab_scales.bitcast(I32).rearrange("a r c -> r a c"))
-        nc.sync.dma_start(tab_w[:], words(tab_words, 0))
+        nc.sync.dma_start(tab_sc[TAB_ROWS : TAB_ROWS + 32, :], tab_scales.bitcast(I32).rearrange("a r c -> r a c"))
+        nc.sync.dma_start(tab_w[:], words(tab_words))
         nc.scalar.dma_start(
             wgt_rows[0:64, :], wgt2.rearrange("(g r) j -> g r j", r=16)[:, 0, :].rearrange("g (b k) -> g b k", k=P)
         )
         nc.sync.dma_start(idx2[:], offs2)
         nc.sync.dma_start(wb_raw[:], wb_words.rearrange("a p n t -> p a (n t)").bitcast(I32))
-        for q in (0, 2, 1, 3):
+        for q in QUADRANTS:
             nc.scalar.dma_start(
                 wb_sc[32 * q : 32 * q + 4, :, :], wb_scales.bitcast(I32).rearrange("a r c -> r a c")[4 * q : 4 * q + 4]
             )
@@ -108,44 +125,42 @@ def tile_list_htabg_max_res_kernel(
             x_pl.append(staged("x_pl%d" % i, [P, T], F32, X_KIB[i]))
             nc.sync.dma_start(x_pl[i][:], x_rows[i])
 
-        def permute_words(eng, perm, raw):
-            eng.tensor_copy(
-                perm.rearrange("p t a (c i) -> p (a c) t i", i=4),
-                raw.rearrange("p a (c i t) -> p (a c) t i", i=4, t=PACK),
-            )
-
         def weight_scale(k, t):
             c0 = 64 * k + 32 * (t % 2)
             return late_sc[:, t // 2, c0 : c0 + 32].bitcast(U8)
 
         load_x(0)
-        turned = bank("turned", [P, 512], 4)
+
+        turned = bank("turned", [P, BANK_FLOATS], 4)
         nc.tensor.transpose(turned[:, 0:P], wgt_rows[:], ident[:])
         nc.scalar.copy(
             wgt_t[:].rearrange("p b (g r) -> p b g r", r=16),
             turned[:, 0:64].rearrange("p (g b) -> p b g", g=8).unsqueeze(3).to_broadcast([P, 8, 8, 16]),
         )
         for hf in range(2):
-            spread = bank("spread%d" % hf, [P, 512], 5 + hf)
-            for u in range(4):
-                nc.tensor.transpose(spread[:, u * P : (u + 1) * P], wgt_t[:, 4 * hf + u, :], ident[:])
+            spread = bank("spread%d" % hf, [P, BANK_FLOATS], 5 + hf)
+            for e in range(4):
+                nc.tensor.transpose(spread[:, e * P : (e + 1) * P], wgt_t[:, 4 * hf + e, :], ident[:])
             if hf == 0:
                 nc.scalar.copy(wgt_head[:], spread[:, 0:QUARTER])
                 nc.scalar.copy(wgt[:, QUARTER:HALF], spread[:, QUARTER:HALF])
             else:
                 nc.scalar.copy(wgt[:, HALF:J], spread[:])
+
         nc.vector.tensor_copy(got_sc[:].bitcast(U8), tab_sc[:].bitcast(U8).indirect(idx[:]))
-        for q in (0, 2, 1, 3):
-            nc.sync.dma_start(planes[32 * q : 32 * q + 4, :, :], got_sc[64 + 8 * q : 72 + 8 * q, :])
+        for q in QUADRANTS:
+            nc.sync.dma_start(planes[32 * q : 32 * q + 4, :, :], got_sc[TAB_ROWS + 8 * q : TAB_ROWS + 8 * q + 8, :])
         load_x(1)
-        sc_raw = staged("sc_raw", [P, R // 4], I32, 16)
+
+        sc_raw = staged("sc_raw", [P, R // 4], I32, WA_RAW_ROWS_KIB)
         for p0, p1 in ((32, 64), (64, P)):
             nc.gpsimd.memset(sc_raw[p0:p1, :], 0)
         nc.sync.dma_start(sc_raw[1:32:2, :].bitcast(U16)[:, 0:255], wa_scales[0].bitcast(U16)[:, 1:256])
         nc.sync.dma_start(sc_raw[0:32:2, :], wa_scales[0].bitcast(I32))
-        late_rows = staged("late_rows", [P, R // 4], I32, 16.5)
+        late_rows = staged("late_rows", [P, R // 4], I32, LATE_ROWS_KIB)
         nc.sync.dma_start(late_rows[0:32, 64:128], wd_scales[0].bitcast(I32).rearrange("i (a c) -> (i a) c", a=2))
         load_x(2)
+
         for h in range(2):
             nc.vector.tensor_copy(
                 got_w[:, h * HALF : (h + 1) * HALF].bitcast(U32), tab_w[:].bitcast(U32).indirect(idx[:, 32 * h : 32 * h + 32])
@@ -164,12 +179,12 @@ def tile_list_htabg_max_res_kernel(
             for half in range(2):
                 for u in range(2):
                     nc.tensor.transpose(
-                        yb[c][:, u, half * BANK_COLS : (half + 1) * BANK_COLS],
+                        yb[c][:, u, half * BLOCK : (half + 1) * BLOCK],
                         ybt_bf[2 * c + half][:].bitcast(F32)[:, u * P : (u + 1) * P],
                         ident[:],
                     )
 
-        for b in range(J // BANK_COLS):
+        def multiply_yb(b):
             acc = bank("ybt%d" % b, [P, R], b)
             for a in range(2):
                 nc.tensor.matmul_mx(
@@ -184,51 +199,50 @@ def tile_list_htabg_max_res_kernel(
             nc.scalar.copy(
                 ybt_bf[b][:].rearrange("p (u m e) -> p u m e", u=2, e=2), acc[:].rearrange("p (m u e) -> p u m e", u=2, e=2)
             )
-            if b == 3:
-                turn_yb(0)
-                turn_yb(1)
-                nc.scalar.copy(yb_sb[:, 0:HALF].rearrange("p (n u) -> p n u", u=2), yb[0][:].rearrange("p u n -> p n u"))
-                nc.scalar.copy(
-                    yb_sb[:, HALF:].rearrange("p (n u) -> p n u", u=2), yb[1][:, :, 0:BANK_COLS].rearrange("p u n -> p n u")
-                )
+
+        for b in range(4):
+            multiply_yb(b)
+        turn_yb(0)
+        turn_yb(1)
+        nc.scalar.copy(yb_sb[:, 0:HALF].rearrange("p (n u) -> p n u", u=2), yb[0][:].rearrange("p u n -> p n u"))
+        nc.scalar.copy(yb_sb[:, HALF:].rearrange("p (n u) -> p n u", u=2), yb[1][:, :, 0:BLOCK].rearrange("p u n -> p n u"))
+        for b in range(4, J // BLOCK):
+            multiply_yb(b)
         turn_yb(2)
         turn_yb(3)
 
-        def place(i, c0):
-            if c0 < QUARTER:
-                return HEAD_BASE + i * HEAD_STEP + c0
-            return i * J + c0
-
         def gather_x(i, c0, c1):
-            at = place(i, c0)
-            weights = wgt_head if c0 < QUARTER else wgt
+            if c0 < QUARTER:
+                at, weights = HEAD_BASE + i * HEAD_STEP + c0, wgt_head
+            else:
+                at, weights = i * J + c0, wgt
             nc.vector.tensor_tensor(
                 xg[:, at : at + c1 - c0], x_pl[i][:].indirect(idx2[:, c0 // 16 : c1 // 16]), weights[:, c0:c1], MULT
             )
 
-        def weave(u):
-            c0, c1 = UNITS[u]
+        def weave(unit):
+            c0, c1 = UNITS[unit]
             if c0 < QUARTER:
-                four = xg[:, HEAD_BASE - P : HEAD_BASE - P + PACK * HEAD_STEP].rearrange("p (t s) -> p t s", t=PACK)
-                four = four[:, :, P + c0 : P + c1]
+                four = xg[:, HEAD_BASE - BLOCK : HEAD_BASE - BLOCK + PACK * HEAD_STEP].rearrange("p (t s) -> p t s", t=PACK)
+                four = four[:, :, BLOCK + c0 : BLOCK + c1]
             else:
                 four = xg[:, 0 : PACK * J].rearrange("p (t s) -> p t s", t=PACK)[:, :, c0:c1]
             nc.scalar.copy(
-                xb[u].rearrange("p (c k t) -> p c t k", k=4, t=PACK), four.rearrange("p t (c k) -> p c t k", k=4)
+                xb[unit].rearrange("p (c k t) -> p c t k", k=4, t=PACK), four.rearrange("p t (c k) -> p c t k", k=4)
             )
 
         ya = {}
 
-        def first(u):
-            c0, c1 = UNITS[u]
-            nc.vector.quantize_mx(out=xq[:, c0:c1].bitcast(FP8X4), scales=xq_sc[:, c0:c1], in_=xb[u])
-            for b in range(c0 // BANK_COLS, c1 // BANK_COLS):
-                cols = slice(b * BANK_COLS, (b + 1) * BANK_COLS)
-                ya[b] = bank("ya%d" % b, [P, PACK, BANK_COLS], YA_BANKS[b])
+        def first_stage(unit):
+            c0, c1 = UNITS[unit]
+            nc.vector.quantize_mx(out=xq[:, c0:c1].bitcast(FP8X4), scales=xq_sc[:, c0:c1], in_=xb[unit])
+            for b in range(c0 // BLOCK, c1 // BLOCK):
+                cols = slice(b * BLOCK, (b + 1) * BLOCK)
+                ya[b] = bank("ya%d" % b, [P, PACK, BLOCK], YA_BANKS[b])
                 for t in range(PACK):
                     nc.tensor.matmul_mx(
                         out=ya[b][:, t, :],
-                        lhsT=w_perm[0][:, t, 0, :].bitcast(FP8X4),
+                        lhsT=w_perm[:, t, 0, :].bitcast(FP8X4),
                         lhsT_scale=weight_scale(0, t),
                         rhs=xq[:, cols].bitcast(FP8X4),
                         rhs_scale=xq_sc[:, cols],
@@ -236,137 +250,124 @@ def tile_list_htabg_max_res_kernel(
                         stop=True,
                     )
 
+        def h_of(b, count=1):
+            n0 = (b % 2) * BLOCK
+            return h_bf[b // 2][:, PACK * n0 : PACK * (n0 + count * BLOCK)]
+
+        def join_direct(b):
+            nc.vector.tensor_tensor(
+                h_of(b).rearrange("p (c e t) -> p c t e", e=2, t=PACK),
+                ya[b][:].rearrange("p t (c e) -> p c t e", e=2),
+                yb_sb[:, 2 * b * BLOCK : 2 * (b + 1) * BLOCK].bitcast(BF16).rearrange("p (c e t) -> p c t e", e=2, t=PACK),
+                MAX,
+            )
+
         def empty_ya(b):
             nc.scalar.copy(
                 ya_bf[:, b * R : (b + 1) * R].rearrange("p (n t) -> p n t", t=PACK), ya[b][:].rearrange("p t n -> p n t")
             )
 
         def join(b, count=1):
-            c, n0, width = b // 2, (b % 2) * BANK_COLS, count * BANK_COLS
-            dst = h_bf[c][:, PACK * n0 : PACK * (n0 + width)]
-            if b < DIRECT:
-                nc.vector.tensor_tensor(
-                    dst.rearrange("p (c e t) -> p c t e", e=2, t=PACK),
-                    ya[b][:].rearrange("p t (c e) -> p c t e", e=2),
-                    yb_sb[:, 2 * b * BANK_COLS : 2 * (b + 1) * BANK_COLS]
-                    .bitcast(BF16)
-                    .rearrange("p (c e t) -> p c t e", e=2, t=PACK),
-                    MAX,
-                )
-            else:
-                nc.vector.tensor_tensor(
-                    dst.rearrange("p (n u e) -> p n u e", u=2, e=2),
-                    yb[c][:].bitcast(BF16).rearrange("p u (n e) -> p n u e", e=2)[:, n0 : n0 + width, :, :],
-                    ya_bf[:, b * R : (b + count) * R].rearrange("p (n u e) -> p n u e", u=2, e=2),
-                    MAX,
-                )
+            n0 = (b % 2) * BLOCK
+            nc.vector.tensor_tensor(
+                h_of(b, count).rearrange("p (n u e) -> p n u e", u=2, e=2),
+                yb[b // 2][:].bitcast(BF16).rearrange("p u (n e) -> p n u e", e=2)[:, n0 : n0 + count * BLOCK, :, :],
+                ya_bf[:, b * R : (b + count) * R].rearrange("p (n u e) -> p n u e", u=2, e=2),
+                MAX,
+            )
 
         sums = {}
 
-        def second(u):
-            c0, c1 = UNITS[u]
-            ch, width = slice(c0, c1), c1 - c0
-            n0 = PACK * (c0 % QUARTER)
-            nc.vector.quantize_mx(
-                out=hq[:, ch].bitcast(FP8X4), scales=hq_sc[:, ch], in_=h_bf[c0 // QUARTER][:, n0 : n0 + PACK * width]
-            )
-            per_bank = 512 // width
-            for g in range(N // P // per_bank):
-                y = bank("y%d_%d" % (u, g), [P, per_bank, width], Y_BANKS[u][g])
-                for e in range(per_bank):
-                    nt = per_bank * g + e
+        def second_stage(c):
+            cols = slice(c * QUARTER, (c + 1) * QUARTER)
+            nc.vector.quantize_mx(out=hq[:, cols].bitcast(FP8X4), scales=hq_sc[:, cols], in_=h_bf[c])
+            for g in range(2):
+                y = bank("y%d_%d" % (c, g), [P, 2, QUARTER], Y_BANKS[c][g])
+                for e in range(2):
+                    nt = 2 * g + e
                     nc.tensor.matmul_mx(
                         out=y[:, e, :],
                         lhsT=late_w[1][:, 0, nt * P : (nt + 1) * P].bitcast(FP8X4),
                         lhsT_scale=weight_scale(1, nt),
-                        rhs=hq[:, ch].bitcast(FP8X4),
-                        rhs_scale=hq_sc[:, ch],
+                        rhs=hq[:, cols].bitcast(FP8X4),
+                        rhs_scale=hq_sc[:, cols],
                         start=True,
                         stop=True,
                     )
-                sums[u, g] = y
+                sums[c, g] = y
 
         out_rows = out.rearrange("(a p) j -> p a j", p=P)
+        res_rows = res.rearrange("(a p) j -> p a j", p=P)
+        res_sb = {}
 
-        def finish(u, g, pieces=1):
-            c0, c1 = UNITS[u]
-            width = c1 - c0
-            per_bank = 512 // width
-            step = per_bank // pieces
-            for e0 in range(0, per_bank, step):
-                nts = slice(per_bank * g + e0, per_bank * g + e0 + step)
-                o = o_sb[:, c0 // BANK_COLS + g, :].rearrange("p (e n) -> p e n", e=per_bank)[:, e0 : e0 + step, :]
-                part, base = res_sb[c0 // BANK_COLS]
-                res_part = part[:, nts, c0 - base : c1 - base]
-                nc.vector.tensor_tensor(o, sums[u, g][:, e0 : e0 + step, :], res_part, ADD)
-                nc.sync.dma_start(out_rows[:, nts, c0:c1], o)
+        def load_res(quarters, banks, kib):
+            nts, cols = slice(2 * banks[0], 2 * banks[-1] + 2), slice(quarters[0] * QUARTER, (quarters[-1] + 1) * QUARTER)
+            part = staged("res_sb%d" % kib, [P, 2 * len(banks), len(quarters) * QUARTER], F32, kib)
+            nc.sync.dma_start(part[:], res_rows[:, nts, cols])
+            for ci, c in enumerate(quarters):
+                for gi, g in enumerate(banks):
+                    res_sb[c, g] = part[:, 2 * gi : 2 * gi + 2, ci * QUARTER : (ci + 1) * QUARTER]
+
+        def finish(c, g, pieces=1):
+            step = 2 // pieces
+            for e0 in range(0, 2, step):
+                es = slice(e0, e0 + step)
+                o = o_sb[:, 2 * c + g, :].rearrange("p (e n) -> p e n", e=2)[:, es, :]
+                nc.vector.tensor_tensor(o, sums[c, g][:, es, :], res_sb[c, g][:, es, :], ADD)
+                nc.sync.dma_start(out_rows[:, 2 * g + e0 : 2 * g + e0 + step, c * QUARTER : (c + 1) * QUARTER], o)
 
         gather_x(0, 0, QUARTER)
         gather_x(0, QUARTER, J)
-        late_w = [staged("late_w%d" % a, [P, 1, R], I32, 2 * a) for a in range(2)]
-        nc.sync.dma_start(late_w[0][:, 0, :], words(wa_words, 0))
-        res_rows = res.rearrange("(a p) j -> p a j", p=P)
-        res_sb = []
+        late_w = [staged("late_w%d" % k, [P, 1, R], I32, LATE_WORDS_KIB[k]) for k in range(2)]
+        nc.sync.dma_start(late_w[0][:, 0, :], words(wa_words))
+        gather_x(1, 0, QUARTER)
+        nc.vector.tensor_copy(
+            late_rows[:, 0:64].bitcast(U8).rearrange("p (t c i) -> p c t i", t=2, i=16),
+            sc_raw[:].bitcast(U8).rearrange("p (c i t) -> p c t i", i=16, t=PACK)[:, :, 0:2, :],
+        )
+        for q in QUADRANTS:
+            nc.sync.dma_start(late_sc[32 * q : 32 * q + 4, :, :], late_rows[8 * q : 8 * q + 8, :])
+        nc.sync.dma_start(late_w[1][:, 0, :], words(wd_words))
+        gather_x(1, QUARTER, J)
+        load_res((0,), (0,), RES_KIB[0])
+        load_res((0,), (1,), RES_KIB[1])
+        load_res((1,), (0, 1), RES_KIB[2])
+        gather_x(2, 0, QUARTER)
+        gather_x(2, QUARTER, J)
+        load_res((2, 3), (0, 1), RES_KIB[3])
 
-        def load_res(c0, c1, kib):
-            part = staged("res_sb%d" % c0, [P, N // P, c1 - c0], F32, kib)
-            nc.sync.dma_start(part[:], res_rows[:, :, c0:c1])
-            res_sb.extend((part, c0) for c in range(c0, c1, BANK_COLS))
+        for unit in range(3):
+            gather_x(3, *UNITS[unit])
+            weave(unit)
+        w_perm = staged("w_perm0", [P, PACK, 1, P], I32, HEAD_WEIGHTS_KIB)
+        nc.vector.tensor_copy(
+            w_perm[:].rearrange("p t a (c i) -> p (a c) t i", i=4),
+            late_w[0][:].rearrange("p a (c i t) -> p (a c) t i", i=4, t=PACK),
+        )
+        for unit in range(2):
+            first_stage(unit)
+            gather_x(3, *UNITS[3 + unit])
+            weave(3 + unit)
 
-        for i in range(2):
-            gather_x(i + 1, 0, QUARTER)
-            if i == 0:
-                nc.vector.tensor_copy(
-                    late_rows[:, 0:64].bitcast(U8).rearrange("p (t c i) -> p c t i", t=2, i=16),
-                    sc_raw[:].bitcast(U8).rearrange("p (c i t) -> p c t i", i=16, t=PACK)[:, :, 0:2, :],
-                )
-                for q in (0, 2, 1, 3):
-                    nc.sync.dma_start(late_sc[32 * q : 32 * q + 4, :, :], late_rows[8 * q : 8 * q + 8, :])
-                nc.sync.dma_start(late_w[1][:, 0, :], words(wd_words, 0))
-            gather_x(i + 1, QUARTER, J)
-            if i == 0:
-                load_res(0, BANK_COLS, 8)
-                load_res(BANK_COLS, QUARTER, 10)
-                load_res(QUARTER, HALF, 12)
-            else:
-                load_res(HALF, J, 18)
-        for u in range(3):
-            gather_x(3, *UNITS[u])
-            weave(u)
-        w_perm = [staged("w_perm0", [P, PACK, 1, P], I32, 54)]
-        permute_words(nc.vector, w_perm[0][:], late_w[0][:])
-        first(0)
-        gather_x(3, *UNITS[3])
-        weave(3)
-        first(1)
-        gather_x(3, *UNITS[4])
-        weave(4)
-        join(0)
-        first(2)
-        second(0)
-        join(1)
-        first(3)
-        second(1)
-        join(2)
-        first(4)
+        for unit in range(2):
+            join_direct(unit)
+            first_stage(2 + unit)
+        second_stage(0)
+        join_direct(2)
+        first_stage(4)
         empty_ya(3)
         join(3)
-        finish(0, 0)
-        second(2)
-        empty_ya(4)
-        empty_ya(5)
-        h_bf[2] = staged("h_third", [P, J], BF16, 8)[:]
-        join(4, 2)
+        for c in (2, 3):
+            finish(0, c - 2)
+            second_stage(c - 1)
+            for b in (2 * c, 2 * c + 1):
+                empty_ya(b)
+            h_bf.append(staged(("h_third", "h_fourth")[c - 2], [P, J], BF16, H_LATE_KIB[c - 2])[:])
+            join(2 * c, 2)
         finish(1, 0)
-        second(3)
-        empty_ya(6)
-        empty_ya(7)
-        h_bf[3] = staged("h_fourth", [P, J], BF16, 10)[:]
-        join(6, 2)
+        second_stage(3)
+        finish(1, 1)
         finish(2, 0)
-        second(4)
         finish(2, 1)
         finish(3, 0)
-        finish(3, 1)
-        finish(4, 0)
-        finish(4, 1, 2)
+        finish(3, 1, 2)

from contextlib import ExitStack

import concourse.mybir as mybir
from concourse.masks import make_identity

K, L, R, N, T, J = 512, 1024, 512, 512, 2048, 1024
FLOPS = 2 * J * (K * R + L * R + R * N)

F32 = mybir.dt.float32
BF16 = mybir.dt.bfloat16
I32 = mybir.dt.int32
U32 = mybir.dt.uint32
U16 = mybir.dt.uint16
U8 = mybir.dt.uint8
FP8X4 = mybir.dt.float8_e4m3fn_x4
FP4X4 = mybir.dt.float4_e2m1fn_x4
MULT = mybir.AluOpType.mult
MAX = mybir.AluOpType.max
ADD = mybir.AluOpType.add

P = 128
PACK = 4
HALF = J // 2
QUARTER = J // 4
BLOCK = 128
BANK_BYTES = 2048
BANK_FLOATS = 512

UNITS = ((0, 128), (128, 256), (256, 512), (512, 768), (768, 1024))
DIRECT = 3

HEAD_BASE = 3 * J + 640
HEAD_STEP = 384

X_KIB = (0, 8, 17, 26)
TAB_SCALES_KIB = 15.5
TAB_WORDS_KIB = 29
WA_RAW_ROWS_KIB = 16
LATE_ROWS_KIB = 16.5
LATE_WORDS_KIB = (0, 2)
RES_KIB = (8, 10, 12, 18)
WOVEN_KIB = 36
HEAD_WEIGHTS_KIB = 54
H_LATE_KIB = (8, 10)

QUADRANTS = (0, 2, 1, 3)
TAB_ROWS = 64

YA_BANKS = (4, 5, 6, 7, 0, 6, 7, 0)
Y_BANKS = ((4, 5), (4, 1), (5, 6), (2, 3))


def tile_list_htabg_max_res_kernel(
    tc, tab_words, tab_scales, xT, wgt2, wa_words, wa_scales, wb_words, wb_scales, wd_words, wd_scales, res, offs, offs2, out
):
    nc = tc.nc

    with ExitStack() as ctx:
        keep = ctx.enter_context(tc.tile_pool(name="keep", bufs=1))
        stage = ctx.enter_context(tc.tile_pool(name="stage", bufs=1))
        psum = ctx.enter_context(tc.psum_pool(name="psum", bufs=1))

        def bank(name, shape, number):
            return psum.tile(shape, F32, name=name, offset=number * BANK_BYTES)

        def staged(name, shape, dtype, kib):
            return stage.tile(shape, dtype, name=name, offset=int(kib * 1024), align_bytes=64)

        def kept(name, shape, dtype):
            return keep.tile(shape, dtype, name=name, align_bytes=64)

        idx = keep.tile([P, J // 16], U16, name="idx")
        idx2 = keep.tile([P, J // 16], U16, name="idx2")
        tab_sc = staged("tab_sc", [P, T // 4], I32, TAB_SCALES_KIB)
        tab_w = staged("tab_w", [P, T], I32, TAB_WORDS_KIB)
        got_sc = kept("got_sc", [P, J // 4], I32)
        got_w = kept("got_w", [P, J], I32)
        part_w = [kept("part_w%d" % h, [P, 2, HALF // 2], I32) for h in range(2)]
        wb_raw = kept("wb_raw", [P, 2, R], I32)
        wgt_head = staged("wgt_head", [P, QUARTER], F32, HEAD_WEIGHTS_KIB)
        planes = kept("planes", [P, 2, J // 4], I32)
        wb_sc = kept("wb_sc", [P, 2, R // 4], I32)
        late_sc = kept("late_sc", [P, 2, R // 4], I32)
        wgt = kept("wgt", [P, J], F32)
        wgt_rows = kept("wgt_rows", [P, P], F32)
        wgt_t = kept("wgt_t", [P, J // P, P], F32)
        ident = kept("ident", [P, P], F32)
        x_pl = []
        xg = kept("xg", [P, 5 * J], F32)
        xb = [staged("xb%d" % u, [P, PACK * (UNITS[u][1] - UNITS[u][0])], BF16, WOVEN_KIB + 2 * u)[:] for u in (0, 2, 3, 4)]
        xb.insert(1, xg[:, 0:QUARTER].bitcast(BF16))
        xq = kept("xq", [P, J], U32)
        xq_sc = kept("xq_sc", [P, J], U8)
        ya_bf = kept("ya_bf", [P, J * PACK], BF16)
        ybt_bf = [kept("ybt_bf%d" % b, [P, R], BF16) for b in range(J // BLOCK)]
        yb_sb = kept("yb_sb", [P, 2 * DIRECT * BLOCK], F32)
        h_bf = [xg[:, HALF * c : HALF * (c + 1)].bitcast(BF16) for c in range(2)]
        hq = kept("hq", [P, J], U32)
        hq_sc = kept("hq_sc", [P, J], U8)
        o_sb = kept("o_sb", [P, J // BLOCK, BANK_FLOATS], F32)

        def words(dram):
            return dram[0].rearrange("p n t -> p (n t)").bitcast(I32)

        for p0, p1 in ((0, TAB_ROWS), (TAB_ROWS + 32, P)):
            nc.vector.memset(tab_sc[p0:p1, :], 0)
        nc.gpsimd.memset(wgt_rows[64:P, :], 0.0)
        make_identity(nc, ident[:])

        nc.sync.dma_start(idx[:], offs)
        nc.sync.dma_start(tab_sc[TAB_ROWS : TAB_ROWS + 32, :], tab_scales.bitcast(I32).rearrange("a r c -> r a c"))
        nc.sync.dma_start(tab_w[:], words(tab_words))
        nc.scalar.dma_start(
            wgt_rows[0:64, :], wgt2.rearrange("(g r) j -> g r j", r=16)[:, 0, :].rearrange("g (b k) -> g b k", k=P)
        )
        nc.sync.dma_start(idx2[:], offs2)
        nc.sync.dma_start(wb_raw[:], wb_words.rearrange("a p n t -> p a (n t)").bitcast(I32))
        for q in QUADRANTS:
            nc.scalar.dma_start(
                wb_sc[32 * q : 32 * q + 4, :, :], wb_scales.bitcast(I32).rearrange("a r c -> r a c")[4 * q : 4 * q + 4]
            )
        x_rows = xT.rearrange("(p i) t -> i p t", i=PACK)

        def load_x(i):
            x_pl.append(staged("x_pl%d" % i, [P, T], F32, X_KIB[i]))
            nc.sync.dma_start(x_pl[i][:], x_rows[i])

        def weight_scale(k, t):
            c0 = 64 * k + 32 * (t % 2)
            return late_sc[:, t // 2, c0 : c0 + 32].bitcast(U8)

        load_x(0)

        turned = bank("turned", [P, BANK_FLOATS], 4)
        nc.tensor.transpose(turned[:, 0:P], wgt_rows[:], ident[:])
        nc.scalar.copy(
            wgt_t[:].rearrange("p b (g r) -> p b g r", r=16),
            turned[:, 0:64].rearrange("p (g b) -> p b g", g=8).unsqueeze(3).to_broadcast([P, 8, 8, 16]),
        )
        for hf in range(2):
            spread = bank("spread%d" % hf, [P, BANK_FLOATS], 5 + hf)
            for e in range(4):
                nc.tensor.transpose(spread[:, e * P : (e + 1) * P], wgt_t[:, 4 * hf + e, :], ident[:])
            if hf == 0:
                nc.scalar.copy(wgt_head[:], spread[:, 0:QUARTER])
                nc.scalar.copy(wgt[:, QUARTER:HALF], spread[:, QUARTER:HALF])
            else:
                nc.scalar.copy(wgt[:, HALF:J], spread[:])

        nc.vector.tensor_copy(got_sc[:].bitcast(U8), tab_sc[:].bitcast(U8).indirect(idx[:]))
        for q in QUADRANTS:
            nc.sync.dma_start(planes[32 * q : 32 * q + 4, :, :], got_sc[TAB_ROWS + 8 * q : TAB_ROWS + 8 * q + 8, :])
        load_x(1)

        sc_raw = staged("sc_raw", [P, R // 4], I32, WA_RAW_ROWS_KIB)
        for p0, p1 in ((32, 64), (64, P)):
            nc.gpsimd.memset(sc_raw[p0:p1, :], 0)
        nc.sync.dma_start(sc_raw[1:32:2, :].bitcast(U16)[:, 0:255], wa_scales[0].bitcast(U16)[:, 1:256])
        nc.sync.dma_start(sc_raw[0:32:2, :], wa_scales[0].bitcast(I32))
        late_rows = staged("late_rows", [P, R // 4], I32, LATE_ROWS_KIB)
        nc.sync.dma_start(late_rows[0:32, 64:128], wd_scales[0].bitcast(I32).rearrange("i (a c) -> (i a) c", a=2))
        load_x(2)

        for h in range(2):
            nc.vector.tensor_copy(
                got_w[:, h * HALF : (h + 1) * HALF].bitcast(U32), tab_w[:].bitcast(U32).indirect(idx[:, 32 * h : 32 * h + 32])
            )
        load_x(3)
        for h in range(2):
            nc.vector.tensor_copy(
                part_w[h][:].bitcast(U16).rearrange("p d (c i) -> p c d i", i=8),
                got_w[:, h * HALF : (h + 1) * HALF].bitcast(U16).rearrange("p (c i d) -> p c d i", i=8, d=2),
            )

        yb = {}

        def turn_yb(c):
            yb[c] = bank("yb%d" % c, [P, 2, QUARTER], c)
            for half in range(2):
                for u in range(2):
                    nc.tensor.transpose(
                        yb[c][:, u, half * BLOCK : (half + 1) * BLOCK],
                        ybt_bf[2 * c + half][:].bitcast(F32)[:, u * P : (u + 1) * P],
                        ident[:],
                    )

        def multiply_yb(b):
            acc = bank("ybt%d" % b, [P, R], b)
            for a in range(2):
                nc.tensor.matmul_mx(
                    out=acc[:],
                    lhsT=part_w[b // 4][:, a, (b % 4) * 64 : (b % 4 + 1) * 64].bitcast(U8).bitcast(FP4X4),
                    lhsT_scale=planes[:, a, 32 * b : 32 * b + 32].bitcast(U8),
                    rhs=wb_raw[:, a, :].bitcast(FP8X4),
                    rhs_scale=wb_sc[:, a, :].bitcast(U8),
                    start=(a == 0),
                    stop=(a == 1),
                )
            nc.scalar.copy(
                ybt_bf[b][:].rearrange("p (u m e) -> p u m e", u=2, e=2), acc[:].rearrange("p (m u e) -> p u m e", u=2, e=2)
            )

        for b in range(4):
            multiply_yb(b)
        turn_yb(0)
        turn_yb(1)
        nc.scalar.copy(yb_sb[:, 0:HALF].rearrange("p (n u) -> p n u", u=2), yb[0][:].rearrange("p u n -> p n u"))
        nc.scalar.copy(yb_sb[:, HALF:].rearrange("p (n u) -> p n u", u=2), yb[1][:, :, 0:BLOCK].rearrange("p u n -> p n u"))
        for b in range(4, J // BLOCK):
            multiply_yb(b)
        turn_yb(2)
        turn_yb(3)

        def gather_x(i, c0, c1):
            if c0 < QUARTER:
                at, weights = HEAD_BASE + i * HEAD_STEP + c0, wgt_head
            else:
                at, weights = i * J + c0, wgt
            nc.vector.tensor_tensor(
                xg[:, at : at + c1 - c0], x_pl[i][:].indirect(idx2[:, c0 // 16 : c1 // 16]), weights[:, c0:c1], MULT
            )

        def weave(unit):
            c0, c1 = UNITS[unit]
            if c0 < QUARTER:
                four = xg[:, HEAD_BASE - BLOCK : HEAD_BASE - BLOCK + PACK * HEAD_STEP].rearrange("p (t s) -> p t s", t=PACK)
                four = four[:, :, BLOCK + c0 : BLOCK + c1]
            else:
                four = xg[:, 0 : PACK * J].rearrange("p (t s) -> p t s", t=PACK)[:, :, c0:c1]
            nc.scalar.copy(
                xb[unit].rearrange("p (c k t) -> p c t k", k=4, t=PACK), four.rearrange("p t (c k) -> p c t k", k=4)
            )

        ya = {}

        def first_stage(unit):
            c0, c1 = UNITS[unit]
            nc.vector.quantize_mx(out=xq[:, c0:c1].bitcast(FP8X4), scales=xq_sc[:, c0:c1], in_=xb[unit])
            for b in range(c0 // BLOCK, c1 // BLOCK):
                cols = slice(b * BLOCK, (b + 1) * BLOCK)
                ya[b] = bank("ya%d" % b, [P, PACK, BLOCK], YA_BANKS[b])
                for t in range(PACK):
                    nc.tensor.matmul_mx(
                        out=ya[b][:, t, :],
                        lhsT=w_perm[:, t, 0, :].bitcast(FP8X4),
                        lhsT_scale=weight_scale(0, t),
                        rhs=xq[:, cols].bitcast(FP8X4),
                        rhs_scale=xq_sc[:, cols],
                        start=True,
                        stop=True,
                    )

        def h_of(b, count=1):
            n0 = (b % 2) * BLOCK
            return h_bf[b // 2][:, PACK * n0 : PACK * (n0 + count * BLOCK)]

        def join_direct(b):
            nc.vector.tensor_tensor(
                h_of(b).rearrange("p (c e t) -> p c t e", e=2, t=PACK),
                ya[b][:].rearrange("p t (c e) -> p c t e", e=2),
                yb_sb[:, 2 * b * BLOCK : 2 * (b + 1) * BLOCK].bitcast(BF16).rearrange("p (c e t) -> p c t e", e=2, t=PACK),
                MAX,
            )

        def empty_ya(b):
            nc.scalar.copy(
                ya_bf[:, b * R : (b + 1) * R].rearrange("p (n t) -> p n t", t=PACK), ya[b][:].rearrange("p t n -> p n t")
            )

        def join(b, count=1):
            n0 = (b % 2) * BLOCK
            nc.vector.tensor_tensor(
                h_of(b, count).rearrange("p (n u e) -> p n u e", u=2, e=2),
                yb[b // 2][:].bitcast(BF16).rearrange("p u (n e) -> p n u e", e=2)[:, n0 : n0 + count * BLOCK, :, :],
                ya_bf[:, b * R : (b + count) * R].rearrange("p (n u e) -> p n u e", u=2, e=2),
                MAX,
            )

        sums = {}

        def second_stage(c):
            cols = slice(c * QUARTER, (c + 1) * QUARTER)
            nc.vector.quantize_mx(out=hq[:, cols].bitcast(FP8X4), scales=hq_sc[:, cols], in_=h_bf[c])
            for g in range(2):
                y = bank("y%d_%d" % (c, g), [P, 2, QUARTER], Y_BANKS[c][g])
                for e in range(2):
                    nt = 2 * g + e
                    nc.tensor.matmul_mx(
                        out=y[:, e, :],
                        lhsT=late_w[1][:, 0, nt * P : (nt + 1) * P].bitcast(FP8X4),
                        lhsT_scale=weight_scale(1, nt),
                        rhs=hq[:, cols].bitcast(FP8X4),
                        rhs_scale=hq_sc[:, cols],
                        start=True,
                        stop=True,
                    )
                sums[c, g] = y

        out_rows = out.rearrange("(a p) j -> p a j", p=P)
        res_rows = res.rearrange("(a p) j -> p a j", p=P)
        res_sb = {}

        def load_res(quarters, banks, kib):
            nts, cols = slice(2 * banks[0], 2 * banks[-1] + 2), slice(quarters[0] * QUARTER, (quarters[-1] + 1) * QUARTER)
            part = staged("res_sb%d" % kib, [P, 2 * len(banks), len(quarters) * QUARTER], F32, kib)
            nc.sync.dma_start(part[:], res_rows[:, nts, cols])
            for ci, c in enumerate(quarters):
                for gi, g in enumerate(banks):
                    res_sb[c, g] = part[:, 2 * gi : 2 * gi + 2, ci * QUARTER : (ci + 1) * QUARTER]

        def finish(c, g, pieces=1):
            step = 2 // pieces
            for e0 in range(0, 2, step):
                es = slice(e0, e0 + step)
                o = o_sb[:, 2 * c + g, :].rearrange("p (e n) -> p e n", e=2)[:, es, :]
                nc.vector.tensor_tensor(o, sums[c, g][:, es, :], res_sb[c, g][:, es, :], ADD)
                nc.sync.dma_start(out_rows[:, 2 * g + e0 : 2 * g + e0 + step, c * QUARTER : (c + 1) * QUARTER], o)

        gather_x(0, 0, QUARTER)
        gather_x(0, QUARTER, J)
        late_w = [staged("late_w%d" % k, [P, 1, R], I32, LATE_WORDS_KIB[k]) for k in range(2)]
        nc.sync.dma_start(late_w[0][:, 0, :], words(wa_words))
        gather_x(1, 0, QUARTER)
        nc.vector.tensor_copy(
            late_rows[:, 0:64].bitcast(U8).rearrange("p (t c i) -> p c t i", t=2, i=16),
            sc_raw[:].bitcast(U8).rearrange("p (c i t) -> p c t i", i=16, t=PACK)[:, :, 0:2, :],
        )
        for q in QUADRANTS:
            nc.sync.dma_start(late_sc[32 * q : 32 * q + 4, :, :], late_rows[8 * q : 8 * q + 8, :])
        nc.sync.dma_start(late_w[1][:, 0, :], words(wd_words))
        gather_x(1, QUARTER, J)
        load_res((0,), (0,), RES_KIB[0])
        load_res((0,), (1,), RES_KIB[1])
        load_res((1,), (0, 1), RES_KIB[2])
        gather_x(2, 0, QUARTER)
        gather_x(2, QUARTER, J)
        load_res((2, 3), (0, 1), RES_KIB[3])

        for unit in range(3):
            gather_x(3, *UNITS[unit])
            weave(unit)
        w_perm = staged("w_perm0", [P, PACK, 1, P], I32, HEAD_WEIGHTS_KIB)
        nc.vector.tensor_copy(
            w_perm[:].rearrange("p t a (c i) -> p (a c) t i", i=4),
            late_w[0][:].rearrange("p a (c i t) -> p (a c) t i", i=4, t=PACK),
        )
        for unit in range(2):
            first_stage(unit)
            gather_x(3, *UNITS[3 + unit])
            weave(3 + unit)

        for unit in range(2):
            join_direct(unit)
            first_stage(2 + unit)
        second_stage(0)
        join_direct(2)
        first_stage(4)
        empty_ya(3)
        join(3)
        for c in (2, 3):
            finish(0, c - 2)
            second_stage(c - 1)
            for b in (2 * c, 2 * c + 1):
                empty_ya(b)
            h_bf.append(staged(("h_third", "h_fourth")[c - 2], [P, J], BF16, H_LATE_KIB[c - 2])[:])
            join(2 * c, 2)
        finish(1, 0)
        second_stage(3)
        finish(1, 1)
        finish(2, 0)
        finish(2, 1)
        finish(3, 0)
        finish(3, 1, 2)
